import numpy as np, ml_dtypes
CORES = [23,119,17,113]
N = 4
import mx_ref
BF = ml_dtypes.bfloat16
def gentries(a):
    return np.ascontiguousarray(a.reshape(8, 16, -1).transpose(0, 2, 1)).reshape(8, -1)
def gtable(e):
    e = np.asarray(e); return np.ascontiguousarray(e.reshape(8, -1, 16).transpose(0, 2, 1)).reshape(128, -1).astype(np.int32)
def gcols(t, e):
    v = np.concatenate([t.reshape(8, 16, -1, 4), np.zeros((8, 16, 1, 4), BF)], axis=2)
    return np.ascontiguousarray(np.stack([v[g][:, e[g]] for g in range(8)])).reshape(128, -1)
def tile(rs):
    return np.stack(rs, axis=2).reshape(128, -1).astype(BF)
def cut(t, i, w=512):
    return t[:, w * i:w * i + w]
def pick(q, e):
    c = np.concatenate([q[0].reshape(128, -1, 4), np.zeros((128, 1, 4), np.uint8)], axis=1); s = np.concatenate([q[1], np.ones((16, 1), np.uint8)], axis=1)
    return (np.ascontiguousarray(c[:, e].reshape(128, -1)), np.ascontiguousarray(s[:, e]))
def join(*qs):
    return (np.concatenate([q[0] for q in qs], axis=1), np.concatenate([q[1] for q in qs], axis=1))
def put(q, e, v):
    c, s = q[0].reshape(128, -1, 4).copy(), q[1].copy(); c[:, e] = v[0].reshape(128, -1, 4); s[:, e] = v[1]
    return (c.reshape(128, -1), s)
def pk(c, s):
    return (np.ascontiguousarray(c), mx_ref.live(s))
def emit(q):
    return q[0], q[1]
def packed(v, rng):
    q = [mx_ref.quantize(np.ascontiguousarray(v[r])) for r in range(N)]
    return np.stack([a for a, b in q]), np.stack([mx_ref.plane(b, rng) for a, b in q])
def values_of_codes():
    e, c = np.zeros((128, 128, 4), np.float32), np.zeros((128, 2, 4), np.uint8)
    e[np.arange(128), np.arange(128), 0] = 1
    c[:127, :, 0] = np.arange(256).reshape(2, 128).T[:127]
    return mx_ref.matmul(mx_ref.quantize(e.reshape(128, 512).astype(BF)), (c.reshape(128, 8), np.full((16, 2), 127, np.uint8))).T.reshape(-1).astype(np.float64)
CODE_VALUE, SCALE_VALUE = values_of_codes(), 2.0 ** (np.arange(256) - 127.0)
def decode(q):
    return (CODE_VALUE[q[0]].reshape(16, 8, -1, 4) * SCALE_VALUE[q[1]][:, None, :, None] + 0.0).reshape(128, -1).astype(np.float32)
def f(rng, *shape):
    return mx_ref.flush((rng.standard_normal(shape, dtype=np.float32) * np.exp2(rng.integers(-2, 3, shape[:-1] + (1,)))).astype(BF))
def wide(rng, *shape, cols=0):
    v = rng.standard_normal(shape, dtype=np.float32) * np.exp2(rng.integers(-12, 13, shape)).astype(np.float32)
    if cols: v *= np.repeat(np.exp2(rng.integers(-cols, cols + 1, shape[:-2] + (1, shape[-1] // 4))) * (rng.random(shape[:-2] + (1, shape[-1] // 4)) > 0.0625), 4, axis=-1).astype(np.float32)
    return mx_ref.flush(v.astype(BF))
C, P, H, R = 384, 48, 56, 3
STEP = [1, 2, 1]
def play(s, n):
    place = np.arange(C)
    pile = np.repeat(np.arange(len(n)), n)
    o = np.lexsort((place, -s, pile))
    top = o[np.searchsorted(pile, np.arange(len(n)))]
    rest = np.delete(place, top)
    o = rest[np.lexsort((rest, s[rest], pile[rest]))]
    low = o[np.searchsorted(pile[rest], np.flatnonzero(n >= 2))]
    a, b = top[np.lexsort((top, -s[top]))], low[np.lexsort((low, s[low]))]
    left = np.delete(place, np.concatenate([top, low]))
    m = np.concatenate([np.maximum(n - 2, 0), [len(a), len(b)]])
    came = np.concatenate([left, C + np.arange(len(a)), C + H + np.arange(len(b))])
    k = np.repeat(np.arange(len(m)), m)
    e = came[np.lexsort((np.arange(C), k, -m[k]))]
    m = m[np.argsort(-m, kind="stable")]
    return a, b, e, m[m > 0]
def big(v):
    v = v.astype(np.float32)
    v[np.abs(v) < np.float32(2.0 ** -16)] = 0
    return v.astype(BF)
def sizes(rng, n, c, *shape):
    e = np.argsort(rng.random(shape + (c - 1,)), axis=-1)[..., :n - 1] + 1
    return np.diff(np.sort(e, axis=-1), axis=-1, prepend=0, append=c)
def pilelist(n):
    return np.stack([gtable(n[r]) for r in range(N)])
def numbers_of(rng):
    return {"x": big(f(rng, N, 128, 4 * C)), "u": np.array(f(rng, N, 128, 512)), "v": np.array(f(rng, N, 128, 512))}
def layers(rng):
    return big(f(rng, N, 128, 2048)).reshape(N, 8, 16, 4, 8, 16, 4)
def weights(rng, w):
    c, p = packed(np.ascontiguousarray(w).reshape(N, 128, 2048), rng)
    return {"wc": c, "ws": p}
def signs(rng):
    return np.stack([rng.permutation(8) % 2 * 2.0 - 1.0 for r in range(N)])
def setup_inputs(rng):
    return {**numbers_of(rng), **weights(rng, layers(rng)), "z": pilelist(sizes(rng, P, C, N, 8))}
def setup_inputs_ties(rng):
    d = numbers_of(rng)
    e = rng.permutation(N)
    x = d["x"].reshape(N, 8, 16, C, 4)
    for r in range(N):
        k = np.zeros(C, int) if r == e[0] else rng.permutation(C) % 3
        a = x[r][:, :8, :3].copy()
        a[:, :, 2] = 0
        x[r][:, :8] = a[:, :, k]
    x[e[1]] = 0
    u = d["u"].reshape(N, 8, 16, 128, 4)
    u[:, :, 8:, ::16] = 0
    w = layers(rng)
    w[:, :, 8:, :, :, :8] = 0
    return {"x": x.reshape(N, 128, 4 * C), "u": u.reshape(N, 128, 512), "v": d["v"], **weights(rng, w), "z": pilelist(sizes(rng, P, C, N, 8))}
def setup_inputs_near(rng):
    d = numbers_of(rng)
    x = np.zeros((N, 8, 16, C, 4), np.float32)
    u = d["u"].reshape(N, 128, 128, 4)
    u[:, :, ::16] = 0
    n = sizes(rng, P, C, N, 8)
    o, c = rng.permutation(N) % 4, signs(rng)
    upper = np.arange(C) // (C // 2)
    for r in range(N):
        i = (np.arange(C) + rng.integers(0, C, (8, 1))) % C
        if o[r] < 2:
            for g in np.flatnonzero(c[r] > 0)[:2]:
                last = int(np.sum(n[r, g, :int(np.argmax(n[r, g])) + 1])) - 1
                i[g] = (last - np.arange(C)) % C
        s = (i + 1) // 2
        size = 1.0 if o[r] < 2 else 2.0 ** -4
        if o[r] < 2: x[r, :, 0, :, 0] = c[r][:, None]
        if o[r] == 3:
            s = i % (C // 2)
            k = rng.permutation(8)
            for g in range(8):
                if k[g] % 2:
                    s[g] = (np.arange(C) - C // 4 - 1) % (C // 2)
                    n[r, g] = 1
                    n[r, g, rng.integers(P)] = C - P + 1
                else: n[r, g] = np.tile(sizes(rng, P // 2, C // 2), 2)
                more = upper ^ (k[g] // 2 % 2)
                x[r, g, 0, :, 0] = more * 4.5 * 2.0 ** -30
                x[r, g, 1, :, 0] = (1 - more) * 4.0 * 2.0 ** -30
        digit = ((s[:, :, None] >> np.arange(8)) & 1) * np.exp2(np.arange(8) - 23.0) * size
        x[r, :, 8] = digit[:, :, :4]
        x[r, :, 9] = digit[:, :, 4:]
        x[r, :, 10:] = rng.integers(4, 8, (8, 6, C, 4)) * 2.0 ** -20 * size
        q = 1.0 if o[r] == 0 else 2.0 ** -30
        for h in range(0, 128, 16):
            u[r, h, h, 0] = q
            u[r, h + 8:h + 10, h] = q
            if o[r] == 3:
                u[r, h, h, 0] = 1.125 * q
                u[r, h + 1, h, 0] = 1.25 * q
    w = layers(rng)
    w[:, :, :10] = 0
    w[:, :, :, :, :, :10] = 0
    return {"x": x.reshape(N, 128, 4 * C).astype(BF), "u": u.reshape(N, 128, 512), "v": d["v"], **weights(rng, w), "z": pilelist(n)}
def setup_inputs_huge(rng):
    d = numbers_of(rng)
    c = np.stack([rng.permutation(C) % 2 * 2.0 - 1.0 for r in range(N)])
    one = rng.permutation(N) < N // 2
    c[one] = -1
    x = (0.6 + 0.2 * rng.random((N, 128, C, 4))) * 2.0 ** 30
    u = d["u"].reshape(N, 128, 128, 4)
    a = 2.0 ** 30 * (1 - 0.25 * rng.random((N, 128, 8, 4)))
    for r in np.flatnonzero(one):
        for k in (x[r], a[r]):
            k[:] = 2.0 ** 30 * (1 - 0.0625 * rng.integers(0, 2, k.shape))
            k[::8, :, 0] = 2.0 ** 30
    x *= c[:, None, :, None]
    a *= signs(rng)[:, None, :, None]
    u[:, :, ::16] = a.astype(np.float32).astype(BF)
    w = np.zeros((N, 128, 4, 128, 4), np.float32)
    i = np.arange(128)
    for b in range(4): w[:, i, b, i, b] = 1
    return {"x": x.astype(np.float32).reshape(N, 128, 4 * C).astype(BF), "u": u.reshape(N, 128, 512), "v": d["v"], **weights(rng, w.astype(BF)), "z": pilelist(sizes(rng, P, C, N, 8))}
def oddsizes(rng, k):
    if k == 0: return 2 * R + sizes(rng, P, C - 2 * R * P)
    if k == 3: return rng.permutation(C // P + (np.arange(P) < C % P))
    if k == 4: return np.sort(sizes(rng, P, C))
    if k == 7: return np.sort(sizes(rng, P, C))[::-1]
    o = np.ones(P, int)
    if k == 8:
        i = np.sort(rng.permutation(P)[:2])
        o[i[0]] = (C - P + 2) // 2 - rng.integers(1, 9)
        o[i[1]] = C - P + 2 - o[i[0]]
        return o
    if k == 2: o += 1
    if k == 5: o += np.arange(P) % 2
    if k == 6: o += 2
    o[0] += C - np.sum(o)
    return rng.permutation(o)
def setup_inputs_ragged(rng):
    d = numbers_of(rng)
    h = int(rng.integers(8))
    n = np.stack([np.stack([oddsizes(rng, 8 if k == 1 and r % 2 else k) for k in np.insert(1 + rng.permutation(7), h, 0)]) for r in range(N)])
    x, u = d["x"].reshape(N, 128, C, 4), d["u"].reshape(N, 128, 128, 4)
    for r in range(0, N, 2):
        g = int(np.argmax(np.max(n[r], axis=1)))
        last = int(np.sum(n[r, g, :int(np.argmax(n[r, g])) + 1])) - 1
        k = big(u[r, :, 16 * g])
        x[r, :, last] = -k if r % 4 else k
    d["x"] = x.reshape(N, 128, 4 * C)
    return {**d, **weights(rng, layers(rng)), "z": pilelist(n)}
def setup_inputs_spread(rng):
    d = setup_inputs(rng)
    d["x"] = big(wide(rng, N, 128, 4 * C, cols=6))
    return d
def check_inputs(d):
    b = []
    for k in ("x", "u", "v"):
        a = np.abs(d[k].astype(np.float32))
        if not (np.isfinite(a).all() and ((a == 0) | (a >= 2.0 ** -30) & (a <= 2.0 ** 30)).all()): b.append("a value of " + k)
    none, least, most = [emit(mx_ref.quantize(np.full((128, 16), k, np.float32).astype(BF)))[1][0, 0] for k in (0.0, 2.0 ** -30, 2.0 ** 30)]
    for r in range(N):
        if ((d["wc"][r] == 0x7F) | (d["wc"][r] == 0xFF)).any(): b.append("wc: a code that is no number")
        s = mx_ref.live(d["ws"][r])
        if ((s != none) & ((s < least) | (s > most))).any(): b.append("ws: a scale out of range")
        n = gentries(d["z"][r]).astype(np.int64)
        if (n < 1).any(): b.append("z: a size under 1")
        if (np.sum(n, axis=1) != C).any(): b.append("z: a sum of sizes")
    return b
def reference(x, u, v, wc, ws, z):
    qu = [mx_ref.quantize(u[r]) for r in range(N)]
    lay = [pk(wc[r], ws[r]) for r in range(N)]
    now = [x[r] for r in range(N)]
    size = [list(gentries(z[r])) for r in range(N)]
    for t in range(R):
        given, sent, new = [], [], []
        for r in range(N):
            s = mx_ref.matmul(qu[r], mx_ref.quantize(now[r]))[::16] + np.float32(0.0)
            e, h = np.full((8, 2 * H), -1), np.zeros((8, C), int)
            for g in range(8):
                a, b, h[g], size[r][g] = play(s[g], size[r][g])
                e[g, :len(a)] = a
                e[g, H:H + len(b)] = b
            k = gcols(now[r], e)
            given.append(k)
            sent.append(mx_ref.quantize(k))
            new.append(h)
        came = decode(join(*sent))
        for r in range(N):
            k = given[r]
            d = cut(came, r ^ STEP[t], 8 * H)
            q = mx_ref.quantize(np.ascontiguousarray(((k.astype(np.float32) + d) * np.float32(0.5)).astype(BF)))
            c = tile([np.maximum(mx_ref.matmul(pick(lay[r], np.arange(128 * b, 128 * b + 128)), q), np.float32(0.0)) * np.float32(0.03125) + k[:, b::4].astype(np.float32) for b in range(4)])
            now[r] = gcols(np.concatenate([now[r], c], axis=1), new[r])
    y, oz = np.zeros((N, 128, C), np.float32), np.zeros((N, 8, H), np.float32)
    oc, osc = np.zeros((N, 128, 4 * C), np.uint8), np.zeros((N, 16, C), np.uint8)
    for r in range(N):
        q = mx_ref.quantize(now[r])
        y[r] = mx_ref.matmul(mx_ref.quantize(v[r]), q)
        for g in range(8): oz[r, g, :len(size[r][g])] = size[r][g]
        oc[r], osc[r] = emit(q)
    return {"y": y, "oz": oz, "oc": oc, "osc": osc}

@@ -1,0 +1,544 @@
+import numpy as np
+from concourse.mybir import dt, AluOpType as A, ActivationFunctionType as F
+
+C, H, R = 384, 56, 3
+PILES = [48, 50, 52]
+STEP = [1, 2, 1]
+G0 = 388
+PW = 4 * (G0 + 2 * H)
+CH = [(192, 384), (0, 192)]
+VPL = [[(0, 1), (0, 1)]] * 3
+VSG = (0,)
+BIG = 2.0 ** 96
+U = -2.0 ** 75
+B1K, B4M = 1024.0, 2.0 ** 22
+OFF = 16383.0
+WAKE, NEAR, TURNS = 100.0, 0.4, 1500
+FLY, RATE, CALL = 1800.0, 80.0, 400.0
+
+ARENA = {"f": 0, "h": 0, "i": 0, "w": 0}
+AT = {}
+KEPT = {}
+
+
+def _take(ar, name, n):
+    al = 8 if ar in "fi" else 16
+    AT[name] = (ar, ARENA[ar])
+    ARENA[ar] += (n + al - 1) // al * al
+
+
+for _n, _k in [("m", 384), ("za", 64), ("n0", 64), ("inv0", 112), ("inv1", 112), ("inv2", 112), ("mm0", 64), ("mm1", 64),
+               ("mm2", 64), ("cum0", 72), ("cum1", 72), ("cum2", 72), ("cum3", 72), ("v2", 64), ("nd", 448),
+               ("s", 384), ("ms", 384), ("io", 456), ("pc", 16), ("j16", 80), ("j8", 64), ("j4", 116), ("e16", 80),
+               ("e16b", 80), ("e4", 116), ("e4b", 116), ("m16", 64), ("m16k", 64), ("m16n", 384), ("m4", 112), ("seln", 64),
+               ("ra8", 64), ("kp", 112), ("k3i", 72), ("k3", 72), ("ck", 64), ("cx", 64), ("i16", 24),
+               ("cp", 24), ("rv", 128), ("vb8", 64), ("tp", 64), ("pd", 64), ("pr", 112), ("ef", 56), ("sr", 112),
+               ("sd", 112), ("lh", 112), ("pk", 112), ("pkr", 384), ("pkd", 384), ("t3o", 72), ("junk", 320), ("r1", 64),
+               ("hold", 384), ("dg", 384), ("xs", 24)]:
+    _take("f", _n, _k)
+for _t in range(4):
+    for _n, _k in [("vr", 456), ("rr", 64), ("ed", 64)]:
+        _take("f", _n + str(_t), _k)
+    _take("w", "en%d" % _t, 8)
+    if _t:
+        _take("f", "n%d" % _t, 64)
+for _t in range(R):
+    for _n, _k in [("vm", 128), ("cn", 64), ("a1", 64), ("mq", 64), ("y", 64), ("yt", 8), ("yv", 64), ("sg4", 8),
+                   ("ys", 64), ("nq", 64), ("rest", 64), ("wu", 64), ("t3", 72), ("b1", 24)]:
+        _take("f", _n + str(_t), _k)
+    for _n, _k in [("kl", 24), ("rk", 4), ("el", 96)]:
+        _take("w", _n + str(_t), _k)
+for _n, _k in [("eq", 384), ("sg", 392), ("cc", 392), ("rs", 392), ("lc", 392), ("li", 392), ("kr", 392), ("ki", 392)]:
+    _take("h", _n, _k)
+for _n, _k in [("pi", 8), ("pj", 8), ("ui", 8), ("xi", 24), ("xk", 24), ("xb", 24), ("ki2", 24), ("hi", 24)]:
+    _take("i", _n, _k)
+for _n, _k in [("zu", 4), ("uo", 8), ("qo", 24), ("pu", 8), ("ru", 8)]:
+    _take("w", _n, _k)
+
+X4, U8, BF, F32 = "float8_e4m3fn_x4", "uint8", "bfloat16", "float32"
+SCRATCH = {"f": ("sbuf", [128, ARENA["f"]], F32), "h": ("sbuf", [128, ARENA["h"]], BF),
+           "i": ("sbuf", [128, ARENA["i"]], "int32"), "w": ("sbuf", [128, ARENA["w"]], "uint16"),
+           "zi": ("sbuf", [128, 4], "int32"), "ps": ("psum", [128, 4096], F32),
+           "pool3": ("sbuf", [128, 4 * C], BF), "ub": ("sbuf", [128, 512], BF), "vb": ("sbuf", [128, 512], BF),
+           "ones": ("sbuf", [128, 528], BF), "eye": ("sbuf", [128, 528], BF), "mt": ("sbuf", [128, 512], BF),
+           "ah": ("sbuf", [128, 448], BF), "rl": ("sbuf", [128, 448], F32), "dh": ("sbuf", [128, 4 * C + 8], F32),
+           "yb": ("sbuf", [128, C], F32)}
+for _n, _k in [("u", 128), ("u2", 128), ("v", 128), ("w", 512), ("e", 512), ("m", 128), ("x0", C), ("x1", C), ("x2", C), ("x3", C),
+               ("l0", C), ("l1", C), ("l2", C)]:
+    SCRATCH["q" + _n] = ("sbuf", [128, _k], X4)
+    SCRATCH["s" + _n] = ("sbuf", [128, _k], U8)
+for _t in range(R):
+    SCRATCH["pool%d" % _t] = ("sbuf", [128, PW], BF)
+    SCRATCH["out%d" % _t] = ("sbuf", [128, 28], "uint16")
+    SCRATCH["lin%d" % _t] = ("sbuf", [128, 28], "uint16")
+NSEM, NDMA = 110, 26
+SEMAPHORES = (["c%d" % k for k in range(NSEM)] + ["d%d" % k for k in range(NDMA)] + ["sent"]
+              + [n + str(t) for n in ("qa", "qb", "la") for t in range(R)])
+
+
+def v(name, a=0, b=None, s=1):
+    if name in AT:
+        ar, o = AT[name]
+        return (ar, o + a, o + b, s)
+    return (name, a, SCRATCH[name][1][1] if b is None else b, s)
+
+
+def ind(win, off):
+    return ("@", win, off)
+
+
+def size(d):
+    return 16 * size(d[2]) if d[0] == "@" else len(range(d[1], d[2], abs(d[3])))
+
+
+def two(d):
+    return d[0] != "@" and SCRATCH[d[0]][2] in (BF, "uint16")
+
+
+def places(ds):
+    o = []
+    for d in ds:
+        if isinstance(d, tuple):
+            o += [d[1], d[2]] if d[0] == "@" else [d]
+    return o
+
+
+def collect(g, T, topo, core, rank):
+    ops = []
+
+    def ap(d):
+        if not isinstance(d, tuple):
+            return d
+        if d[0] == "@":
+            return ap(d[1]).indirect(ap(d[2]))
+        if d[3] < 0:
+            return T[d[0]][:, d[2] - 1:d[1] - 1:-1] if d[1] else T[d[0]][:, d[2] - 1::-1]
+        return T[d[0]][:, d[1]:d[2]:d[3]] if d[3] > 1 else T[d[0]][:, d[1]:d[2]]
+
+    def add(q, cost, fn, rd, wr, late=0.0, **k):
+        ops.append(dict(q=q, cost=cost, fn=fn, rd=places(rd), wr=places(wr), late=late, **k))
+        return len(ops) - 1
+
+    def cyc(out, ins, k=1.0):
+        n = size(out) if out[0] != "@" else size(ins[0])
+        if out[0] == "@":
+            return 60 + 3.8 * n
+        if ins and ins[0][0] == "@":
+            return 60 + 1.56 * n
+        if all(two(d) for d in [out] + ins):
+            k *= 0.5
+        return max(64.0, n * k)
+
+    def tt(out, a, b, op):
+        add("v", cyc(out, [a, b], 1 if "ps" in (a[0], b[0]) else 2), lambda: g.vector.tensor_tensor(ap(out), ap(a), ap(b), op), [a, b], [out])
+
+    def ts(out, a, s1, op0, s2=None, op1=None):
+        if op1 is None:
+            fn = lambda: g.vector.tensor_scalar(ap(out), ap(a), ap(s1), None, op0)
+        else:
+            fn = lambda: g.vector.tensor_scalar(ap(out), ap(a), ap(s1), ap(s2), op0, op1)
+        add("v", cyc(out, [a]), fn, [a, s1, s2], [out])
+
+    def cp(out, a):
+        if out[0] == "@":
+            add("v", cyc(out, [a]), lambda: g.vector.tensor_copy(ap(out), ap(a)), [a, out[2]], [out[1]])
+        else:
+            add("v", cyc(out, [a]), lambda: g.vector.tensor_copy(ap(out), ap(a)), [a], [out])
+
+    def scan(out, d0, d1, init, op0, op1):
+        add("v", cyc(out, [d0, d1]), lambda: g.vector.tensor_tensor_scan(ap(out), ap(d0), ap(d1), ap(init), op0, op1), [d0, d1, init], [out])
+
+    def fill(out, c):
+        add("v", cyc(out, []), lambda: g.vector.memset(ap(out), c), [], [out])
+
+    def act(out, a, fn, scale=None, bias=None, acc=None):
+        k = {}
+        if scale is not None:
+            k["scale"] = scale
+        if bias is not None:
+            k["bias"] = bias
+        if acc is not None:
+            k["accum_out"] = acc
+        c = 20 + (cyc(out, [a]) if a[0] == "@" else max(64.0, size(out)))
+        add("s", c, lambda: g.scalar.activation(ap(out), ap(a), fn, **{x: ap(y) for x, y in k.items()}), [a, scale, bias], [out, acc])
+
+    def iota(out, pat, base, cm=0):
+        if SCRATCH[out[0]][2] == "int32":
+            fn = lambda: g.iota(ap(out), pat, base, cm)
+        else:
+            fn = lambda: g.iota(ap(out), pat, base, cm, allow_small_or_imprecise_dtypes=True)
+        add("g", 130 + 2 * size(out), fn, [], [out])
+
+    def quant(name, c0, c1, src):
+        q, s = v("q" + name, c0, c1), v("s" + name, c0, c1)
+        add("v", 12 + 0.22 * size(src), lambda: g.vector.quantize_mx(ap(q), ap(s), ap(src)), [src], [q, s])
+
+    def mm(bank, st, s0, mv, c0, c1):
+        out = v("ps", 512 * bank, 512 * bank + c1 - c0)
+        a, b, c, d = v("q" + st, s0, s0 + 128), v("s" + st, s0, s0 + 128), v("q" + mv, c0, c1), v("s" + mv, c0, c1)
+        add("t", 1.2 * (c1 - c0 + 16), lambda: g.tensor.matmul_mx(ap(out), ap(a), ap(b), ap(c), ap(d), True, True), [a, b, c, d], [out])
+        return out
+
+    def dma(q, out, src, rd, wr, nbytes, last=False):
+        e = g.sync if q == "y" else g.scalar
+        add(q, 60, lambda: e.dma_start(out(), src()), rd, wr, late=1800 + nbytes / 200.0, dma=True, last=last)
+
+    def byt(d):
+        return ap(d).bitcast(dt.uint8)
+
+    Q16, HH, QQ, T4, S4, SGN, H56, THR, C4, CE, CB, CQ, TMP, Z16 = [v("pc", k, k + 1) for k in range(14)]
+
+    dma("y", lambda: T.zi[:, 0:3], lambda: T.z[:, :], [], [v("zi", 0, 3)], 2e3)
+    dma("s", lambda: T.ub[:, :], lambda: T.u[:, :], [], [v("ub")], 131e3)
+    for k, (c0, c1) in enumerate(CH):
+        dma("ys"[k % 2], lambda c0=c0, c1=c1: T.pool0[:, 4 * c0:4 * c1], lambda c0=c0, c1=c1: T.x[:, 4 * c0:4 * c1], [],
+            [v("pool0", 4 * c0, 4 * c1)], 131e3 + 1024 * (C - c0))
+    dma("y", lambda: byt(v("qw")), lambda: T.wc[:, :], [v("pool0", 0, 4 * C)], [v("qw")], 262e3)
+    dma("y", lambda: T.sw[:, :], lambda: T.ws[:, :], [v("pool0", 0, 4 * C)], [v("sw")], 330e3)
+    dma("y", lambda: T.vb[:, :], lambda: T.v[:, :], [v("pool0", 0, 4 * C)], [v("vb")], 460e3)
+
+    iota(v("pi", 0, 1), [[0, 1]], 0, 1)
+    iota(v("j16", 0, 80), [[0, 5], [1, 16]], 0)
+    iota(v("io", 0, 385), [[1, 385]], 0)
+    ops[-1]["after"] = [len(ops) - 3]
+    iota(v("io", 385, 456), [[0, 71]], C)
+    iota(v("j8", 0, 64), [[0, 8], [1, 8]], 0)
+    iota(v("ui", 0, 8), [[16, 8]], 0)
+    for k, (sh, msk) in enumerate([(0, 15), (0, 1), (1, 7), (0, 3), (2, 3)]):
+        ts(v("pj", k, k + 1), v("pi", 0, 1), sh, A.logical_shift_right, msk, A.bitwise_and)
+    cp(v("pc", 0, 5), v("pj", 0, 5))
+    act(SGN, HH, F.Identity, -2.0, 1.0)
+    act(H56, HH, F.Identity, float(H))
+    act(THR, HH, F.Identity, -1.0, -0.5)
+    ts(TMP, S4, 0.0, A.is_equal, 8 * B1K, A.mult)
+    ts(C4, TMP, T4, A.add, -4 * B1K, A.add)
+    ts(Z16, Q16, 0.0, A.is_equal)
+    act(CE, Z16, F.Identity, 2 * B1K, -B1K)
+    act(CB, Z16, F.Identity, 2 * B4M, -B4M - 1)
+    ts(CQ, CB, Q16, A.add, 1.0, A.add)
+    fill(v("za", 0, 128), 0.0)
+    fill(v("cum0", 0, 288, 72), 0.0)
+    fill(v("nd", 384, 448), 0.0)
+    fill(v("ones"), 1.0)
+    act(v("inv0", 0, 528), v("ones"), F.Identity, 0.0)
+    act(v("v2", H, 64), v("ones", 0, 8), F.Identity, 0.0)
+    act(v("sr", 48, 112), v("ones", 0, 64), F.Identity, float(C))
+    act(v("pr", 96, 112), v("ones", 0, 16), F.Identity, float(C))
+    act(v("mt", 448, 512), v("ones", 0, 64), F.Identity, 0.0)
+    act(v("dh", 4 * C, 4 * C + 8), v("ones", 0, 8), F.Identity, 0.0)
+    for t in range(R):
+        act(v("pool%d" % t, 4 * C, 4 * G0), v("ones", 0, 16), F.Identity, 0.0)
+    for t in range(4):
+        act(v("vr%d" % t, 0, 456), v("ones", 0, 456), F.Identity, 0.0)
+    ts(v("seln", 0, 64), v("j8", 0, 64), QQ, A.not_equal, -BIG, A.mult)
+    ts(v("ra8", 0, 64), v("j8", 0, 64), 0.0, A.is_equal, -2 * BIG, A.mult)
+    ts(v("e16", 0, 80), v("j16", 0, 80), Q16, A.is_equal, B1K, A.mult)
+    act(v("e16b", 0, 80), v("e16", 0, 80), F.Identity, -2.0)
+    tt(v("m16", 0, 64), v("e16", 0, 64), v("e16b", 1, 65), A.add)
+    act(v("r1", 0, 64), v("io", 0, 64), F.Identity, -1.0 / (64 * B1K), 1.0)
+    tt(v("m16k", 0, 64), v("e16", 0, 64), v("r1", 0, 64), A.mult)
+    tt(v("m16k", 0, 64), v("m16k", 0, 64), v("e16b", 1, 65), A.add)
+    act(v("cx", 0, 64), v("io", 0, 64), F.Identity, U * 2.0 ** 15, U * OFF)
+    add("g", 170 + 2 * 516, lambda: g.affine_select(T.eye[:, 0:516], T.ones[:, 0:516], [[1, 516]], A.is_equal, 0.0, -3, -4),
+        [v("ones", 0, 516)], [v("eye", 0, 516)])
+    iota(v("ck", 0, 64), [[512, 64]], -int(OFF))
+    for t in range(R):
+        p = PILES[t]
+        iota(v("a1%d" % t, p, p + 2), [[512 + H, 2]], 512 * p + G0 - 2 - int(OFF))
+        iota(v("y%d" % t, p + 2, 64), [[512, 62 - p]], 512 * (p + 2) - int(OFF))
+    iota(v("i16", 0, 24), [[16, 24]], 0)
+    iota(v("li", 0, 392), [[-8, 7], [1, 56]], 0)
+    iota(v("ki", 0, 392), [[0, 7], [1, 56]], 0)
+    iota(v("j4", 0, 116), [[0, 29], [1, 4]], 0)
+    iota(v("kp", 0, 112), [[0, 56], [1024, 2]], 0)
+    iota(v("k3i", 0, 72), [[0, 24], [1, 3]], 0)
+    ts(v("qo", 0, 24), v("i16", 0, 24), 0.0, A.mult, Q16, A.add)
+    act(v("m16n", 0, 384), ind(v("m16", 0, 16), v("qo", 0, 24)), F.Identity, U * B4M / B1K)
+    ts(v("cp", 0, 24), v("i16", 0, 24), CQ, A.add, U, A.mult)
+    ts(v("lc", 0, 392), v("li", 0, 392), QQ, A.is_lt, 2.0 ** -120, A.mult)
+    act(v("kr", 0, 392), v("ki", 0, 392), F.Sign)
+    act(v("k3", 0, 72), v("k3i", 0, 72), F.Sign)
+    ts(v("e4", 0, 116), v("j4", 0, 116), S4, A.is_equal, B1K, A.mult)
+    act(v("e4b", 0, 116), v("e4", 0, 116), F.Identity, -2.0)
+    tt(v("m4", 0, 112), v("e4", 0, 112), v("e4b", 1, 113), A.add)
+    for b in range(4):
+        quant("e", 128 * b, 128 * b + 128, v("eye", 3 - b, 515 - b))
+
+    quant("u", 0, 128, v("ub"))
+    cp(v("uo", 0, 8), v("ui", 0, 8))
+    add("v", 260, lambda: g.vector.tensor_copy(T.qu2[:, 0:128].bitcast(dt.uint32), T.qu[:, 0:128].bitcast(dt.uint32).indirect(ap(v("uo", 0, 8)))),
+        [v("qu"), v("uo", 0, 8)], [v("qu2")])
+    add("s", 280, lambda: g.scalar.activation(T.su2[:, 0:128], T.su[:, 0:128].indirect(ap(v("uo", 0, 8))), F.Copy),
+        [v("su"), v("uo", 0, 8)], [v("su2")])
+    quant("v", 0, 128, v("vb"))
+
+    def derive(t):
+        n = lambda a=0, b=64: v("n%d" % t, a, b)
+        w = lambda name, a=0, b=64, s=1: v(name + str(t), a, b, s)
+        act(w("rr"), n(), F.Relu, 1.0, -1.0)
+        scan(w("cum", 1, 65), w("rr"), v("ones", 0, 64), 0.0, A.add, A.add)
+        scan(w("ed"), w("cum"), v("m16", 0, 64), -B1K, A.max, A.add)
+        ts(w("en", 0, 4), w("ed", 15, 64, 16), CE, A.add)
+        if t == R:
+            return
+        ts(w("en", 4, 8), w("ed", 15, 64, 16), CE, A.add)
+        act(w("vm", 64, 128), n(), F.Sign, 1.0, THR)
+        act(w("vm"), w("vm", 64, 128), F.Identity, BIG / 2, -BIG / 2)
+        tt(w("vm", 64, 128), w("vm"), v("seln", 0, 64), A.min)
+        tt(w("cn"), w("cum"), v("seln", 0, 64), A.add)
+        act(w("inv", 1, 112, 2), w("rr", 0, H), F.Relu, -float(C + 1), float(C + 1))
+
+    def onward(t):
+        p = PILES[t]
+        w = lambda name, a=0, b=64, s=1: v(name + str(t), a, b, s)
+        x = lambda name, a=0, b=64, s=1: v(name + str(t + 1), a, b, s)
+        act(w("mm", 0, p), w("n", 0, p), F.Relu, 1.0, -2.0)
+        act(v("junk", 0, 64), w("n"), F.Sign, acc=w("mm", p, p + 1))
+        act(v("r1", 0, 64), w("rr"), F.Sign, acc=w("mm", p + 1, p + 2))
+        act(w("mq", 0, p + 2), w("mm", 0, p + 2), F.Identity, 2.0 ** 15)
+        tt(w("a1", 0, p), w("cum", 0, p), v("ck", 0, p), A.add)
+        tt(w("y", 0, p + 2), w("a1", 0, p + 2), w("mq", 0, p + 2), A.subtract)
+        scan(w("yv"), w("mm"), v("m16k", 0, 64), -B1K, A.max, A.add)
+        act(w("yt", 0, 4), w("yv", 15, 64, 16), F.Identity, 1.0, CE)
+        act(w("yt", 4, 8), w("yt", 0, 4), F.Identity, -2.0 ** 15, -OFF - 1)
+        for k in range(4):
+            act(v("junk", 64 * k + 64, 64 * k + 128), w("y"), F.Sign, -1.0, w("yt", 4 + k, 5 + k), acc=w("sg4", k, k + 1))
+        ts(w("rk", 0, 4), w("sg4", 0, 4), 0.5, A.mult, 32.0, A.add)
+        cp(ind(w("ys"), w("rk", 0, 4)), w("y"))
+        act(w("wu"), w("ys"), F.Identity, -2.0 ** -15, 1.5 * 2.0 ** 23)
+        act(x("n"), w("wu"), F.Identity, 1.0, -1.5 * 2.0 ** 23)
+        act(w("nq"), x("n"), F.Identity, 2.0 ** 15)
+        tt(w("rest", 0, H), w("ys", 0, H), w("nq", 0, H), A.add)
+        derive(t + 1)
+        tt(w("rest", 0, H), w("rest", 0, H), x("cum", 0, H), A.subtract)
+        act(w("wu", 0, H), w("rest", 0, H), F.Identity, U)
+        tt(v("v2", 0, H), w("wu", 0, H), v("cx", 0, H), A.add)
+        cp(ind(x("vr", 8, 456), x("en", 0, 4)), v("v2", 0, 64))
+        scan(v("hold", 0, C), x("vr", 8, 8 + C), x("vr", 8, 8 + C), 0.0, A.min, A.min)
+        scan(v("dg", 0, C), v("hold", 0, C), v("m16n", 0, C), -U * B4M, A.min, A.add)
+        tt(v("xs", 0, 24), v("dg", 15, C, 16), v("cp", 0, 24), A.add)
+        ts(v("xi", 0, 24), v("xs", 0, 24), 1.0 / U, A.mult)
+        ts(v("xk", 0, 24), v("xi", 0, 24), 9, A.logical_shift_right, 63, A.bitwise_and)
+        ts(w("kl", 0, 24), v("xk", 0, 24), 2.0, A.mult, 1.0, A.add)
+        ts(v("xb", 0, 24), v("xi", 0, 24), 511, A.bitwise_and)
+        cp(w("t3", 0, 72, 3), v("xb", 0, 24))
+        act(w("b1", 0, 24), w("t3", 0, 72, 3), F.Identity, B1K, B1K)
+
+    cp(v("zu", 0, 3), v("zi", 0, 3))
+    cp(v("n0", 0, 48), ind(v("io", 0, 456), v("zu", 0, 3)))
+    derive(0)
+    cp(ind(v("vr0", 8, 456), v("en0", 0, 4)), v("cx", 0, 64))
+    for t in range(R):
+        onward(t)
+    dma("y", lambda: T.oz[:, :], lambda: T.f[0:128:16, AT["n3"][1]:AT["n3"][1] + H], [v("n3", 0, H)], [], 2e3, last=True)
+
+    sent = [0]
+
+    def send(src, dst, sem, peer, codes, nbytes):
+        rid, pid = topo.addr(peer)[:2]
+        m = topo.mask(core, peer)
+        k = len(topo.engines(core, peer))
+        sent[0] += k
+        pick = byt if codes else ap
+        return k, add("g", CALL, lambda: g.remote_dma(pick(dst), pick(src), T.sem[sem], T.sem.sent, pid, rid, m), [src], [],
+                      late=FLY + nbytes / RATE)
+
+    for t in range(R):
+        pool, nxt, xq, lq = "pool%d" % t, "pool%d" % (t + 1), "x%d" % t, "l%d" % t
+        w = lambda name, a=0, b=64, s=1: v(name + str(t), a, b, s)
+        ns = (PILES[t] + 7) // 8
+        peer = T.cores[rank ^ STEP[t]]
+        for k, (c0, c1) in enumerate(CH):
+            quant(xq, c0, c1, v(pool, 4 * c0, 4 * c1))
+            o = mm(k, "u2", 0, xq, c0, c1)
+            act(v("s", c0, c1), o, F.Identity, SGN)
+            scan(v("m", c0, c1, -1), w("vr", 9 + c0, 9 + c1, -1), v("s", c0, c1, -1), v("m", c1, c1 + 1) if k else -BIG, A.add, A.max)
+            act(v("ms", c0, c1), v("m", c0, c1), F.Identity, SGN)
+            tt(v("eq", c0, c1), o, v("ms", c0, c1), A.not_equal)
+            scan(v("nd", c0, c1, -1), v("ones", c0, c1), v("eq", c0, c1, -1), v("nd", c1, c1 + 1), A.add, A.mult)
+        (a0, a1), (b0, b1) = CH[0], (0, CH[0][0])
+        k1, o1 = send(v("q" + xq, a0, a1), v("q" + lq, a0, a1), "qa%d" % t, peer, True, 512 * (a1 - a0))
+        k2, o2 = send(v("s" + xq), v("s" + lq), "qa%d" % t, peer, False, 512 * (a1 - a0) + 49152)
+        k3, o3 = send(v("q" + xq, b0, b1), v("q" + lq, b0, b1), "qb%d" % t, peer, True, 245760)
+        add("x", 0, None, [], [v("q" + lq, a0, a1), v("s" + lq)], after=[o1, o2], sem="qa%d" % t, cnt=k1 + k2)
+        add("x", 0, None, [], [v("q" + lq, b0, b1)], after=[o3], sem="qb%d" % t, cnt=k3)
+        for c0, c1 in ((a0, a1), (b0, b1)):
+            for b in range(4):
+                o = mm(3 + b, "e", 128 * b, lq, c0, c1)
+                act(v("dh", 4 * c0 + b, 4 * c1, 4), o, F.Identity, 0.5)
+        tt(v("rv", 0, 128), ind(v("m", 0, 448), w("en", 0, 8)), w("vm", 0, 128), A.add)
+        scan(v("vb8", 0, H), v("ra8", 0, H), v("rv", 64, 64 + H), 0.0, A.add, A.max)
+        for k in range(ns):
+            if k in VSG:
+                ts(v("sg", H * k, H * k + H), v("rv", 0, H), v("vb8", 8 * k + 7, 8 * k + 8), A.subtract, -1.0, A.mult)
+            else:
+                act(v("sg", H * k, H * k + H), v("rv", 0, H), F.Sign, -1.0, v("vb8", 8 * k + 7, 8 * k + 8))
+        tt(v("tp", 0, 64), ind(v("nd", 0, 448), w("en", 0, 4)), w("cn"), A.add)
+        scan(v("pd", 0, H), v("tp", 0, H), v("tp", 0, H), 0.0, A.max, A.max)
+        cp(v("pu", 0, ns), v("pd", 7, 8 * ns, 8))
+        tt(v("pr", 0, 16 * ns), ind(v("io", 0, 456), v("pu", 0, ns)), w("inv", 0, 16 * ns), A.max)
+        tt(v("ef", 0, 8 * ns), v("pr", 0, 16 * ns, 2), v("pr", 1, 16 * ns, 2), A.is_equal)
+        tt(v("pr", 1, 16 * ns, 2), v("pr", 1, 16 * ns, 2), v("ef", 0, 8 * ns), A.add)
+        tt(v("cc", 0, H * ns), v("sg", 0, H * ns), v("lc", 0, H * ns), A.is_lt)
+        scan(v("rs", 0, H * ns), v("kr", 0, H * ns), v("cc", 0, H * ns), 0.0, A.mult, A.add)
+        ts(v("ru", 0, ns), v("rs", H - 1, H * ns, H), H56, A.add)
+        cp(ind(v("sr", 0, 112), v("ru", 0, ns)), v("pr", 0, 16 * ns))
+        scan(v("sd", 0, 112), v("sr", 0, 112), v("m4", 0, 112), -B1K, A.max, A.add)
+        lst, lin = v("out%d" % t), v("lin%d" % t)
+        ts(lst, v("sd", 3, 112, 4), 4.0, A.mult, C4, A.add)
+        k1, o1 = send(lst, lin, "la%d" % t, peer, False, 7168)
+        add("x", 0, None, [], [lin], after=[o1], sem="la%d" % t, cnt=k1)
+        act(v("ah"), ind(v(pool, 0, 4 * C + 8), lst), F.Identity, 0.5)
+        tt(v("mt", 0, 448), ind(v("dh"), lin), v("ah"), A.add)
+        quant("m", 0, 128, v("mt"))
+        for b in range(4):
+            o = mm((7, 0, 1, 2)[b], "w", 128 * b, "m", 0, 128)
+            act(v("rl", b, 448, 4), (o[0], o[1], o[1] + 112, 1), F.Relu, 0.03125)
+        tt(v(pool, 4 * G0, PW), ind(v(pool, 0, 4 * C + 8), lst), v("rl"), A.add)
+        tt(v("lh", 0, 112, 2), v("pr", 0, 112, 2), v("pr", 1, 112, 2), A.min)
+        tt(v("lh", 1, 112, 2), v("pr", 0, 112, 2), v("pr", 1, 112, 2), A.max)
+        scan(v("pk", 0, 112), v("kp", 0, 112), v("lh", 0, 112), 0.0, A.mult, A.add)
+        act(v("pkr", 0, C), ind(v("pk", 0, 112), w("kl", 0, 24)), F.Identity, U)
+        scan(v("pkd", 0, C), v("pkr", 0, C), v("m16n", 0, C), -U * B4M, A.min, A.add)
+        ts(v("ki2", 0, 24), v("pkd", 15, C, 16), 1.0 / U, A.mult, CB, A.add)
+        ts(v("hi", 0, 24), v("ki2", 0, 24), 1023, A.bitwise_and)
+        tt(w("t3", 1, 72, 3), v("ki2", 0, 24), w("b1", 0, 24), A.is_lt)
+        tt(w("t3", 2, 72, 3), v("hi", 0, 24), w("t3", 0, 72, 3), A.is_le)
+        scan(v("t3o", 0, 72), v("k3", 0, 72), w("t3", 0, 72), 0.0, A.mult, A.add)
+        for b in range(4):
+            ts(w("el", 24 * b, 24 * b + 24), v("t3o", 2, 72, 3), 4.0, A.mult, float(b), A.add)
+        for k, (c0, c1) in enumerate(CH):
+            for b in range(4):
+                o, s = v(nxt, 4 * c0 + b, 4 * c1, 4), ind(v(pool), w("el", 24 * b + c0 // 16, 24 * b + c1 // 16))
+                if b in VPL[t][k]:
+                    cp(o, s)
+                else:
+                    act(o, s, F.Identity)
+
+    for k, (c0, c1) in enumerate(CH):
+        quant("x3", c0, c1, v("pool3", 4 * c0, 4 * c1))
+        o = mm(k, "v", 0, "x3", c0, c1)
+        if k % 2:
+            cp(v("yb", c0, c1), o)
+        else:
+            act(v("yb", c0, c1), o, F.Identity)
+        dma("y", lambda c0=c0, c1=c1: T.oc[:, 4 * c0:4 * c1], lambda c0=c0, c1=c1: byt(v("qx3", c0, c1)), [v("qx3", c0, c1)], [], 98e3, last=True)
+        dma("sy"[k % 2], lambda c0=c0, c1=c1: T.y[:, c0:c1], lambda c0=c0, c1=c1: T.yb[:, c0:c1], [v("yb", c0, c1)], [], 98e3, last=True)
+    for k in range(4):
+        dma("ys"[k % 2], lambda k=k: T.osc[4 * k:4 * k + 4, :], lambda k=k: T.sx3[32 * k:32 * k + 4, :], [v("sx3")], [], 2e3, last=True)
+    return ops, sent[0]
+
+
+def cells(d):
+    if d[0] == "ps":
+        return d[0], {d[1] // 512}
+    return d[0], set(range(d[1], d[2], abs(d[3])))
+
+
+def order(ops):
+    n = len(ops)
+    deps = [set(o.get("after", [])) for o in ops]
+    seen = {}
+    for j, o in enumerate(ops):
+        for wr, ds in ((False, o["rd"]), (True, o["wr"])):
+            for d in ds:
+                name, c = cells(d)
+                for i, wi, ci in seen.get(name, []):
+                    if i != j and (wr or wi or (name == "ps" and ops[i]["q"] != o["q"])) and not c.isdisjoint(ci):
+                        deps[j].add(i)
+        for wr, ds in ((False, o["rd"]), (True, o["wr"])):
+            for d in ds:
+                name, c = cells(d)
+                if wr:
+                    seen[name] = [e for e in seen.get(name, []) if not e[2] <= c]
+                seen.setdefault(name, []).append((j, wr, c))
+    kids = [[] for _ in ops]
+    for j in range(n):
+        for i in deps[j]:
+            kids[i].append(j)
+    tail = [0.0] * n
+    for j in range(n - 1, -1, -1):
+        tail[j] = ops[j]["cost"] + ops[j]["late"] + max([WAKE + tail[k] for k in kids[j]] + [0.0])
+    rng = np.random.default_rng(7)
+    best, prio = None, np.array(tail)
+    for turn in range(TURNS):
+        p = prio + (rng.standard_normal(n) * 700.0 * (rng.random(n) < 0.04) if turn else 0.0)
+        seq, end = lay(ops, deps, kids, p)
+        if best is None or end <= best[1]:
+            best, prio = (seq, end), p
+    return deps, best[0], best[1]
+
+
+def lay(ops, deps, kids, tail):
+    done, free, seq, can = {}, {}, [], {}
+    left = [len(d) for d in deps]
+    ready = [j for j in range(len(ops)) if not left[j]]
+    for j in ready:
+        can[j] = 0.0
+    while ready:
+        est = {j: max(free.get(ops[j]["q"], 0.0), can[j]) for j in ready}
+        c = min(ready, key=lambda j: (est[j], -tail[j]))
+        near = [j for j in ready if ops[j]["q"] == ops[c]["q"] and est[j] <= est[c] + NEAR * ops[c]["cost"]]
+        c = max(near, key=lambda j: tail[j])
+        ready.remove(c)
+        seq.append((c, est[c]))
+        if ops[c]["q"] != "x":
+            free[ops[c]["q"]] = est[c] + ops[c]["cost"]
+        done[c] = est[c] + ops[c]["cost"] + ops[c]["late"]
+        for k in kids[c]:
+            left[k] -= 1
+            if not left[k]:
+                ready.append(k)
+                can[k] = max(done[i] + WAKE for i in deps[k])
+    return seq, max(done.values())
+
+
+def rank_program(g, core, T, topo):
+    rank = T.rank_of(core)
+    if rank is None:
+        return
+    ops, sent = collect(g, T, topo, core, rank)
+    if "order" not in KEPT:
+        KEPT["order"] = order(ops)
+    deps, seq, _ = KEPT["order"]
+    seq = [j for j, _t in seq if ops[j]["q"] != "x"]
+    at = {j: k for k, j in enumerate(seq)}
+    known, before, waits, need = {}, {}, {}, set()
+    for j in seq:
+        kn = known.setdefault(ops[j]["q"], set())
+        waits[j] = []
+        for i in sorted(deps[j], key=lambda i: -at.get(i, 10 ** 6)):
+            if i not in kn:
+                waits[j].append(i)
+                need.add(i)
+                kn.add(i)
+                kn |= before.get(i, set())
+        before[j] = set(kn)
+    last = [j for j in seq if ops[j].get("last")]
+    need |= set(last)
+    sig, user, count, nd = {}, [None] * NSEM, [0] * NSEM, 0
+    for j, o in enumerate(ops):
+        if o["q"] == "x":
+            sig[j] = (o["sem"], o["cnt"])
+    for j in seq:
+        if j not in need:
+            continue
+        if ops[j].get("dma"):
+            sig[j] = ("d%d" % nd, 16)
+            nd += 1
+            continue
+        k = [k for k in range(NSEM) if user[k] is None or user[k] in before[j]][0]
+        user[k] = j
+        count[k] += 1
+        sig[j] = ("c%d" % k, count[k])
+    eng = {"v": g.vector, "s": g.scalar, "t": g.tensor, "y": g.sync, "g": g}
+    for j in seq:
+        o = ops[j]
+        for i in waits[j]:
+            eng[o["q"]].wait_ge(T.sem[sig[i][0]], sig[i][1])
+        ins = o["fn"]()
+        if j in need:
+            ins.then_inc(T.sem[sig[j][0]], 16 if o.get("dma") else 1)
+    for j in last:
+        g.sync.wait_ge(T.sem[sig[j][0]], 16)
+    g.wait_ge(T.sem.sent, sent)

@@ -1,20 +1,20 @@
 import numpy as np
 from concourse.mybir import dt, AluOpType as A, ActivationFunctionType as F
 
-C, H, R = 384, 56, 3
-PILES = [48, 50, 52]
+C, H, R, P0 = 384, 56, 3, 48
 STEP = [1, 2, 1]
-G0 = 388
-PW = 4 * (G0 + 2 * H)
+G0 = [388, 452, 452]
 CH = [(192, 384), (0, 192)]
-VPL = [[(0, 1), (0, 1)]] * 3
-VSG = (0,)
-BIG = 2.0 ** 96
+SEND = [(192, 384), (0, 192)]
+BIG = 2.0 ** 80
 U = -2.0 ** 75
-B1K, B4M = 1024.0, 2.0 ** 22
-OFF = 16383.0
-WAKE, NEAR, TURNS = 100.0, 0.4, 1500
-FLY, RATE, CALL = 1800.0, 80.0, 400.0
+B1K, LIFT = 1024.0, 2.0 ** 24
+MAGIC = 1.5 * 2.0 ** 23
+OFF = 13112.0
+NEW = 50 * 512
+EARLY = [True, True, True]
+CYC, SFIX, WAKE, NEAR, TURNS, SLACK = 1.04, 40.0, 120.0, 0.4, 12000, 150.0
+FLY, RATE, CALL, FIRST, LOAD = 1500.0, 80.0, 300.0, 1000.0, 1400.0
 
 ARENA = {"f": 0, "h": 0, "i": 0, "w": 0}
 AT = {}
@@ -27,32 +27,25 @@ def _take(ar, name, n):
     ARENA[ar] += (n + al - 1) // al * al
 
 
-for _n, _k in [("m", 384), ("za", 64), ("n0", 64), ("inv0", 112), ("inv1", 112), ("inv2", 112), ("mm0", 64), ("mm1", 64),
-               ("mm2", 64), ("cum0", 72), ("cum1", 72), ("cum2", 72), ("cum3", 72), ("v2", 64), ("nd", 448),
-               ("s", 384), ("ms", 384), ("io", 456), ("pc", 16), ("j16", 80), ("j8", 64), ("j4", 116), ("e16", 80),
-               ("e16b", 80), ("e4", 116), ("e4b", 116), ("m16", 64), ("m16k", 64), ("m16n", 384), ("m4", 112), ("seln", 64),
-               ("ra8", 64), ("kp", 112), ("k3i", 72), ("k3", 72), ("ck", 64), ("cx", 64), ("i16", 24),
-               ("cp", 24), ("rv", 128), ("vb8", 64), ("tp", 64), ("pd", 64), ("pr", 112), ("ef", 56), ("sr", 112),
-               ("sd", 112), ("lh", 112), ("pk", 112), ("pkr", 384), ("pkd", 384), ("t3o", 72), ("junk", 320), ("r1", 64),
-               ("hold", 384), ("dg", 384), ("xs", 24)]:
+for _n, _k in [("m", 448), ("s", 384), ("ms", 384), ("tb", 392), ("pc", 16), ("j16", 64), ("j8", 64), ("j4", 112),
+               ("m16", 64), ("l16", 32), ("lift", 384), ("m4", 112), ("sel", 64), ("down", 64), ("up", 64), ("kp", 112),
+               ("k3", 72), ("i16", 48), ("cj", 48), ("c513", 48), ("c1k", 64), ("k2", 136), ("junk", 640), ("id", 64), ("mq", 64),
+               ("y", 64), ("yv", 64), ("sg4", 8), ("ys", 64), ("wu", 64), ("nq", 64), ("rest", 64), ("oz", 64),
+               ("rv", 128), ("vb8", 64), ("tp", 64), ("pd", 64), ("p0", 112), ("pr", 112), ("sr", 112), ("sd", 112),
+               ("lh", 112), ("pk", 112), ("pkr", 384), ("pkd", 384), ("t3o", 72), ("hold", 384), ("dg", 1152),
+               ("t3", 216), ("b1", 72), ("vr0", 456), ("vr1", 1032), ("vr2", 520), ("vr3", 456)]:
     _take("f", _n, _k)
 for _t in range(4):
-    for _n, _k in [("vr", 456), ("rr", 64), ("ed", 64)]:
+    for _n, _k in [("cum", 72), ("d", 72), ("r", 64), ("nv", 64), ("g", 64), ("born", 64), ("bc", 64), ("e", 64), ("ed", 64),
+                   ("p", 128), ("fa", 64), ("fx", 112), ("pay", 64), ("v2", 64)]:
         _take("f", _n + str(_t), _k)
-    _take("w", "en%d" % _t, 8)
-    if _t:
-        _take("f", "n%d" % _t, 64)
-for _t in range(R):
-    for _n, _k in [("vm", 128), ("cn", 64), ("a1", 64), ("mq", 64), ("y", 64), ("yt", 8), ("yv", 64), ("sg4", 8),
-                   ("ys", 64), ("nq", 64), ("rest", 64), ("wu", 64), ("t3", 72), ("b1", 24)]:
-        _take("f", _n + str(_t), _k)
-    for _n, _k in [("kl", 24), ("rk", 4), ("el", 96)]:
-        _take("w", _n + str(_t), _k)
-for _n, _k in [("eq", 384), ("sg", 392), ("cc", 392), ("rs", 392), ("lc", 392), ("li", 392), ("kr", 392), ("ki", 392)]:
+    _take("w", "en%d" % _t, 12)
+    _take("w", "el%d" % _t, 96)
+for _n, _k in [("eq", 384), ("pos", 448), ("qr", 384), ("sg", 392), ("cc", 392), ("rs", 392), ("lc", 392), ("li", 392), ("kr", 392)]:
     _take("h", _n, _k)
-for _n, _k in [("pi", 8), ("pj", 8), ("ui", 8), ("xi", 24), ("xk", 24), ("xb", 24), ("ki2", 24), ("hi", 24)]:
+for _n, _k in [("pi", 8), ("pj", 8), ("ui", 8), ("xi", 72), ("xk", 72), ("xb", 72), ("ki2", 24), ("hi", 24)]:
     _take("i", _n, _k)
-for _n, _k in [("zu", 4), ("uo", 8), ("qo", 24), ("pu", 8), ("ru", 8)]:
+for _n, _k in [("zu", 4), ("uo", 8), ("qo", 24), ("pu", 8), ("ru", 8), ("rk", 4), ("kl", 72)]:
     _take("w", _n, _k)
 
 X4, U8, BF, F32 = "float8_e4m3fn_x4", "uint8", "bfloat16", "float32"
@@ -61,14 +54,14 @@ SCRATCH = {"f": ("sbuf", [128, ARENA["f"]], F32), "h": ("sbuf", [128, ARENA["h"]
            "zi": ("sbuf", [128, 4], "int32"), "ps": ("psum", [128, 4096], F32),
            "pool3": ("sbuf", [128, 4 * C], BF), "ub": ("sbuf", [128, 512], BF), "vb": ("sbuf", [128, 512], BF),
            "ones": ("sbuf", [128, 528], BF), "eye": ("sbuf", [128, 528], BF), "mt": ("sbuf", [128, 512], BF),
-           "ah": ("sbuf", [128, 448], BF), "rl": ("sbuf", [128, 448], F32), "dh": ("sbuf", [128, 4 * C + 8], F32),
-           "yb": ("sbuf", [128, C], F32)}
+           "ah": ("sbuf", [128, 448], BF), "aa": ("sbuf", [128, 512], BF), "rl": ("sbuf", [128, 448], F32),
+           "dh": ("sbuf", [128, 4 * C + 8], F32), "yb": ("sbuf", [128, C], F32)}
 for _n, _k in [("u", 128), ("u2", 128), ("v", 128), ("w", 512), ("e", 512), ("m", 128), ("x0", C), ("x1", C), ("x2", C), ("x3", C),
-               ("l0", C), ("l1", C), ("l2", C)]:
+               ("l0", C), ("l1", C), ("l2", C), ("a0", 128), ("a1", 128), ("a2", 128)]:
     SCRATCH["q" + _n] = ("sbuf", [128, _k], X4)
     SCRATCH["s" + _n] = ("sbuf", [128, _k], U8)
 for _t in range(R):
-    SCRATCH["pool%d" % _t] = ("sbuf", [128, PW], BF)
+    SCRATCH["pool%d" % _t] = ("sbuf", [128, 4 * (G0[_t] + 2 * H)], BF)
     SCRATCH["out%d" % _t] = ("sbuf", [128, 28], "uint16")
     SCRATCH["lin%d" % _t] = ("sbuf", [128, 28], "uint16")
 NSEM, NDMA = 110, 26
@@ -115,43 +108,44 @@ def collect(g, T, topo, core, rank):
             return T[d[0]][:, d[2] - 1:d[1] - 1:-1] if d[1] else T[d[0]][:, d[2] - 1::-1]
         return T[d[0]][:, d[1]:d[2]:d[3]] if d[3] > 1 else T[d[0]][:, d[1]:d[2]]
 
-    def add(q, cost, fn, rd, wr, late=0.0, **k):
-        ops.append(dict(q=q, cost=cost, fn=fn, rd=places(rd), wr=places(wr), late=late, **k))
+    def add(ways, rd, wr, late=0.0, **k):
+        ops.append(dict(ways=ways, rd=places(rd), wr=places(wr), late=late, **k))
         return len(ops) - 1
 
     def cyc(out, ins, k=1.0):
-        n = size(out) if out[0] != "@" else size(ins[0])
         if out[0] == "@":
-            return 60 + 3.8 * n
+            return 50 + CYC * 3.8 * size(out)
         if ins and ins[0][0] == "@":
-            return 60 + 1.56 * n
+            return 50 + CYC * 1.56 * size(out)
         if all(two(d) for d in [out] + ins):
             k *= 0.5
-        return max(64.0, n * k)
+        return CYC * max(64.0, size(out) * k)
 
     def tt(out, a, b, op):
-        add("v", cyc(out, [a, b], 1 if "ps" in (a[0], b[0]) else 2), lambda: g.vector.tensor_tensor(ap(out), ap(a), ap(b), op), [a, b], [out])
+        c = cyc(out, [a, b], 1 if "ps" in (a[0], b[0]) else 2)
+        add([("v", c, lambda: g.vector.tensor_tensor(ap(out), ap(a), ap(b), op))], [a, b], [out])
+
+    def vts(out, a, s1, op0, s2=None, op1=None):
+        if op1 is None:
+            return ("v", cyc(out, [a]), lambda: g.vector.tensor_scalar(ap(out), ap(a), ap(s1), None, op0))
+        return ("v", cyc(out, [a]), lambda: g.vector.tensor_scalar(ap(out), ap(a), ap(s1), ap(s2), op0, op1))
 
     def ts(out, a, s1, op0, s2=None, op1=None):
-        if op1 is None:
-            fn = lambda: g.vector.tensor_scalar(ap(out), ap(a), ap(s1), None, op0)
-        else:
-            fn = lambda: g.vector.tensor_scalar(ap(out), ap(a), ap(s1), ap(s2), op0, op1)
-        add("v", cyc(out, [a]), fn, [a, s1, s2], [out])
+        add([vts(out, a, s1, op0, s2, op1)], [a, s1, s2], [out])
+
+    def vcp(out, a):
+        return ("v", cyc(out, [a]), lambda: g.vector.tensor_copy(ap(out), ap(a)))
 
     def cp(out, a):
         if out[0] == "@":
-            add("v", cyc(out, [a]), lambda: g.vector.tensor_copy(ap(out), ap(a)), [a, out[2]], [out[1]])
+            add([vcp(out, a)], [a, out[2]], [out[1]])
         else:
-            add("v", cyc(out, [a]), lambda: g.vector.tensor_copy(ap(out), ap(a)), [a], [out])
+            add([vcp(out, a)], [a], [out])
 
     def scan(out, d0, d1, init, op0, op1):
-        add("v", cyc(out, [d0, d1]), lambda: g.vector.tensor_tensor_scan(ap(out), ap(d0), ap(d1), ap(init), op0, op1), [d0, d1, init], [out])
+        add([("v", cyc(out, [d0, d1]), lambda: g.vector.tensor_tensor_scan(ap(out), ap(d0), ap(d1), ap(init), op0, op1))], [d0, d1, init], [out])
 
-    def fill(out, c):
-        add("v", cyc(out, []), lambda: g.vector.memset(ap(out), c), [], [out])
-
-    def act(out, a, fn, scale=None, bias=None, acc=None):
+    def sact(out, a, fn, scale=None, bias=None, acc=None):
         k = {}
         if scale is not None:
             k["scale"] = scale
@@ -159,34 +153,62 @@ def collect(g, T, topo, core, rank):
             k["bias"] = bias
         if acc is not None:
             k["accum_out"] = acc
-        c = 20 + (cyc(out, [a]) if a[0] == "@" else max(64.0, size(out)))
-        add("s", c, lambda: g.scalar.activation(ap(out), ap(a), fn, **{x: ap(y) for x, y in k.items()}), [a, scale, bias], [out, acc])
+        c = 15 + cyc(out, [a]) if a[0] == "@" else SFIX + CYC * max(64.0, size(out)) + (20 if acc else 0)
+        return ("s", c, lambda: g.scalar.activation(ap(out), ap(a), fn, **{x: ap(y) for x, y in k.items()}))
 
-    def iota(out, pat, base, cm=0):
+    def act(out, a, fn, scale=None, bias=None, acc=None):
+        add([sact(out, a, fn, scale, bias, acc)], [a, scale, bias], [out, acc])
+
+    def lin(out, a, scale=None, bias=None):
+        if scale is None and bias is None:
+            w = vcp(out, a)
+        elif bias is None:
+            w = vts(out, a, scale, A.mult)
+        elif scale is None:
+            w = vts(out, a, bias, A.add)
+        else:
+            w = vts(out, a, scale, A.mult, bias, A.add)
+        add([sact(out, a, F.Identity, scale, bias), w], [a, scale, bias], [out])
+
+    def relu(out, a, scale=None, bias=None):
+        ways = [sact(out, a, F.Relu, scale, bias)]
+        if bias is None:
+            ways.append(vts(out, a, scale, A.mult, 0.0, A.max))
+        elif scale is None:
+            ways.append(vts(out, a, bias, A.add, 0.0, A.max))
+        add(ways, [a, scale, bias], [out])
+
+    def giota(out, pat, base, cm=0):
         if SCRATCH[out[0]][2] == "int32":
             fn = lambda: g.iota(ap(out), pat, base, cm)
         else:
             fn = lambda: g.iota(ap(out), pat, base, cm, allow_small_or_imprecise_dtypes=True)
-        add("g", 130 + 2 * size(out), fn, [], [out])
+        return ("g", 130 + 2 * CYC * size(out), fn)
+
+    def iota(out, pat, base, cm=0):
+        add([giota(out, pat, base, cm)], [], [out])
+
+    def fill(out, c):
+        add([("v", cyc(out, []), lambda: g.vector.memset(ap(out), float(c))), giota(out, [[0, size(out)]], int(c))], [], [out])
 
     def quant(name, c0, c1, src):
         q, s = v("q" + name, c0, c1), v("s" + name, c0, c1)
-        add("v", 12 + 0.22 * size(src), lambda: g.vector.quantize_mx(ap(q), ap(s), ap(src)), [src], [q, s])
+        add([("v", (12 + 0.22 * size(src)) * CYC / 0.83, lambda: g.vector.quantize_mx(ap(q), ap(s), ap(src)))], [src], [q, s])
 
     def mm(bank, st, s0, mv, c0, c1):
         out = v("ps", 512 * bank, 512 * bank + c1 - c0)
         a, b, c, d = v("q" + st, s0, s0 + 128), v("s" + st, s0, s0 + 128), v("q" + mv, c0, c1), v("s" + mv, c0, c1)
-        add("t", 1.2 * (c1 - c0 + 16), lambda: g.tensor.matmul_mx(ap(out), ap(a), ap(b), ap(c), ap(d), True, True), [a, b, c, d], [out])
+        add([("t", 1.0 * (c1 - c0 + 16), lambda: g.tensor.matmul_mx(ap(out), ap(a), ap(b), ap(c), ap(d), True, True))], [a, b, c, d], [out])
         return out
 
     def dma(q, out, src, rd, wr, nbytes, last=False):
         e = g.sync if q == "y" else g.scalar
-        add(q, 60, lambda: e.dma_start(out(), src()), rd, wr, late=1800 + nbytes / 200.0, dma=True, last=last)
+        add([(q, 60, lambda: e.dma_start(out(), src()))], rd, wr, late=LOAD + nbytes / 200.0, dma=True, last=last)
 
     def byt(d):
         return ap(d).bitcast(dt.uint8)
 
-    Q16, HH, QQ, T4, S4, SGN, H56, THR, C4, CE, CB, CQ, TMP, Z16 = [v("pc", k, k + 1) for k in range(14)]
+    Q16, HH, QQ, T4, S4, SGN, H56, THR, C4, TMP, CE = [v("pc", k, k + 1) for k in range(11)]
 
     dma("y", lambda: T.zi[:, 0:3], lambda: T.z[:, :], [], [v("zi", 0, 3)], 2e3)
     dma("s", lambda: T.ub[:, :], lambda: T.u[:, :], [], [v("ub")], 131e3)
@@ -198,139 +220,152 @@ def collect(g, T, topo, core, rank):
     dma("y", lambda: T.vb[:, :], lambda: T.v[:, :], [v("pool0", 0, 4 * C)], [v("vb")], 460e3)
 
     iota(v("pi", 0, 1), [[0, 1]], 0, 1)
-    iota(v("j16", 0, 80), [[0, 5], [1, 16]], 0)
-    iota(v("io", 0, 385), [[1, 385]], 0)
-    ops[-1]["after"] = [len(ops) - 3]
-    iota(v("io", 385, 456), [[0, 71]], C)
+    iota(v("tb", 1, 386), [[1, 385]], 0)
+    fill(v("tb", 0, 1), C)
+    iota(v("j16", 0, 64), [[0, 4], [1, 16]], 0)
     iota(v("j8", 0, 64), [[0, 8], [1, 8]], 0)
     iota(v("ui", 0, 8), [[16, 8]], 0)
     for k, (sh, msk) in enumerate([(0, 15), (0, 1), (1, 7), (0, 3), (2, 3)]):
         ts(v("pj", k, k + 1), v("pi", 0, 1), sh, A.logical_shift_right, msk, A.bitwise_and)
     cp(v("pc", 0, 5), v("pj", 0, 5))
-    act(SGN, HH, F.Identity, -2.0, 1.0)
-    act(H56, HH, F.Identity, float(H))
-    act(THR, HH, F.Identity, -1.0, -0.5)
-    ts(TMP, S4, 0.0, A.is_equal, 8 * B1K, A.mult)
-    ts(C4, TMP, T4, A.add, -4 * B1K, A.add)
-    ts(Z16, Q16, 0.0, A.is_equal)
-    act(CE, Z16, F.Identity, 2 * B1K, -B1K)
-    act(CB, Z16, F.Identity, 2 * B4M, -B4M - 1)
-    ts(CQ, CB, Q16, A.add, 1.0, A.add)
-    fill(v("za", 0, 128), 0.0)
-    fill(v("cum0", 0, 288, 72), 0.0)
-    fill(v("nd", 384, 448), 0.0)
-    fill(v("ones"), 1.0)
-    act(v("inv0", 0, 528), v("ones"), F.Identity, 0.0)
-    act(v("v2", H, 64), v("ones", 0, 8), F.Identity, 0.0)
-    act(v("sr", 48, 112), v("ones", 0, 64), F.Identity, float(C))
-    act(v("pr", 96, 112), v("ones", 0, 16), F.Identity, float(C))
-    act(v("mt", 448, 512), v("ones", 0, 64), F.Identity, 0.0)
-    act(v("dh", 4 * C, 4 * C + 8), v("ones", 0, 8), F.Identity, 0.0)
+    lin(SGN, HH, -2.0, 1.0)
+    lin(H56, HH, float(H))
+    lin(THR, HH, BIG, BIG / 2)
+    lin(TMP, S4, 2 * B1K, -B1K)
+    ts(C4, TMP, 2.0, A.mult, T4, A.add)
+    lin(C4, C4, None, 18 * B1K)
+    add([("v", cyc(v("ones"), []), lambda: g.vector.memset(T.ones[:, :], 0.5))], [], [v("ones")])
+    fill(v("aa", 448, 512), 0)
+    fill(v("m", C, 448), 0)
+    fill(v("pos", C, 448), 0)
+    for name in ("cum", "d"):
+        for t in range(4):
+            fill(v(name + str(t), 0, 1), 0)
+    fill(v("id", 0, 1), 0)
+    fill(v("r0", P0, 64), 0)
+    fill(v("nv0", P0, 64), 0)
+    fill(v("k2", 0, 66), 1000)
+    fill(v("k2", 66 + P0, 67 + P0), 2 * (P0 + 2))
+    fill(v("k2", 66 + P0 + 6, 130), 0)
+    fill(v("c513", 0, 48), 513)
+    fill(v("born0", 0, 64), 1)
+    fill(v("c1k", 0, 64), 1 - 1024)
+    fill(v("sr", P0, 112), C)
+    fill(v("pr", 2 * P0, 112), C)
+    fill(v("mt", 448, 512), 0)
+    fill(v("dh", 4 * C, 4 * C + 8), 0)
     for t in range(R):
-        act(v("pool%d" % t, 4 * C, 4 * G0), v("ones", 0, 16), F.Identity, 0.0)
+        fill(v("pool%d" % t, 4 * C, 4 * G0[t]), 0)
+        fill(v("fx%d" % t, 0, 112, 2), 0)
     for t in range(4):
-        act(v("vr%d" % t, 0, 456), v("ones", 0, 456), F.Identity, 0.0)
-    ts(v("seln", 0, 64), v("j8", 0, 64), QQ, A.not_equal, -BIG, A.mult)
-    ts(v("ra8", 0, 64), v("j8", 0, 64), 0.0, A.is_equal, -2 * BIG, A.mult)
-    ts(v("e16", 0, 80), v("j16", 0, 80), Q16, A.is_equal, B1K, A.mult)
-    act(v("e16b", 0, 80), v("e16", 0, 80), F.Identity, -2.0)
-    tt(v("m16", 0, 64), v("e16", 0, 64), v("e16b", 1, 65), A.add)
-    act(v("r1", 0, 64), v("io", 0, 64), F.Identity, -1.0 / (64 * B1K), 1.0)
-    tt(v("m16k", 0, 64), v("e16", 0, 64), v("r1", 0, 64), A.mult)
-    tt(v("m16k", 0, 64), v("m16k", 0, 64), v("e16b", 1, 65), A.add)
-    act(v("cx", 0, 64), v("io", 0, 64), F.Identity, U * 2.0 ** 15, U * OFF)
-    add("g", 170 + 2 * 516, lambda: g.affine_select(T.eye[:, 0:516], T.ones[:, 0:516], [[1, 516]], A.is_equal, 0.0, -3, -4),
-        [v("ones", 0, 516)], [v("eye", 0, 516)])
-    iota(v("ck", 0, 64), [[512, 64]], -int(OFF))
-    for t in range(R):
-        p = PILES[t]
-        iota(v("a1%d" % t, p, p + 2), [[512 + H, 2]], 512 * p + G0 - 2 - int(OFF))
-        iota(v("y%d" % t, p + 2, 64), [[512, 62 - p]], 512 * (p + 2) - int(OFF))
-    iota(v("i16", 0, 24), [[16, 24]], 0)
-    iota(v("li", 0, 392), [[-8, 7], [1, 56]], 0)
-    iota(v("ki", 0, 392), [[0, 7], [1, 56]], 0)
-    iota(v("j4", 0, 116), [[0, 29], [1, 4]], 0)
-    iota(v("kp", 0, 112), [[0, 56], [1024, 2]], 0)
-    iota(v("k3i", 0, 72), [[0, 24], [1, 3]], 0)
+        fill(v("vr%d" % t, 8, 400), 0)
+    fill(v("pay3", 0, 64), -1)
+    lin(v("v23", 0, 64), v("pay3", 0, 64), -U)
+    iota(v("id", P0, P0 + 6), [[512, 3], [H, 2]], NEW - 512 + G0[0] - 2)
+    iota(v("id", P0 + 6, 64), [[1, 10]], 0)
+    ts(v("sel", 0, 64), v("j8", 0, 64), QQ, A.not_equal, BIG * 2.0 ** 13, A.mult)
+    ts(v("down", 0, 64), v("j8", 0, 64), 0.0, A.is_equal, -BIG * 2.0 ** 15, A.mult)
+    lin(v("up", 0, 64), v("down", 0, 64), -1.0)
+    ts(v("m16", 0, 64), v("j16", 0, 64), Q16, A.subtract, 4 * B1K, A.mult)
+    ts(v("m16", 0, 64), v("m16", 0, 64), 2 * B1K, A.add, 2 * B1K, A.min)
+    lin(CE, Q16, 2 * B1K, 32 * B1K)
+    ts(v("l16", 0, 16), v("j16", 0, 16), Q16, A.is_equal, LIFT, A.mult)
+    ts(v("l16", 16, 32), v("j16", 0, 16), Q16, A.is_gt)
+    tt(v("l16", 0, 16), v("l16", 0, 16), v("l16", 16, 32), A.add)
+    lin(v("l16", 15, 16), v("l16", 15, 16), 1.0 / (U * LIFT))
+    lin(v("m16", 15, 64, 16), v("m16", 15, 64, 16), None, -64 * B1K)
+    iota(v("i16", 0, 48), [[0, 2], [16, 24]], 0)
     ts(v("qo", 0, 24), v("i16", 0, 24), 0.0, A.mult, Q16, A.add)
-    act(v("m16n", 0, 384), ind(v("m16", 0, 16), v("qo", 0, 24)), F.Identity, U * B4M / B1K)
-    ts(v("cp", 0, 24), v("i16", 0, 24), CQ, A.add, U, A.mult)
+    lin(v("lift", 0, C), ind(v("l16", 0, 16), v("qo", 0, 24)))
+    lin(v("cj", 0, 48), v("i16", 0, 48), None, Q16)
+    lin(v("qr", 0, C), v("tb", 1, C + 1), -1.0 / 512, 0.375)
+    add([("g", 170 + 2 * CYC * 516, lambda: g.affine_select(T.eye[:, 0:516], T.ones[:, 0:516], [[1, 516]], A.is_equal, 0.0, -3, -4))],
+        [v("ones", 0, 516)], [v("eye", 0, 516)])
+    iota(v("li", 0, 392), [[-8, 7], [1, H]], 0)
+    iota(v("kr", 0, 392), [[0, 7], [64, H]], 0)
+    iota(v("j4", 0, 112), [[0, 28], [2048, 4]], 0)
+    iota(v("kp", 0, 112), [[0, H], [1024, 2]], 0)
+    iota(v("k3", 0, 72), [[0, 24], [1024, 3]], 0)
     ts(v("lc", 0, 392), v("li", 0, 392), QQ, A.is_lt, 2.0 ** -120, A.mult)
-    act(v("kr", 0, 392), v("ki", 0, 392), F.Sign)
-    act(v("k3", 0, 72), v("k3i", 0, 72), F.Sign)
-    ts(v("e4", 0, 116), v("j4", 0, 116), S4, A.is_equal, B1K, A.mult)
-    act(v("e4b", 0, 116), v("e4", 0, 116), F.Identity, -2.0)
-    tt(v("m4", 0, 112), v("e4", 0, 112), v("e4b", 1, 113), A.add)
+    ts(v("m4", 0, 112), v("j4", 0, 112), TMP, A.subtract, B1K, A.min)
+    lin(v("m4", 3, 112, 4), v("m4", 3, 112, 4), None, -8 * B1K)
     for b in range(4):
         quant("e", 128 * b, 128 * b + 128, v("eye", 3 - b, 515 - b))
 
     quant("u", 0, 128, v("ub"))
     cp(v("uo", 0, 8), v("ui", 0, 8))
-    add("v", 260, lambda: g.vector.tensor_copy(T.qu2[:, 0:128].bitcast(dt.uint32), T.qu[:, 0:128].bitcast(dt.uint32).indirect(ap(v("uo", 0, 8)))),
+    add([("v", 260, lambda: g.vector.tensor_copy(T.qu2[:, 0:128].bitcast(dt.uint32), T.qu[:, 0:128].bitcast(dt.uint32).indirect(ap(v("uo", 0, 8)))))],
         [v("qu"), v("uo", 0, 8)], [v("qu2")])
-    add("s", 280, lambda: g.scalar.activation(T.su2[:, 0:128], T.su[:, 0:128].indirect(ap(v("uo", 0, 8))), F.Copy),
+    add([("s", 280, lambda: g.scalar.activation(T.su2[:, 0:128], T.su[:, 0:128].indirect(ap(v("uo", 0, 8))), F.Copy))],
         [v("su"), v("uo", 0, 8)], [v("su2")])
     quant("v", 0, 128, v("vb"))
 
-    def derive(t):
-        n = lambda a=0, b=64: v("n%d" % t, a, b)
+    def starts(t, e):
         w = lambda name, a=0, b=64, s=1: v(name + str(t), a, b, s)
-        act(w("rr"), n(), F.Relu, 1.0, -1.0)
-        scan(w("cum", 1, 65), w("rr"), v("ones", 0, 64), 0.0, A.add, A.add)
-        scan(w("ed"), w("cum"), v("m16", 0, 64), -B1K, A.max, A.add)
-        ts(w("en", 0, 4), w("ed", 15, 64, 16), CE, A.add)
-        if t == R:
-            return
-        ts(w("en", 4, 8), w("ed", 15, 64, 16), CE, A.add)
-        act(w("vm", 64, 128), n(), F.Sign, 1.0, THR)
-        act(w("vm"), w("vm", 64, 128), F.Identity, BIG / 2, -BIG / 2)
-        tt(w("vm", 64, 128), w("vm"), v("seln", 0, 64), A.min)
-        tt(w("cn"), w("cum"), v("seln", 0, 64), A.add)
-        act(w("inv", 1, 112, 2), w("rr", 0, H), F.Relu, -float(C + 1), float(C + 1))
-
-    def onward(t):
-        p = PILES[t]
-        w = lambda name, a=0, b=64, s=1: v(name + str(t), a, b, s)
-        x = lambda name, a=0, b=64, s=1: v(name + str(t + 1), a, b, s)
-        act(w("mm", 0, p), w("n", 0, p), F.Relu, 1.0, -2.0)
-        act(v("junk", 0, 64), w("n"), F.Sign, acc=w("mm", p, p + 1))
-        act(v("r1", 0, 64), w("rr"), F.Sign, acc=w("mm", p + 1, p + 2))
-        act(w("mq", 0, p + 2), w("mm", 0, p + 2), F.Identity, 2.0 ** 15)
-        tt(w("a1", 0, p), w("cum", 0, p), v("ck", 0, p), A.add)
-        tt(w("y", 0, p + 2), w("a1", 0, p + 2), w("mq", 0, p + 2), A.subtract)
-        scan(w("yv"), w("mm"), v("m16k", 0, 64), -B1K, A.max, A.add)
-        act(w("yt", 0, 4), w("yv", 15, 64, 16), F.Identity, 1.0, CE)
-        act(w("yt", 4, 8), w("yt", 0, 4), F.Identity, -2.0 ** 15, -OFF - 1)
-        for k in range(4):
-            act(v("junk", 64 * k + 64, 64 * k + 128), w("y"), F.Sign, -1.0, w("yt", 4 + k, 5 + k), acc=w("sg4", k, k + 1))
-        ts(w("rk", 0, 4), w("sg4", 0, 4), 0.5, A.mult, 32.0, A.add)
-        cp(ind(w("ys"), w("rk", 0, 4)), w("y"))
-        act(w("wu"), w("ys"), F.Identity, -2.0 ** -15, 1.5 * 2.0 ** 23)
-        act(x("n"), w("wu"), F.Identity, 1.0, -1.5 * 2.0 ** 23)
-        act(w("nq"), x("n"), F.Identity, 2.0 ** 15)
-        tt(w("rest", 0, H), w("ys", 0, H), w("nq", 0, H), A.add)
-        derive(t + 1)
-        tt(w("rest", 0, H), w("rest", 0, H), x("cum", 0, H), A.subtract)
-        act(w("wu", 0, H), w("rest", 0, H), F.Identity, U)
-        tt(v("v2", 0, H), w("wu", 0, H), v("cx", 0, H), A.add)
-        cp(ind(x("vr", 8, 456), x("en", 0, 4)), v("v2", 0, 64))
-        scan(v("hold", 0, C), x("vr", 8, 8 + C), x("vr", 8, 8 + C), 0.0, A.min, A.min)
-        scan(v("dg", 0, C), v("hold", 0, C), v("m16n", 0, C), -U * B4M, A.min, A.add)
-        tt(v("xs", 0, 24), v("dg", 15, C, 16), v("cp", 0, 24), A.add)
-        ts(v("xi", 0, 24), v("xs", 0, 24), 1.0 / U, A.mult)
-        ts(v("xk", 0, 24), v("xi", 0, 24), 9, A.logical_shift_right, 63, A.bitwise_and)
-        ts(w("kl", 0, 24), v("xk", 0, 24), 2.0, A.mult, 1.0, A.add)
-        ts(v("xb", 0, 24), v("xi", 0, 24), 511, A.bitwise_and)
-        cp(w("t3", 0, 72, 3), v("xb", 0, 24))
-        act(w("b1", 0, 24), w("t3", 0, 72, 3), F.Identity, B1K, B1K)
+        scan(w("ed"), e, v("m16", 0, 64), -B1K, A.max, A.add)
+        if t in (1, 2):
+            ts(w("en", 8, 12), w("ed", 15, 64, 16), CE, A.add)
+        for k in range(2 if t < R else 1):
+            ts(w("en", 4 * k, 4 * k + 4), w("ed", 15, 64, 16), CE, A.add, 447.0, A.min)
+        if t < R:
+            act(w("p"), w("nv"), F.Relu, -BIG, THR)
+            tt(w("p", 64, 128), w("p"), v("sel", 0, 64), A.max)
+            act(w("fa", 0, H), (e[0], e[1], e[1] + H, 1), F.Relu, -2.0, 2.0 * C - 1)
+            lin(w("fx", 1, 112, 2), w("fa", 0, H), -1.0, 2.0 * C)
 
     cp(v("zu", 0, 3), v("zi", 0, 3))
-    cp(v("n0", 0, 48), ind(v("io", 0, 456), v("zu", 0, 3)))
-    derive(0)
-    cp(ind(v("vr0", 8, 456), v("en0", 0, 4)), v("cx", 0, 64))
-    for t in range(R):
-        onward(t)
-    dma("y", lambda: T.oz[:, :], lambda: T.f[0:128:16, AT["n3"][1]:AT["n3"][1] + H], [v("n3", 0, H)], [], 2e3, last=True)
+    lin(v("r0", 0, P0), ind(v("tb", 0, 386), v("zu", 0, 3)))
+    lin(v("nv0", 0, P0), v("r0", 0, P0), None, 1.0)
+    scan(v("cum0", 1, 65), v("r0", 0, 64), v("born0", 0, 64), 0.0, A.add, A.add)
+    starts(0, v("cum0", 0, 64))
+    cp(ind(v("vr0", 8, 456), v("en0", 0, 4)), v("v23", 0, 64))
+
+    k2 = lambda a, b: v("k2", 66 + a, 66 + b)
+    lin(k2(0, P0), v("r0", 0, P0), 2.0, 2.0)
+    act(v("junk", 0, 100), k2(-52, P0), F.Sign, None, -3.0, acc=k2(P0 + 1, P0 + 2))
+    for k, (more, least) in enumerate([(58, 5.0), (58, 7.0), (66, 9.0), (66, 11.0)]):
+        act(v("junk", 128 * k + 128, 128 * k + 178 + more), k2(-more, P0 + 2), F.Sign, None, -least, acc=k2(P0 + 2 + k, P0 + 3 + k))
+    scan(v("id", 1, P0), v("r0", 0, P0 - 1), v("c513", 0, P0 - 1), 0.0, A.add, A.add)
+    lin(v("mq", 0, 64), k2(0, 64), 2.0 ** 14, OFF)
+    tt(v("y", 0, 64), v("id", 0, 64), v("mq", 0, 64), A.subtract)
+    scan(v("yv", 0, 64), v("y", 0, 64), v("lift", 0, 64), 0.0, A.min, A.mult)
+    for k in range(4):
+        act(v("junk", 128 * k + 128, 128 * k + 192), v("y", 0, 64), F.Sign, -1.0 / U, v("yv", 16 * k + 15, 16 * k + 16), acc=v("sg4", k, k + 1))
+    ts(v("rk", 0, 4), v("sg4", 0, 4), -0.5, A.mult, 31.5, A.add)
+    cp(ind(v("ys", 0, 64), v("rk", 0, 4)), v("y", 0, 64))
+    lin(v("wu", 0, 64), v("ys", 0, 64), -2.0 ** -15, MAGIC)
+    lin(v("nq", 0, 64), v("wu", 0, 64), 2.0 ** 15, -MAGIC * 2.0 ** 15)
+    tt(v("rest", 0, 64), v("nq", 0, 64), v("ys", 0, 64), A.add)
+    for t in (1, 2, 3):
+        w = lambda name, a=0, b=64, s=1: v(name + str(t), a, b, s)
+        step = 2.0 ** 15 if t == 1 else B1K
+        lin(w("nv"), v("wu", 0, 64), None, -MAGIC - 2 * t)
+        if t < R:
+            relu(w("g"), v("rest", 0, 64), None, OFF - NEW - 512 * (t - 1) + G0[1] - G0[0])
+            tt(w("nv"), w("nv"), w("g"), A.subtract)
+            relu(w("born"), w("g"), -1.0, 1.0)
+            lin(w("bc"), w("born"), None, -step)
+        relu(w("r"), w("nv"), None, -1.0)
+        scan(w("cum", 1, 65), w("r"), w("born") if t < R else v("born0", 0, 64), 0.0, A.add, A.add)
+        scan(w("d", 1, 65), w("r"), w("bc") if t < R else v("c1k", 0, 64), 0.0, A.add, A.add)
+        if t < R:
+            tt(w("e"), w("cum"), w("g"), A.max)
+        starts(t, w("e") if t < R else w("cum"))
+        tt(w("pay"), v("rest", 0, 64) if t == 1 else v("e%d" % (t - 1), 0, 64), w("d"), A.subtract)
+        lin(w("v2") if t < R else v("v20", 0, 64), w("pay"), U, U * (step + (OFF if t == 1 else 0.0)))
+        win = w("vr", 8, (1032, 520, 456)[t - 1])
+        cp(ind(win, w("en", 8, 12) if t < R else w("en", 0, 4)), w("v2") if t < R else v("v20", 0, 64))
+        scan(v("hold", 0, C), w("vr", 8, 8 + C), w("vr", 8, 8 + C), 0.0, A.min, A.min)
+        scan(v("dg", C * (t - 1), C * t), v("hold", 0, C), v("lift", 0, C), 0.0, A.min, A.mult)
+    for a, b, sh, one in ((0, 24, 8, 1.0), (24, 72, 9, -1.0)):
+        tt(v("xi", a, b), v("dg", 16 * a + 15, 16 * b, 16), v("cj", 0, b - a), A.add)
+        ts(v("xk", a, b), v("xi", a, b), sh, A.logical_shift_right, 126, A.bitwise_and)
+        ts(v("kl", a, b), v("xk", a, b), one, A.add)
+        ts(v("xb", a, b), v("xi", a, b), (2 << sh) - 1, A.bitwise_and)
+        cp(v("t3", 3 * a, 3 * b, 3), v("xb", a, b))
+        lin(v("b1", a, b), v("t3", 3 * a, 3 * b, 3), B1K, B1K)
+    relu(v("oz", 0, H), v("nv3", 0, H), None, 0.0)
+    dma("y", lambda: T.oz[:, :], lambda: T.f[0:128:16, AT["oz"][1]:AT["oz"][1] + H], [v("oz", 0, H)], [], 2e3, last=True)
 
     sent = [0]
 
@@ -338,90 +373,91 @@ def collect(g, T, topo, core, rank):
         rid, pid = topo.addr(peer)[:2]
         m = topo.mask(core, peer)
         k = len(topo.engines(core, peer))
+        c = CALL + (0.0 if sent[0] else FIRST)
         sent[0] += k
         pick = byt if codes else ap
-        return k, add("g", CALL, lambda: g.remote_dma(pick(dst), pick(src), T.sem[sem], T.sem.sent, pid, rid, m), [src], [],
+        return k, add([("g", c, lambda: g.remote_dma(pick(dst), pick(src), T.sem[sem], T.sem.sent, pid, rid, m))], [src], [],
                       late=FLY + nbytes / RATE)
 
     for t in range(R):
         pool, nxt, xq, lq = "pool%d" % t, "pool%d" % (t + 1), "x%d" % t, "l%d" % t
         w = lambda name, a=0, b=64, s=1: v(name + str(t), a, b, s)
-        ns = (PILES[t] + 7) // 8
+        ns = 7 if t else 6
         peer = T.cores[rank ^ STEP[t]]
         for k, (c0, c1) in enumerate(CH):
             quant(xq, c0, c1, v(pool, 4 * c0, 4 * c1))
             o = mm(k, "u2", 0, xq, c0, c1)
-            act(v("s", c0, c1), o, F.Identity, SGN)
+            lin(v("s", c0, c1), o, SGN)
             scan(v("m", c0, c1, -1), w("vr", 9 + c0, 9 + c1, -1), v("s", c0, c1, -1), v("m", c1, c1 + 1) if k else -BIG, A.add, A.max)
-            act(v("ms", c0, c1), v("m", c0, c1), F.Identity, SGN)
-            tt(v("eq", c0, c1), o, v("ms", c0, c1), A.not_equal)
-            scan(v("nd", c0, c1, -1), v("ones", c0, c1), v("eq", c0, c1, -1), v("nd", c1, c1 + 1), A.add, A.mult)
-        (a0, a1), (b0, b1) = CH[0], (0, CH[0][0])
-        k1, o1 = send(v("q" + xq, a0, a1), v("q" + lq, a0, a1), "qa%d" % t, peer, True, 512 * (a1 - a0))
-        k2, o2 = send(v("s" + xq), v("s" + lq), "qa%d" % t, peer, False, 512 * (a1 - a0) + 49152)
-        k3, o3 = send(v("q" + xq, b0, b1), v("q" + lq, b0, b1), "qb%d" % t, peer, True, 245760)
-        add("x", 0, None, [], [v("q" + lq, a0, a1), v("s" + lq)], after=[o1, o2], sem="qa%d" % t, cnt=k1 + k2)
-        add("x", 0, None, [], [v("q" + lq, b0, b1)], after=[o3], sem="qb%d" % t, cnt=k3)
-        for c0, c1 in ((a0, a1), (b0, b1)):
-            for b in range(4):
-                o = mm(3 + b, "e", 128 * b, lq, c0, c1)
-                act(v("dh", 4 * c0 + b, 4 * c1, 4), o, F.Identity, 0.5)
-        tt(v("rv", 0, 128), ind(v("m", 0, 448), w("en", 0, 8)), w("vm", 0, 128), A.add)
-        scan(v("vb8", 0, H), v("ra8", 0, H), v("rv", 64, 64 + H), 0.0, A.add, A.max)
+            lin(v("ms", c0, c1), v("m", c0, c1), SGN)
+            tt(v("eq", c0, c1), o, v("ms", c0, c1), A.is_equal)
+            scan(v("pos", c0, c1, -1), v("eq", c0, c1, -1), v("qr", c0, c1, -1), v("pos", c1, c1 + 1), A.add, A.min)
+        if EARLY[t]:
+            for k, (c0, c1) in enumerate(SEND):
+                sem, far = "q%s%d" % ("ab"[k], t), 640 * (C - c0) - 300 * k * (C - c1)
+                k1, o1 = send(v("q" + xq, c0, c1), v("q" + lq, c0, c1), sem, peer, True, far)
+                k2_, o2 = send(v("s" + xq, c0, c1), v("s" + lq, c0, c1), sem, peer, False, far)
+                add([("x", 0, None)], [], [v("q" + lq, c0, c1), v("s" + lq, c0, c1)], after=[o1, o2], sem=sem, cnt=k1 + k2_)
+                for b in range(4):
+                    lin(v("dh", 4 * c0 + b, 4 * c1, 4), mm(3 + b, "e", 128 * b, lq, c0, c1))
+        tt(v("rv", 0, 128), ind(v("m", 0, 448), w("en", 0, 8)), w("p", 0, 128), A.subtract)
+        scan(v("vb8", 0, H), v("down", 0, H), v("rv", 64, 64 + H), 0.0, A.add, A.max)
         for k in range(ns):
-            if k in VSG:
-                ts(v("sg", H * k, H * k + H), v("rv", 0, H), v("vb8", 8 * k + 7, 8 * k + 8), A.subtract, -1.0, A.mult)
-            else:
-                act(v("sg", H * k, H * k + H), v("rv", 0, H), F.Sign, -1.0, v("vb8", 8 * k + 7, 8 * k + 8))
-        tt(v("tp", 0, 64), ind(v("nd", 0, 448), w("en", 0, 4)), w("cn"), A.add)
-        scan(v("pd", 0, H), v("tp", 0, H), v("tp", 0, H), 0.0, A.max, A.max)
-        cp(v("pu", 0, ns), v("pd", 7, 8 * ns, 8))
-        tt(v("pr", 0, 16 * ns), ind(v("io", 0, 456), v("pu", 0, ns)), w("inv", 0, 16 * ns), A.max)
-        tt(v("ef", 0, 8 * ns), v("pr", 0, 16 * ns, 2), v("pr", 1, 16 * ns, 2), A.is_equal)
-        tt(v("pr", 1, 16 * ns, 2), v("pr", 1, 16 * ns, 2), v("ef", 0, 8 * ns), A.add)
+            o, a, b = v("sg", H * k, H * k + H), v("rv", 0, H), v("vb8", 8 * k + 7, 8 * k + 8)
+            add([sact(o, a, F.Sign, -1.0, b), vts(o, a, b, A.subtract, -1.0, A.mult)], [a, b], [o])
+        tt(v("tp", 0, 64), ind(v("pos", 0, 448), w("en", 0, 4)), w("p", 64, 128), A.add)
+        scan(v("pd", 0, H), v("up", 0, H), v("tp", 0, H), 0.0, A.add, A.min)
+        ts(v("pu", 0, ns), v("pd", 7, 8 * ns, 8), -512.0, A.mult, 193.0, A.add)
+        lin(v("p0", 0, 16 * ns), ind(v("tb", 0, 386), v("pu", 0, ns)))
+        scan(v("pr", 0, 16 * ns), w("fx", 0, 16 * ns), v("p0", 0, 16 * ns), 0.0, A.subtract, A.max)
         tt(v("cc", 0, H * ns), v("sg", 0, H * ns), v("lc", 0, H * ns), A.is_lt)
-        scan(v("rs", 0, H * ns), v("kr", 0, H * ns), v("cc", 0, H * ns), 0.0, A.mult, A.add)
+        scan(v("rs", 0, H * ns), v("kr", 0, H * ns), v("cc", 0, H * ns), 0.0, A.min, A.add)
         ts(v("ru", 0, ns), v("rs", H - 1, H * ns, H), H56, A.add)
         cp(ind(v("sr", 0, 112), v("ru", 0, ns)), v("pr", 0, 16 * ns))
         scan(v("sd", 0, 112), v("sr", 0, 112), v("m4", 0, 112), -B1K, A.max, A.add)
-        lst, lin = v("out%d" % t), v("lin%d" % t)
+        lst, lin_ = v("out%d" % t), v("lin%d" % t)
         ts(lst, v("sd", 3, 112, 4), 4.0, A.mult, C4, A.add)
-        k1, o1 = send(lst, lin, "la%d" % t, peer, False, 7168)
-        add("x", 0, None, [], [lin], after=[o1], sem="la%d" % t, cnt=k1)
-        act(v("ah"), ind(v(pool, 0, 4 * C + 8), lst), F.Identity, 0.5)
-        tt(v("mt", 0, 448), ind(v("dh"), lin), v("ah"), A.add)
+        for k in range(2):
+            lin(v("aa", 224 * k, 224 * k + 224), ind(v(pool, 0, 4 * C + 8), v(lst[0], 14 * k, 14 * k + 14)))
+        lin(v("ah"), v("aa", 0, 448), 0.5)
+        if EARLY[t]:
+            k1, o1 = send(lst, lin_, "la%d" % t, peer, False, 7168)
+            add([("x", 0, None)], [], [lin_], after=[o1], sem="la%d" % t, cnt=k1)
+            tt(v("mt", 0, 448), ind(v("dh"), lin_), v("ah"), A.add)
+        else:
+            quant("a%d" % t, 0, 128, v("aa"))
+            k1, o1 = send(v("sa%d" % t), v("s" + lq, 0, 128), "qa%d" % t, peer, False, 128 * 128)
+            k2_, o2 = send(v("qa%d" % t), v("q" + lq, 0, 128), "qa%d" % t, peer, True, 640 * 128)
+            add([("x", 0, None)], [], [v("q" + lq, 0, 128), v("s" + lq, 0, 128)], after=[o1, o2], sem="qa%d" % t, cnt=k1 + k2_)
+            for b in range(4):
+                o = mm(3 + b, "e", 128 * b, lq, 0, 128)
+                tt(v("mt", b, 448, 4), (o[0], o[1], o[1] + 112, 1), v("ah", b, 448, 4), A.add)
         quant("m", 0, 128, v("mt"))
         for b in range(4):
             o = mm((7, 0, 1, 2)[b], "w", 128 * b, "m", 0, 128)
-            act(v("rl", b, 448, 4), (o[0], o[1], o[1] + 112, 1), F.Relu, 0.03125)
-        tt(v(pool, 4 * G0, PW), ind(v(pool, 0, 4 * C + 8), lst), v("rl"), A.add)
+            relu(v("rl", 112 * b, 112 * b + 112), (o[0], o[1], o[1] + 112, 1), 0.03125)
+            tt(v(pool, 4 * G0[t] + b, None, 4), v("rl", 112 * b, 112 * b + 112), v("aa", b, 448, 4), A.add)
         tt(v("lh", 0, 112, 2), v("pr", 0, 112, 2), v("pr", 1, 112, 2), A.min)
         tt(v("lh", 1, 112, 2), v("pr", 0, 112, 2), v("pr", 1, 112, 2), A.max)
         scan(v("pk", 0, 112), v("kp", 0, 112), v("lh", 0, 112), 0.0, A.mult, A.add)
-        act(v("pkr", 0, C), ind(v("pk", 0, 112), w("kl", 0, 24)), F.Identity, U)
-        scan(v("pkd", 0, C), v("pkr", 0, C), v("m16n", 0, C), -U * B4M, A.min, A.add)
-        ts(v("ki2", 0, 24), v("pkd", 15, C, 16), 1.0 / U, A.mult, CB, A.add)
+        lin(v("pkr", 0, C), ind(v("pk", 0, 112), v("kl", 24 * t, 24 * t + 24)), U)
+        scan(v("pkd", 0, C), v("pkr", 0, C), v("lift", 0, C), 0.0, A.min, A.mult)
+        t3 = lambda k: v("t3", 72 * t + k, 72 * t + 72, 3)
+        ts(v("ki2", 0, 24), v("pkd", 15, C, 16), -1.0, A.add)
         ts(v("hi", 0, 24), v("ki2", 0, 24), 1023, A.bitwise_and)
-        tt(w("t3", 1, 72, 3), v("ki2", 0, 24), w("b1", 0, 24), A.is_lt)
-        tt(w("t3", 2, 72, 3), v("hi", 0, 24), w("t3", 0, 72, 3), A.is_le)
-        scan(v("t3o", 0, 72), v("k3", 0, 72), w("t3", 0, 72), 0.0, A.mult, A.add)
+        tt(t3(1), v("pkd", 15, C, 16), v("b1", 24 * t, 24 * t + 24), A.is_lt)
+        tt(t3(2), v("hi", 0, 24), t3(0), A.is_le)
+        scan(v("t3o", 0, 72), v("k3", 0, 72), v("t3", 72 * t, 72 * t + 72), 0.0, A.min, A.add)
         for b in range(4):
             ts(w("el", 24 * b, 24 * b + 24), v("t3o", 2, 72, 3), 4.0, A.mult, float(b), A.add)
         for k, (c0, c1) in enumerate(CH):
             for b in range(4):
-                o, s = v(nxt, 4 * c0 + b, 4 * c1, 4), ind(v(pool), w("el", 24 * b + c0 // 16, 24 * b + c1 // 16))
-                if b in VPL[t][k]:
-                    cp(o, s)
-                else:
-                    act(o, s, F.Identity)
+                lin(v(nxt, 4 * c0 + b, 4 * c1, 4), ind(v(pool), w("el", 24 * b + c0 // 16, 24 * b + c1 // 16)))
 
     for k, (c0, c1) in enumerate(CH):
         quant("x3", c0, c1, v("pool3", 4 * c0, 4 * c1))
         o = mm(k, "v", 0, "x3", c0, c1)
-        if k % 2:
-            cp(v("yb", c0, c1), o)
-        else:
-            act(v("yb", c0, c1), o, F.Identity)
+        lin(v("yb", c0, c1), o)
         dma("y", lambda c0=c0, c1=c1: T.oc[:, 4 * c0:4 * c1], lambda c0=c0, c1=c1: byt(v("qx3", c0, c1)), [v("qx3", c0, c1)], [], 98e3, last=True)
         dma("sy"[k % 2], lambda c0=c0, c1=c1: T.y[:, c0:c1], lambda c0=c0, c1=c1: T.yb[:, c0:c1], [v("yb", c0, c1)], [], 98e3, last=True)
     for k in range(4):
@@ -444,7 +480,7 @@ def order(ops):
             for d in ds:
                 name, c = cells(d)
                 for i, wi, ci in seen.get(name, []):
-                    if i != j and (wr or wi or (name == "ps" and ops[i]["q"] != o["q"])) and not c.isdisjoint(ci):
+                    if i != j and (wr or wi or name == "ps") and not c.isdisjoint(ci):
                         deps[j].add(i)
         for wr, ds in ((False, o["rd"]), (True, o["wr"])):
             for d in ds:
@@ -458,39 +494,63 @@ def order(ops):
             kids[i].append(j)
     tail = [0.0] * n
     for j in range(n - 1, -1, -1):
-        tail[j] = ops[j]["cost"] + ops[j]["late"] + max([WAKE + tail[k] for k in kids[j]] + [0.0])
+        tail[j] = ops[j]["ways"][0][1] + ops[j]["late"] + max([WAKE + tail[k] for k in kids[j]] + [0.0])
     rng = np.random.default_rng(7)
-    best, prio = None, np.array(tail)
+    prio, way = list(tail), [0] * n
+    now = best = lay(ops, deps, kids, prio, way)
+    keep = way
     for turn in range(TURNS):
-        p = prio + (rng.standard_normal(n) * 700.0 * (rng.random(n) < 0.04) if turn else 0.0)
-        seq, end = lay(ops, deps, kids, p)
-        if best is None or end <= best[1]:
-            best, prio = (seq, end), p
-    return deps, best[0], best[1]
+        p, y = list(prio), list(way)
+        for _ in range(1 + int(rng.integers(3))):
+            j = now[2][int(rng.integers(len(now[2])))] if rng.random() < 0.7 else int(rng.integers(n))
+            if len(ops[j]["ways"]) > 1 and rng.random() < 0.5:
+                y[j] = int(rng.integers(len(ops[j]["ways"])))
+            else:
+                p[j] += float(rng.standard_normal()) * 1000.0
+        new = lay(ops, deps, kids, p, y)
+        if new[1] <= now[1] + SLACK * (1 - turn / TURNS) * rng.random():
+            now, prio, way = new, p, y
+            if new[1] <= best[1]:
+                best, keep = new, y
+    return deps, best[0], best[1], keep
 
 
-def lay(ops, deps, kids, tail):
-    done, free, seq, can = {}, {}, [], {}
+def lay(ops, deps, kids, tail, way):
+    n = len(ops)
+    done, can, why, free, last, seq = [0.0] * n, [0.0] * n, [-1] * n, {}, {}, []
+    q = [o["ways"][y][0] for o, y in zip(ops, way)]
+    cost = [o["ways"][y][1] for o, y in zip(ops, way)]
     left = [len(d) for d in deps]
-    ready = [j for j in range(len(ops)) if not left[j]]
-    for j in ready:
-        can[j] = 0.0
-    while ready:
-        est = {j: max(free.get(ops[j]["q"], 0.0), can[j]) for j in ready}
-        c = min(ready, key=lambda j: (est[j], -tail[j]))
-        near = [j for j in ready if ops[j]["q"] == ops[c]["q"] and est[j] <= est[c] + NEAR * ops[c]["cost"]]
-        c = max(near, key=lambda j: tail[j])
-        ready.remove(c)
-        seq.append((c, est[c]))
-        if ops[c]["q"] != "x":
-            free[ops[c]["q"]] = est[c] + ops[c]["cost"]
-        done[c] = est[c] + ops[c]["cost"] + ops[c]["late"]
-        for k in kids[c]:
-            left[k] -= 1
-            if not left[k]:
-                ready.append(k)
-                can[k] = max(done[i] + WAKE for i in deps[k])
-    return seq, max(done.values())
+    ready = {k: [] for k in "vstygx"}
+    for k in ready:
+        free[k] = 0.0
+    for j in range(n):
+        if not left[j]:
+            ready[q[j]].append(j)
+    for _ in range(n):
+        at, k = min((max(free[k], min(can[j] for j in r)), k) for k, r in ready.items() if r)
+        r = ready[k]
+        c = max((j for j in r if can[j] <= at), key=lambda j: tail[j])
+        c = max((j for j in r if can[j] <= at + NEAR * cost[c]), key=lambda j: tail[j])
+        r.remove(c)
+        at = max(free[k], can[c])
+        if free[k] > can[c]:
+            why[c] = last[k]
+        seq.append((c, at))
+        if k != "x":
+            free[k], last[k] = at + cost[c], c
+        done[c] = at + cost[c] + ops[c]["late"]
+        for j in kids[c]:
+            left[j] -= 1
+            if done[c] + WAKE > can[j]:
+                can[j], why[j] = done[c] + WAKE, c
+            if not left[j]:
+                ready[q[j]].append(j)
+    end = max(done)
+    chain = [done.index(end)]
+    while why[chain[-1]] >= 0:
+        chain.append(why[chain[-1]])
+    return seq, end, chain
 
 
 def rank_program(g, core, T, topo):
@@ -500,12 +560,13 @@ def rank_program(g, core, T, topo):
     ops, sent = collect(g, T, topo, core, rank)
     if "order" not in KEPT:
         KEPT["order"] = order(ops)
-    deps, seq, _ = KEPT["order"]
-    seq = [j for j, _t in seq if ops[j]["q"] != "x"]
+    deps, seq, _, way = KEPT["order"]
+    q = [o["ways"][y][0] for o, y in zip(ops, way)]
+    seq = [j for j, _t in seq if q[j] != "x"]
     at = {j: k for k, j in enumerate(seq)}
     known, before, waits, need = {}, {}, {}, set()
     for j in seq:
-        kn = known.setdefault(ops[j]["q"], set())
+        kn = known.setdefault(q[j], set())
         waits[j] = []
         for i in sorted(deps[j], key=lambda i: -at.get(i, 10 ** 6)):
             if i not in kn:
@@ -518,7 +579,7 @@ def rank_program(g, core, T, topo):
     need |= set(last)
     sig, user, count, nd = {}, [None] * NSEM, [0] * NSEM, 0
     for j, o in enumerate(ops):
-        if o["q"] == "x":
+        if q[j] == "x":
             sig[j] = (o["sem"], o["cnt"])
     for j in seq:
         if j not in need:
@@ -535,8 +596,8 @@ def rank_program(g, core, T, topo):
     for j in seq:
         o = ops[j]
         for i in waits[j]:
-            eng[o["q"]].wait_ge(T.sem[sig[i][0]], sig[i][1])
-        ins = o["fn"]()
+            eng[q[j]].wait_ge(T.sem[sig[i][0]], sig[i][1])
+        ins = o["ways"][way[j]][2]()
         if j in need:
             ins.then_inc(T.sem[sig[j][0]], 16 if o.get("dma") else 1)
     for j in last:

@@ -3,18 +3,19 @@ from concourse.mybir import dt, AluOpType as A, ActivationFunctionType as F
 
 C, H, R, P0 = 384, 56, 3, 48
 STEP = [1, 2, 1]
+XO = 8 * H
 G0 = [388, 452, 452]
-CH = [(192, 384), (0, 192)]
-SEND = [(192, 384), (0, 192)]
+CH = [[(192, 384), (0, 192)]] * 4
+SEND = [[(192, 384), (0, 192)]] * 3
 BIG = 2.0 ** 80
 U = -2.0 ** 75
 B1K, LIFT = 1024.0, 2.0 ** 24
 MAGIC = 1.5 * 2.0 ** 23
 OFF = 13112.0
 NEW = 50 * 512
-EARLY = [True, True, True]
-CYC, SFIX, WAKE, NEAR, TURNS, SLACK = 1.04, 40.0, 120.0, 0.4, 12000, 150.0
+CYC, VFIX, SFIX, WAKE = 0.9, 20.0, 75.0, 140.0
 FLY, RATE, CALL, FIRST, LOAD = 1500.0, 80.0, 300.0, 1000.0, 1400.0
+TURNS, SLACK, SOON, SEED = 300000, 100.0, 0.08, 7
 
 ARENA = {"f": 0, "h": 0, "i": 0, "w": 0}
 AT = {}
@@ -27,25 +28,24 @@ def _take(ar, name, n):
     ARENA[ar] += (n + al - 1) // al * al
 
 
-for _n, _k in [("m", 448), ("s", 384), ("ms", 384), ("tb", 392), ("pc", 16), ("j16", 64), ("j8", 64), ("j4", 112),
-               ("m16", 64), ("l16", 32), ("lift", 384), ("m4", 112), ("sel", 64), ("down", 64), ("up", 64), ("kp", 112),
-               ("k3", 72), ("i16", 48), ("cj", 48), ("c513", 48), ("c1k", 64), ("k2", 136), ("junk", 640), ("id", 64), ("mq", 64),
-               ("y", 64), ("yv", 64), ("sg4", 8), ("ys", 64), ("wu", 64), ("nq", 64), ("rest", 64), ("oz", 64),
-               ("rv", 128), ("vb8", 64), ("tp", 64), ("pd", 64), ("p0", 112), ("pr", 112), ("sr", 112), ("sd", 112),
-               ("lh", 112), ("pk", 112), ("pkr", 384), ("pkd", 384), ("t3o", 72), ("hold", 384), ("dg", 1152),
-               ("t3", 216), ("b1", 72), ("vr0", 456), ("vr1", 1032), ("vr2", 520), ("vr3", 456)]:
+for _n, _k in [("m", 448), ("r0", 64), ("nv0", 64), ("cum0", 72), ("id", 64), ("vr0", 456), ("vr1", 1032), ("vr2", 520), ("vr3", 456),
+               ("s", 384), ("ms", 384), ("tb", 392), ("pc", 16), ("j16", 128), ("j8", 64), ("j4", 112), ("m16", 128), ("lift", 384),
+               ("m4", 112), ("sel", 64), ("down", 64), ("up", 64), ("kp", 112), ("k3", 72), ("i16", 72), ("cj", 72), ("c513", 48),
+               ("k2", 136), ("junk", 640), ("mq", 64), ("y", 64), ("yv", 64), ("sg4", 8), ("ys", 64), ("wu", 64), ("nq", 64),
+               ("rest", 256), ("oz", 64), ("mark", 64), ("ed0", 64), ("nv", 192), ("g", 128), ("born", 192), ("np", 200),
+               ("rlo", 128), ("rhi", 128), ("nc", 192), ("d", 192), ("ed", 192), ("p", 384), ("fa", 128), ("fx", 384),
+               ("pay", 192), ("v2", 192), ("rv", 128), ("vb8", 64), ("tp", 64), ("pd", 64), ("p0", 112), ("pr", 112), ("sr", 112),
+               ("sd", 112), ("lh", 112), ("pk", 112), ("pkr", 384), ("pkd", 384), ("t3o", 72), ("hold", 384), ("dg", 1152),
+               ("t3", 216), ("b1", 72), ("gs", 72), ("xl", 24)]:
     _take("f", _n, _k)
-for _t in range(4):
-    for _n, _k in [("cum", 72), ("d", 72), ("r", 64), ("nv", 64), ("g", 64), ("born", 64), ("bc", 64), ("e", 64), ("ed", 64),
-                   ("p", 128), ("fa", 64), ("fx", 112), ("pay", 64), ("v2", 64)]:
-        _take("f", _n + str(_t), _k)
-    _take("w", "en%d" % _t, 12)
+for _t in range(R):
+    _take("w", "en%d" % _t, 8)
     _take("w", "el%d" % _t, 96)
 for _n, _k in [("eq", 384), ("pos", 448), ("qr", 384), ("sg", 392), ("cc", 392), ("rs", 392), ("lc", 392), ("li", 392), ("kr", 392)]:
     _take("h", _n, _k)
 for _n, _k in [("pi", 8), ("pj", 8), ("ui", 8), ("xi", 72), ("xk", 72), ("xb", 72), ("ki2", 24), ("hi", 24)]:
     _take("i", _n, _k)
-for _n, _k in [("zu", 4), ("uo", 8), ("qo", 24), ("pu", 8), ("ru", 8), ("rk", 4), ("kl", 72)]:
+for _n, _k in [("zu", 4), ("uo", 8), ("es", 12), ("pu", 8), ("ru", 8), ("rk", 4), ("kl", 72)]:
     _take("w", _n, _k)
 
 X4, U8, BF, F32 = "float8_e4m3fn_x4", "uint8", "bfloat16", "float32"
@@ -53,18 +53,18 @@ SCRATCH = {"f": ("sbuf", [128, ARENA["f"]], F32), "h": ("sbuf", [128, ARENA["h"]
            "i": ("sbuf", [128, ARENA["i"]], "int32"), "w": ("sbuf", [128, ARENA["w"]], "uint16"),
            "zi": ("sbuf", [128, 4], "int32"), "ps": ("psum", [128, 4096], F32),
            "pool3": ("sbuf", [128, 4 * C], BF), "ub": ("sbuf", [128, 512], BF), "vb": ("sbuf", [128, 512], BF),
-           "ones": ("sbuf", [128, 528], BF), "eye": ("sbuf", [128, 528], BF), "mt": ("sbuf", [128, 512], BF),
-           "ah": ("sbuf", [128, 448], BF), "aa": ("sbuf", [128, 512], BF), "rl": ("sbuf", [128, 448], F32),
+           "half": ("sbuf", [128, 528], BF), "eye": ("sbuf", [128, 528], BF), "mt": ("sbuf", [128, 512], BF),
+           "ah": ("sbuf", [128, 448], BF), "aa": ("sbuf", [128, 448], BF), "rl": ("sbuf", [128, 448], F32),
            "dh": ("sbuf", [128, 4 * C + 8], F32), "yb": ("sbuf", [128, C], F32)}
 for _n, _k in [("u", 128), ("u2", 128), ("v", 128), ("w", 512), ("e", 512), ("m", 128), ("x0", C), ("x1", C), ("x2", C), ("x3", C),
-               ("l0", C), ("l1", C), ("l2", C), ("a0", 128), ("a1", 128), ("a2", 128)]:
+               ("l0", C), ("l1", C), ("l2", C)]:
     SCRATCH["q" + _n] = ("sbuf", [128, _k], X4)
     SCRATCH["s" + _n] = ("sbuf", [128, _k], U8)
 for _t in range(R):
-    SCRATCH["pool%d" % _t] = ("sbuf", [128, 4 * (G0[_t] + 2 * H)], BF)
+    SCRATCH["pool%d" % _t] = ("sbuf", [128, XO + 4 * (G0[_t] + 2 * H)], BF)
     SCRATCH["out%d" % _t] = ("sbuf", [128, 28], "uint16")
     SCRATCH["lin%d" % _t] = ("sbuf", [128, 28], "uint16")
-NSEM, NDMA = 110, 26
+NSEM, NDMA = 110, 28
 SEMAPHORES = (["c%d" % k for k in range(NSEM)] + ["d%d" % k for k in range(NDMA)] + ["sent"]
               + [n + str(t) for n in ("qa", "qb", "la") for t in range(R)])
 
@@ -119,7 +119,7 @@ def collect(g, T, topo, core, rank):
             return 50 + CYC * 1.56 * size(out)
         if all(two(d) for d in [out] + ins):
             k *= 0.5
-        return CYC * max(64.0, size(out) * k)
+        return VFIX + CYC * max(64.0, size(out) * k)
 
     def tt(out, a, b, op):
         c = cyc(out, [a, b], 1 if "ps" in (a[0], b[0]) else 2)
@@ -205,6 +205,9 @@ def collect(g, T, topo, core, rank):
         e = g.sync if q == "y" else g.scalar
         add([(q, 60, lambda: e.dma_start(out(), src()))], rd, wr, late=LOAD + nbytes / 200.0, dma=True, last=last)
 
+    def zero(out, src):
+        dma("y", lambda: ap(out), lambda: ap(src), [src], [out], 128 * 4 * size(out))
+
     def byt(d):
         return ap(d).bitcast(dt.uint8)
 
@@ -212,17 +215,17 @@ def collect(g, T, topo, core, rank):
 
     dma("y", lambda: T.zi[:, 0:3], lambda: T.z[:, :], [], [v("zi", 0, 3)], 2e3)
     dma("s", lambda: T.ub[:, :], lambda: T.u[:, :], [], [v("ub")], 131e3)
-    for k, (c0, c1) in enumerate(CH):
-        dma("ys"[k % 2], lambda c0=c0, c1=c1: T.pool0[:, 4 * c0:4 * c1], lambda c0=c0, c1=c1: T.x[:, 4 * c0:4 * c1], [],
-            [v("pool0", 4 * c0, 4 * c1)], 131e3 + 1024 * (C - c0))
-    dma("y", lambda: byt(v("qw")), lambda: T.wc[:, :], [v("pool0", 0, 4 * C)], [v("qw")], 262e3)
-    dma("y", lambda: T.sw[:, :], lambda: T.ws[:, :], [v("pool0", 0, 4 * C)], [v("sw")], 330e3)
-    dma("y", lambda: T.vb[:, :], lambda: T.v[:, :], [v("pool0", 0, 4 * C)], [v("vb")], 460e3)
+    for k, (c0, c1) in enumerate(CH[0]):
+        dma("ys"[k % 2], lambda c0=c0, c1=c1: T.pool0[:, XO + 4 * c0:XO + 4 * c1], lambda c0=c0, c1=c1: T.x[:, 4 * c0:4 * c1], [],
+            [v("pool0", XO + 4 * c0, XO + 4 * c1)], 131e3 + 1024 * (C - c0))
+    dma("y", lambda: byt(v("qw")), lambda: T.wc[:, :], [v("pool0", XO, XO + 4 * C)], [v("qw")], 262e3)
+    dma("y", lambda: T.sw[:, :], lambda: T.ws[:, :], [v("pool0", XO, XO + 4 * C)], [v("sw")], 330e3)
+    dma("y", lambda: T.vb[:, :], lambda: T.v[:, :], [v("pool0", XO, XO + 4 * C)], [v("vb")], 460e3)
 
     iota(v("pi", 0, 1), [[0, 1]], 0, 1)
     iota(v("tb", 1, 386), [[1, 385]], 0)
     fill(v("tb", 0, 1), C)
-    iota(v("j16", 0, 64), [[0, 4], [1, 16]], 0)
+    iota(v("j16", 0, 128), [[0, 8], [1, 16]], 0)
     iota(v("j8", 0, 64), [[0, 8], [1, 8]], 0)
     iota(v("ui", 0, 8), [[16, 8]], 0)
     for k, (sh, msk) in enumerate([(0, 15), (0, 1), (1, 7), (0, 3), (2, 3)]):
@@ -234,55 +237,51 @@ def collect(g, T, topo, core, rank):
     lin(TMP, S4, 2 * B1K, -B1K)
     ts(C4, TMP, 2.0, A.mult, T4, A.add)
     lin(C4, C4, None, 18 * B1K)
-    add([("v", cyc(v("ones"), []), lambda: g.vector.memset(T.ones[:, :], 0.5))], [], [v("ones")])
-    fill(v("aa", 448, 512), 0)
-    fill(v("m", C, 448), 0)
+    lin(CE, Q16, 2 * B1K, 32 * B1K)
+    add([("v", cyc(v("half"), []), lambda: g.vector.memset(T.half[:, :], 0.5))], [], [v("half")])
+    fill(("f", AT["m"][1] + C, AT["vr0"][1] + 400, 1), 0)
+    for t in (1, 2, 3):
+        zero(v("vr%d" % t, 8, 400), v("vr0", 8, 400))
+    zero(v("fx", 0, 384), v("vr0", 8, 392))
+    fill(v("dh", 4 * C, 4 * C + 8), 0)
+    for t in range(R):
+        fill(v("pool%d" % t, XO + 4 * C, XO + 4 * C + 16), 0)
+    fill(v("mt", 448, 512), 0)
     fill(v("pos", C, 448), 0)
-    for name in ("cum", "d"):
-        for t in range(4):
-            fill(v(name + str(t), 0, 1), 0)
-    fill(v("id", 0, 1), 0)
-    fill(v("r0", P0, 64), 0)
-    fill(v("nv0", P0, 64), 0)
     fill(v("k2", 0, 66), 1000)
     fill(v("k2", 66 + P0, 67 + P0), 2 * (P0 + 2))
     fill(v("k2", 66 + P0 + 6, 130), 0)
     fill(v("c513", 0, 48), 513)
-    fill(v("born0", 0, 64), 1)
-    fill(v("c1k", 0, 64), 1 - 1024)
-    fill(v("sr", P0, 112), C)
-    fill(v("pr", 2 * P0, 112), C)
-    fill(v("mt", 448, 512), 0)
-    fill(v("dh", 4 * C, 4 * C + 8), 0)
-    for t in range(R):
-        fill(v("pool%d" % t, 4 * C, 4 * G0[t]), 0)
-        fill(v("fx%d" % t, 0, 112, 2), 0)
-    for t in range(4):
-        fill(v("vr%d" % t, 8, 400), 0)
-    fill(v("pay3", 0, 64), -1)
-    lin(v("v23", 0, 64), v("pay3", 0, 64), -U)
+    fill(v("born", 128, 192), 1)
+    fill(v("np", 7, 8), 1)
+    fill(v("rlo", 0, 128), 1023)
+    fill(v("rlo", 0, 128, 64), -1)
+    lin(v("rhi", 0, 128), v("rlo", 0, 128), -8192.0, -8193.0)
+    fill(v("pr", 2 * P0, 112 + 112), C)
+    lin(v("mark", 0, 64), v("born", 128, 192), U)
     iota(v("id", P0, P0 + 6), [[512, 3], [H, 2]], NEW - 512 + G0[0] - 2)
     iota(v("id", P0 + 6, 64), [[1, 10]], 0)
     ts(v("sel", 0, 64), v("j8", 0, 64), QQ, A.not_equal, BIG * 2.0 ** 13, A.mult)
     ts(v("down", 0, 64), v("j8", 0, 64), 0.0, A.is_equal, -BIG * 2.0 ** 15, A.mult)
     lin(v("up", 0, 64), v("down", 0, 64), -1.0)
-    ts(v("m16", 0, 64), v("j16", 0, 64), Q16, A.subtract, 4 * B1K, A.mult)
-    ts(v("m16", 0, 64), v("m16", 0, 64), 2 * B1K, A.add, 2 * B1K, A.min)
-    lin(CE, Q16, 2 * B1K, 32 * B1K)
-    ts(v("l16", 0, 16), v("j16", 0, 16), Q16, A.is_equal, LIFT, A.mult)
-    ts(v("l16", 16, 32), v("j16", 0, 16), Q16, A.is_gt)
-    tt(v("l16", 0, 16), v("l16", 0, 16), v("l16", 16, 32), A.add)
-    lin(v("l16", 15, 16), v("l16", 15, 16), 1.0 / (U * LIFT))
-    lin(v("m16", 15, 64, 16), v("m16", 15, 64, 16), None, -64 * B1K)
-    iota(v("i16", 0, 48), [[0, 2], [16, 24]], 0)
-    ts(v("qo", 0, 24), v("i16", 0, 24), 0.0, A.mult, Q16, A.add)
-    lin(v("lift", 0, C), ind(v("l16", 0, 16), v("qo", 0, 24)))
-    lin(v("cj", 0, 48), v("i16", 0, 48), None, Q16)
+    ts(v("m16", 0, 128), v("j16", 0, 128), Q16, A.subtract, 4 * B1K, A.mult)
+    ts(v("m16", 0, 128), v("m16", 0, 128), 2 * B1K, A.add, 2 * B1K, A.min)
+    lin(v("m16", 15, 128, 16), v("m16", 15, 128, 16), None, -64 * B1K)
+    ts(v("lift", 0, 64), v("j16", 0, 64), Q16, A.is_equal, LIFT, A.mult)
+    ts(v("lift", 64, 128), v("j16", 0, 64), Q16, A.is_gt)
+    tt(v("lift", 0, 64), v("lift", 0, 64), v("lift", 64, 128), A.add)
+    lin(v("lift", 15, 64, 16), v("lift", 15, 64, 16), 1.0 / (U * LIFT))
+    for a, b in ((64, 128), (128, 256), (256, 384)):
+        lin(v("lift", a, b), v("lift", 0, b - a))
+    iota(v("i16", 0, 24), [[16, 24]], int(OFF))
+    iota(v("i16", 24, 72), [[0, 2], [16, 24]], 0)
+    lin(v("cj", 0, 72), v("i16", 0, 72), None, Q16)
     lin(v("qr", 0, C), v("tb", 1, C + 1), -1.0 / 512, 0.375)
-    add([("g", 170 + 2 * CYC * 516, lambda: g.affine_select(T.eye[:, 0:516], T.ones[:, 0:516], [[1, 516]], A.is_equal, 0.0, -3, -4))],
-        [v("ones", 0, 516)], [v("eye", 0, 516)])
+    add([("g", 170 + 2 * CYC * 516, lambda: g.affine_select(T.eye[:, 0:516], T.half[:, 0:516], [[1, 516]], A.is_equal, 0.0, -3, -4))],
+        [v("half", 0, 516)], [v("eye", 0, 516)])
     iota(v("li", 0, 392), [[-8, 7], [1, H]], 0)
-    iota(v("kr", 0, 392), [[0, 7], [64, H]], 0)
+    fill(v("kr", 0, 392), 64)
+    fill(v("kr", 0, 392, H), 0)
     iota(v("j4", 0, 112), [[0, 28], [2048, 4]], 0)
     iota(v("kp", 0, 112), [[0, H], [1024, 2]], 0)
     iota(v("k3", 0, 72), [[0, 24], [1024, 3]], 0)
@@ -294,31 +293,29 @@ def collect(g, T, topo, core, rank):
 
     quant("u", 0, 128, v("ub"))
     cp(v("uo", 0, 8), v("ui", 0, 8))
-    add([("v", 260, lambda: g.vector.tensor_copy(T.qu2[:, 0:128].bitcast(dt.uint32), T.qu[:, 0:128].bitcast(dt.uint32).indirect(ap(v("uo", 0, 8)))))],
+    add([("v", 50 + 200 * CYC, lambda: g.vector.tensor_copy(T.qu2[:, 0:128].bitcast(dt.uint32), T.qu[:, 0:128].bitcast(dt.uint32).indirect(ap(v("uo", 0, 8)))))],
         [v("qu"), v("uo", 0, 8)], [v("qu2")])
-    add([("s", 280, lambda: g.scalar.activation(T.su2[:, 0:128], T.su[:, 0:128].indirect(ap(v("uo", 0, 8))), F.Copy))],
+    add([("s", 65 + 200 * CYC, lambda: g.scalar.activation(T.su2[:, 0:128], T.su[:, 0:128].indirect(ap(v("uo", 0, 8))), F.Copy))],
         [v("su"), v("uo", 0, 8)], [v("su2")])
     quant("v", 0, 128, v("vb"))
 
-    def starts(t, e):
-        w = lambda name, a=0, b=64, s=1: v(name + str(t), a, b, s)
-        scan(w("ed"), e, v("m16", 0, 64), -B1K, A.max, A.add)
-        if t in (1, 2):
-            ts(w("en", 8, 12), w("ed", 15, 64, 16), CE, A.add)
-        for k in range(2 if t < R else 1):
-            ts(w("en", 4 * k, 4 * k + 4), w("ed", 15, 64, 16), CE, A.add, 447.0, A.min)
-        if t < R:
-            act(w("p"), w("nv"), F.Relu, -BIG, THR)
-            tt(w("p", 64, 128), w("p"), v("sel", 0, 64), A.max)
-            act(w("fa", 0, H), (e[0], e[1], e[1] + H, 1), F.Relu, -2.0, 2.0 * C - 1)
-            lin(w("fx", 1, 112, 2), w("fa", 0, H), -1.0, 2.0 * C)
+    PLAIN, OWN = [0, 128, 256], [64, 192, 320]
+
+    def marks(t, e, nv):
+        act(v("p", PLAIN[t], PLAIN[t] + 64), nv, F.Relu, -BIG, THR)
+        act(v("fa", 0, 64), e, F.Relu, -2.0, 2.0 * C - 1)
+        lin(v("fx", 128 * t + 1, 128 * t + 128, 2), v("fa", 0, 64), -1.0, 2.0 * C)
+        tt(v("p", OWN[t], OWN[t] + 64), v("p", PLAIN[t], PLAIN[t] + 64), v("sel", 0, 64), A.max)
 
     cp(v("zu", 0, 3), v("zi", 0, 3))
     lin(v("r0", 0, P0), ind(v("tb", 0, 386), v("zu", 0, 3)))
     lin(v("nv0", 0, P0), v("r0", 0, P0), None, 1.0)
-    scan(v("cum0", 1, 65), v("r0", 0, 64), v("born0", 0, 64), 0.0, A.add, A.add)
-    starts(0, v("cum0", 0, 64))
-    cp(ind(v("vr0", 8, 456), v("en0", 0, 4)), v("v23", 0, 64))
+    scan(v("cum0", 1, 65), v("r0", 0, 64), v("born", 128, 192), 0.0, A.add, A.add)
+    scan(v("ed0", 0, 64), v("cum0", 0, 64), v("m16", 0, 64), -B1K, A.max, A.add)
+    for k in range(2):
+        ts(v("en0", 4 * k, 4 * k + 4), v("ed0", 15, 64, 16), CE, A.add)
+    marks(0, v("cum0", 0, 64), v("nv0", 0, 64))
+    cp(ind(v("vr0", 8, 456), v("en0", 0, 4)), v("mark", 0, 64))
 
     k2 = lambda a, b: v("k2", 66 + a, 66 + b)
     lin(k2(0, P0), v("r0", 0, P0), 2.0, 2.0)
@@ -337,34 +334,38 @@ def collect(g, T, topo, core, rank):
     lin(v("nq", 0, 64), v("wu", 0, 64), 2.0 ** 15, -MAGIC * 2.0 ** 15)
     tt(v("rest", 0, 64), v("nq", 0, 64), v("ys", 0, 64), A.add)
     for t in (1, 2, 3):
-        w = lambda name, a=0, b=64, s=1: v(name + str(t), a, b, s)
-        step = 2.0 ** 15 if t == 1 else B1K
-        lin(w("nv"), v("wu", 0, 64), None, -MAGIC - 2 * t)
-        if t < R:
-            relu(w("g"), v("rest", 0, 64), None, OFF - NEW - 512 * (t - 1) + G0[1] - G0[0])
-            tt(w("nv"), w("nv"), w("g"), A.subtract)
-            relu(w("born"), w("g"), -1.0, 1.0)
-            lin(w("bc"), w("born"), None, -step)
-        relu(w("r"), w("nv"), None, -1.0)
-        scan(w("cum", 1, 65), w("r"), w("born") if t < R else v("born0", 0, 64), 0.0, A.add, A.add)
-        scan(w("d", 1, 65), w("r"), w("bc") if t < R else v("c1k", 0, 64), 0.0, A.add, A.add)
-        if t < R:
-            tt(w("e"), w("cum"), w("g"), A.max)
-        starts(t, w("e") if t < R else w("cum"))
-        tt(w("pay"), v("rest", 0, 64) if t == 1 else v("e%d" % (t - 1), 0, 64), w("d"), A.subtract)
-        lin(w("v2") if t < R else v("v20", 0, 64), w("pay"), U, U * (step + (OFF if t == 1 else 0.0)))
-        win = w("vr", 8, (1032, 520, 456)[t - 1])
-        cp(ind(win, w("en", 8, 12) if t < R else w("en", 0, 4)), w("v2") if t < R else v("v20", 0, 64))
-        scan(v("hold", 0, C), w("vr", 8, 8 + C), w("vr", 8, 8 + C), 0.0, A.min, A.min)
+        lin(v("nv", 64 * t - 64, 64 * t), v("wu", 0, 64), None, -MAGIC - 2 * t)
+    for t in (1, 2):
+        relu(v("g", 64 * t - 64, 64 * t), v("rest", 0, 64), None, OFF - NEW - 512 * (t - 1) + G0[1] - G0[0])
+    for t, a, b in ((1, 0, 64), (2, 64, 192)):
+        n = b - a
+        tt(v("nv", a, a + 64), v("nv", a, a + 64), v("g", a, a + 64), A.subtract)
+        relu(v("born", a, a + 64), v("g", a, a + 64), -1.0, 1.0)
+        tt(v("np", 8 + a, 8 + b), v("nv", a, b), v("born", a, b), A.max)
+        scan(v("rest", 64 + a, 64 + b), v("rlo", 0, n), v("np", 7 + a, 7 + b), 0.0, A.min, A.add)
+        lin(v("nc", a, b), v("np", 7 + a, 7 + b), None, -2.0 ** 15)
+        scan(v("d", a, b), v("rhi", 0, n), v("nc", a, b), -2.0 ** 22, A.max, A.add)
+        tt(v("rest", 64 + a, 128 + a), v("rest", 64 + a, 128 + a), v("g", a, a + 64), A.max)
+        scan(v("ed", a, b), v("rest", 64 + a, 64 + b), v("m16", 0, n), -B1K, A.max, A.add)
+        ts(v("es", a // 16, b // 16), v("ed", a + 15, b, 16), CE, A.add)
+        for k in range(2):
+            ts(v("en%d" % t, 4 * k, 4 * k + 4), v("ed", a + 15, a + 64, 16), CE, A.add, 447.0, A.min)
+        marks(t, v("rest", 64 + a, 128 + a), v("nv", a, a + 64))
+        tt(v("pay", a, b), v("rest", a, b), v("d", a, b), A.subtract)
+        lin(v("v2", a, b), v("pay", a, b), U)
+    for t in (1, 2, 3):
+        cp(ind(v("vr%d" % t, 8, (1032, 520, 456)[t - 1]), v("es", 4 * t - 4, 4 * t)), v("v2", 64 * t - 64, 64 * t))
+        scan(v("hold", 0, C), v("vr%d" % t, 8, 8 + C), v("vr%d" % t, 8, 8 + C), 0.0, A.min, A.min)
         scan(v("dg", C * (t - 1), C * t), v("hold", 0, C), v("lift", 0, C), 0.0, A.min, A.mult)
-    for a, b, sh, one in ((0, 24, 8, 1.0), (24, 72, 9, -1.0)):
-        tt(v("xi", a, b), v("dg", 16 * a + 15, 16 * b, 16), v("cj", 0, b - a), A.add)
+    for a, b, sh, msk, one in ((0, 24, 8, 511, 1.0), (24, 72, 14, 1023, -1.0)):
+        tt(v("xi", a, b), v("dg", 16 * a + 15, 16 * b, 16), v("cj", a, b), A.add)
         ts(v("xk", a, b), v("xi", a, b), sh, A.logical_shift_right, 126, A.bitwise_and)
         ts(v("kl", a, b), v("xk", a, b), one, A.add)
-        ts(v("xb", a, b), v("xi", a, b), (2 << sh) - 1, A.bitwise_and)
+        ts(v("xb", a, b), v("xi", a, b), msk, A.bitwise_and)
         cp(v("t3", 3 * a, 3 * b, 3), v("xb", a, b))
         lin(v("b1", a, b), v("t3", 3 * a, 3 * b, 3), B1K, B1K)
-    relu(v("oz", 0, H), v("nv3", 0, H), None, 0.0)
+        ts(v("gs", a, b), v("xb", a, b), float(C), A.is_ge, -float(G0[a // 24] + 2 * H), A.mult)
+    relu(v("oz", 0, H), v("nv", 128, 128 + H), None, 0.0)
     dma("y", lambda: T.oz[:, :], lambda: T.f[0:128:16, AT["oz"][1]:AT["oz"][1] + H], [v("oz", 0, H)], [], 2e3, last=True)
 
     sent = [0]
@@ -384,32 +385,31 @@ def collect(g, T, topo, core, rank):
         w = lambda name, a=0, b=64, s=1: v(name + str(t), a, b, s)
         ns = 7 if t else 6
         peer = T.cores[rank ^ STEP[t]]
-        for k, (c0, c1) in enumerate(CH):
-            quant(xq, c0, c1, v(pool, 4 * c0, 4 * c1))
+        for k, (c0, c1) in enumerate(CH[t]):
+            quant(xq, c0, c1, v(pool, XO + 4 * c0, XO + 4 * c1))
             o = mm(k, "u2", 0, xq, c0, c1)
             lin(v("s", c0, c1), o, SGN)
             scan(v("m", c0, c1, -1), w("vr", 9 + c0, 9 + c1, -1), v("s", c0, c1, -1), v("m", c1, c1 + 1) if k else -BIG, A.add, A.max)
             lin(v("ms", c0, c1), v("m", c0, c1), SGN)
             tt(v("eq", c0, c1), o, v("ms", c0, c1), A.is_equal)
             scan(v("pos", c0, c1, -1), v("eq", c0, c1, -1), v("qr", c0, c1, -1), v("pos", c1, c1 + 1), A.add, A.min)
-        if EARLY[t]:
-            for k, (c0, c1) in enumerate(SEND):
-                sem, far = "q%s%d" % ("ab"[k], t), 640 * (C - c0) - 300 * k * (C - c1)
-                k1, o1 = send(v("q" + xq, c0, c1), v("q" + lq, c0, c1), sem, peer, True, far)
-                k2_, o2 = send(v("s" + xq, c0, c1), v("s" + lq, c0, c1), sem, peer, False, far)
-                add([("x", 0, None)], [], [v("q" + lq, c0, c1), v("s" + lq, c0, c1)], after=[o1, o2], sem=sem, cnt=k1 + k2_)
-                for b in range(4):
-                    lin(v("dh", 4 * c0 + b, 4 * c1, 4), mm(3 + b, "e", 128 * b, lq, c0, c1))
-        tt(v("rv", 0, 128), ind(v("m", 0, 448), w("en", 0, 8)), w("p", 0, 128), A.subtract)
+        for k, (c0, c1) in enumerate(SEND[t]):
+            sem, far = "q%s%d" % ("ab"[k], t), 640 * (C - c0) - 300 * k * (C - c1)
+            k1, o1 = send(v("q" + xq, c0, c1), v("q" + lq, c0, c1), sem, peer, True, far)
+            k3, o2 = send(v("s" + xq, c0, c1), v("s" + lq, c0, c1), sem, peer, False, far)
+            add([("x", 0, None)], [], [v("q" + lq, c0, c1), v("s" + lq, c0, c1)], after=[o1, o2], sem=sem, cnt=k1 + k3)
+            for b in range(4):
+                lin(v("dh", 4 * c0 + b, 4 * c1, 4), mm(3 + b, "e", 128 * b, lq, c0, c1))
+        tt(v("rv", 0, 128), ind(v("m", 0, 448), w("en", 0, 8)), v("p", PLAIN[t], PLAIN[t] + 128), A.subtract)
         scan(v("vb8", 0, H), v("down", 0, H), v("rv", 64, 64 + H), 0.0, A.add, A.max)
         for k in range(ns):
             o, a, b = v("sg", H * k, H * k + H), v("rv", 0, H), v("vb8", 8 * k + 7, 8 * k + 8)
             add([sact(o, a, F.Sign, -1.0, b), vts(o, a, b, A.subtract, -1.0, A.mult)], [a, b], [o])
-        tt(v("tp", 0, 64), ind(v("pos", 0, 448), w("en", 0, 4)), w("p", 64, 128), A.add)
+        tt(v("tp", 0, 64), ind(v("pos", 0, 448), w("en", 0, 4)), v("p", OWN[t], OWN[t] + 64), A.add)
         scan(v("pd", 0, H), v("up", 0, H), v("tp", 0, H), 0.0, A.add, A.min)
         ts(v("pu", 0, ns), v("pd", 7, 8 * ns, 8), -512.0, A.mult, 193.0, A.add)
         lin(v("p0", 0, 16 * ns), ind(v("tb", 0, 386), v("pu", 0, ns)))
-        scan(v("pr", 0, 16 * ns), w("fx", 0, 16 * ns), v("p0", 0, 16 * ns), 0.0, A.subtract, A.max)
+        scan(v("pr", 0, 16 * ns), v("fx", 128 * t, 128 * t + 16 * ns), v("p0", 0, 16 * ns), 0.0, A.subtract, A.max)
         tt(v("cc", 0, H * ns), v("sg", 0, H * ns), v("lc", 0, H * ns), A.is_lt)
         scan(v("rs", 0, H * ns), v("kr", 0, H * ns), v("cc", 0, H * ns), 0.0, A.min, A.add)
         ts(v("ru", 0, ns), v("rs", H - 1, H * ns, H), H56, A.add)
@@ -417,26 +417,17 @@ def collect(g, T, topo, core, rank):
         scan(v("sd", 0, 112), v("sr", 0, 112), v("m4", 0, 112), -B1K, A.max, A.add)
         lst, lin_ = v("out%d" % t), v("lin%d" % t)
         ts(lst, v("sd", 3, 112, 4), 4.0, A.mult, C4, A.add)
+        k1, o1 = send(lst, lin_, "la%d" % t, peer, False, 7168)
+        add([("x", 0, None)], [], [lin_], after=[o1], sem="la%d" % t, cnt=k1)
         for k in range(2):
-            lin(v("aa", 224 * k, 224 * k + 224), ind(v(pool, 0, 4 * C + 8), v(lst[0], 14 * k, 14 * k + 14)))
-        lin(v("ah"), v("aa", 0, 448), 0.5)
-        if EARLY[t]:
-            k1, o1 = send(lst, lin_, "la%d" % t, peer, False, 7168)
-            add([("x", 0, None)], [], [lin_], after=[o1], sem="la%d" % t, cnt=k1)
-            tt(v("mt", 0, 448), ind(v("dh"), lin_), v("ah"), A.add)
-        else:
-            quant("a%d" % t, 0, 128, v("aa"))
-            k1, o1 = send(v("sa%d" % t), v("s" + lq, 0, 128), "qa%d" % t, peer, False, 128 * 128)
-            k2_, o2 = send(v("qa%d" % t), v("q" + lq, 0, 128), "qa%d" % t, peer, True, 640 * 128)
-            add([("x", 0, None)], [], [v("q" + lq, 0, 128), v("s" + lq, 0, 128)], after=[o1, o2], sem="qa%d" % t, cnt=k1 + k2_)
-            for b in range(4):
-                o = mm(3 + b, "e", 128 * b, lq, 0, 128)
-                tt(v("mt", b, 448, 4), (o[0], o[1], o[1] + 112, 1), v("ah", b, 448, 4), A.add)
+            lin(v("aa", 224 * k, 224 * k + 224), ind(v(pool, XO, XO + 4 * C + 8), v(lst[0], 14 * k, 14 * k + 14)))
+        lin(v("ah"), v("aa"), 0.5)
+        tt(v("mt", 0, 448), ind(v("dh"), lin_), v("ah"), A.add)
         quant("m", 0, 128, v("mt"))
         for b in range(4):
             o = mm((7, 0, 1, 2)[b], "w", 128 * b, "m", 0, 128)
-            relu(v("rl", 112 * b, 112 * b + 112), (o[0], o[1], o[1] + 112, 1), 0.03125)
-            tt(v(pool, 4 * G0[t] + b, None, 4), v("rl", 112 * b, 112 * b + 112), v("aa", b, 448, 4), A.add)
+            relu(v("rl", b, 448, 4), (o[0], o[1], o[1] + 112, 1), 0.03125)
+            tt(v(pool, b, XO, 4) if b < 2 else v(pool, XO + 4 * G0[t] + b, None, 4), v("rl", b, 448, 4), v("aa", b, 448, 4), A.add)
         tt(v("lh", 0, 112, 2), v("pr", 0, 112, 2), v("pr", 1, 112, 2), A.min)
         tt(v("lh", 1, 112, 2), v("pr", 0, 112, 2), v("pr", 1, 112, 2), A.max)
         scan(v("pk", 0, 112), v("kp", 0, 112), v("lh", 0, 112), 0.0, A.mult, A.add)
@@ -448,13 +439,15 @@ def collect(g, T, topo, core, rank):
         tt(t3(1), v("pkd", 15, C, 16), v("b1", 24 * t, 24 * t + 24), A.is_lt)
         tt(t3(2), v("hi", 0, 24), t3(0), A.is_le)
         scan(v("t3o", 0, 72), v("k3", 0, 72), v("t3", 72 * t, 72 * t + 72), 0.0, A.min, A.add)
+        tt(v("xl", 0, 24), v("t3o", 2, 72, 3), v("gs", 24 * t, 24 * t + 24), A.add)
         for b in range(4):
-            ts(w("el", 24 * b, 24 * b + 24), v("t3o", 2, 72, 3), 4.0, A.mult, float(b), A.add)
-        for k, (c0, c1) in enumerate(CH):
+            ts(w("el", 24 * b, 24 * b + 24), v("xl", 0, 24) if b < 2 else v("t3o", 2, 72, 3), 4.0, A.mult, float(b + (XO if b < 2 else 0)), A.add)
+        for k, (c0, c1) in enumerate(CH[t + 1]):
             for b in range(4):
-                lin(v(nxt, 4 * c0 + b, 4 * c1, 4), ind(v(pool), w("el", 24 * b + c0 // 16, 24 * b + c1 // 16)))
+                at, win = XO if t + 1 < R else 0, v(pool, 0, XO + 4 * C) if b < 2 else v(pool, XO)
+                lin(v(nxt, at + 4 * c0 + b, at + 4 * c1, 4), ind(win, w("el", 24 * b + c0 // 16, 24 * b + c1 // 16)))
 
-    for k, (c0, c1) in enumerate(CH):
+    for k, (c0, c1) in enumerate(CH[R]):
         quant("x3", c0, c1, v("pool3", 4 * c0, 4 * c1))
         o = mm(k, "v", 0, "x3", c0, c1)
         lin(v("yb", c0, c1), o)
@@ -495,62 +488,97 @@ def order(ops):
     tail = [0.0] * n
     for j in range(n - 1, -1, -1):
         tail[j] = ops[j]["ways"][0][1] + ops[j]["late"] + max([WAKE + tail[k] for k in kids[j]] + [0.0])
-    rng = np.random.default_rng(7)
-    prio, way = list(tail), [0] * n
-    now = best = lay(ops, deps, kids, prio, way)
-    keep = way
-    for turn in range(TURNS):
-        p, y = list(prio), list(way)
-        for _ in range(1 + int(rng.integers(3))):
-            j = now[2][int(rng.integers(len(now[2])))] if rng.random() < 0.7 else int(rng.integers(n))
-            if len(ops[j]["ways"]) > 1 and rng.random() < 0.5:
-                y[j] = int(rng.integers(len(ops[j]["ways"])))
-            else:
-                p[j] += float(rng.standard_normal()) * 1000.0
-        new = lay(ops, deps, kids, p, y)
-        if new[1] <= now[1] + SLACK * (1 - turn / TURNS) * rng.random():
-            now, prio, way = new, p, y
-            if new[1] <= best[1]:
-                best, keep = new, y
-    return deps, best[0], best[1], keep
+    return (deps,) + mend(ops, [sorted(d) for d in deps], kids, lay(ops, deps, kids, tail))
 
 
-def lay(ops, deps, kids, tail, way):
+def lay(ops, deps, kids, tail):
     n = len(ops)
-    done, can, why, free, last, seq = [0.0] * n, [0.0] * n, [-1] * n, {}, {}, []
-    q = [o["ways"][y][0] for o, y in zip(ops, way)]
-    cost = [o["ways"][y][1] for o, y in zip(ops, way)]
+    can, seq = [0.0] * n, []
     left = [len(d) for d in deps]
-    ready = {k: [] for k in "vstygx"}
-    for k in ready:
-        free[k] = 0.0
+    ready, free = {k: [] for k in "vstygx"}, {k: 0.0 for k in "vstygx"}
     for j in range(n):
         if not left[j]:
-            ready[q[j]].append(j)
+            ready[ops[j]["ways"][0][0]].append(j)
     for _ in range(n):
         at, k = min((max(free[k], min(can[j] for j in r)), k) for k, r in ready.items() if r)
-        r = ready[k]
-        c = max((j for j in r if can[j] <= at), key=lambda j: tail[j])
-        c = max((j for j in r if can[j] <= at + NEAR * cost[c]), key=lambda j: tail[j])
-        r.remove(c)
-        at = max(free[k], can[c])
-        if free[k] > can[c]:
-            why[c] = last[k]
-        seq.append((c, at))
+        c = max((j for j in ready[k] if can[j] <= at), key=lambda j: tail[j])
+        ready[k].remove(c)
+        seq.append(c)
+        cost = ops[c]["ways"][0][1]
         if k != "x":
-            free[k], last[k] = at + cost[c], c
-        done[c] = at + cost[c] + ops[c]["late"]
+            free[k] = at + cost
         for j in kids[c]:
             left[j] -= 1
-            if done[c] + WAKE > can[j]:
-                can[j], why[j] = done[c] + WAKE, c
+            can[j] = max(can[j], at + cost + ops[c]["late"] + WAKE)
             if not left[j]:
-                ready[q[j]].append(j)
-    end = max(done)
-    chain = [done.index(end)]
-    while why[chain[-1]] >= 0:
-        chain.append(why[chain[-1]])
-    return seq, end, chain
+                ready[ops[j]["ways"][0][0]].append(j)
+    return seq
+
+
+def times(seq, p, was, deps, q, cost, late):
+    start, done, why = list(was[0]), list(was[1]), list(was[2])
+    free, last = [0.0] * 6, [-1] * 6
+    for j in seq[max(p - 60, 0):p]:
+        free[q[j]], last[q[j]] = start[j] + cost[j], j
+    free[5], last[5] = 0.0, -1
+    for j in seq[p:]:
+        k = q[j]
+        at, by = free[k], last[k]
+        for i in deps[j]:
+            if done[i] > at:
+                at, by = done[i], i
+        start[j], why[j] = at, by
+        at += cost[j]
+        done[j] = at + late[j]
+        if k < 5:
+            free[k], last[k] = at, j
+    return start, done, why
+
+
+def mend(ops, deps, kids, seq):
+    n = len(ops)
+    rng = np.random.default_rng(SEED)
+    ways = [[("vstygx".index(w[0]), w[1]) for w in o["ways"]] for o in ops]
+    late = [o["late"] + WAKE for o in ops]
+    way = [0] * n
+    q, cost = [w[0][0] for w in ways], [w[0][1] for w in ways]
+    best = now = None
+    was = ([0.0] * n, [0.0] * n, [-1] * n)
+    for turn, (a, b, c, d, e) in enumerate(rng.random((TURNS, 5)).tolist()):
+        new, j, old, p = seq, 0, way[0], 0
+        if turn:
+            j = chain[int(a * len(chain))] if b < 0.7 else int(a * n)
+            old, p = way[j], at[j]
+            if len(ways[j]) > 1 and c < 0.3:
+                way[j] = 1 - old
+                q[j], cost[j] = ways[j][way[j]]
+            if way[j] == old or c < 0.15:
+                lo = max([at[i] + 1 for i in deps[j]] + [0])
+                hi = min([at[i] - 1 for i in kids[j]] + [n - 1])
+                to = min(max(p + int((d - 0.5) * (40 if c < 0.8 else 300)), lo), hi)
+                if to == p and way[j] == old:
+                    continue
+                new = seq[:p] + seq[p + 1:]
+                new.insert(to, j)
+                p = min(p, to)
+        got = times(new, p, was, deps, q, cost, late)
+        worth = max(got[1]) + SOON * sum(got[1]) / n
+        if now is None or worth <= now + SLACK * (1 - turn / TURNS) * e:
+            now = worth
+            seq = sorted(new, key=lambda i: got[0][i])
+            was = times(seq, 0, got, deps, q, cost, late)
+            at = [0] * n
+            for p, i in enumerate(seq):
+                at[i] = p
+            chain = [was[1].index(max(was[1]))]
+            while was[2][chain[-1]] >= 0:
+                chain.append(was[2][chain[-1]])
+            if best is None or max(was[1]) < best[1]:
+                best = ([(i, was[0][i]) for i in seq], max(was[1]), list(way))
+        elif way[j] != old:
+            way[j] = old
+            q[j], cost[j] = ways[j][old]
+    return best
 
 
 def rank_program(g, core, T, topo):

@@ -5,7 +5,7 @@ C, H, R, P0 = 384, 56, 3, 48
 STEP = [1, 2, 1]
 XO = 8 * H
 G0 = [388, 452, 452]
-CH = [[(192, 384), (0, 192)]] * 4
+CH = [[(192, 384), (0, 192)]] * 3 + [[(128, 384), (0, 128)]]
 SEND = [[(192, 384), (0, 192)]] * 3
 BIG = 2.0 ** 80
 U = -2.0 ** 75
@@ -13,9 +13,9 @@ B1K, LIFT = 1024.0, 2.0 ** 24
 MAGIC = 1.5 * 2.0 ** 23
 OFF = 13112.0
 NEW = 50 * 512
-CYC, VFIX, SFIX, WAKE = 0.9, 20.0, 75.0, 140.0
-FLY, RATE, CALL, FIRST, LOAD = 1500.0, 80.0, 300.0, 1000.0, 1400.0
-TURNS, SLACK, SOON, SEED = 300000, 100.0, 0.08, 7
+CYC, VFIX, SFIX, WAKE = 1.03, 10.0, 76.0, 185.0
+FLY, RATE, NEARBY, CALL, FIRST, LOAD = 1500.0, 80.0, 1.5, 250.0, 1000.0, 1300.0
+TURNS, SLACK, SOON, SHAKE, FAR, SEED = 280000, 200.0, 0.08, 200, (30, 200), 1
 
 ARENA = {"f": 0, "h": 0, "i": 0, "w": 0}
 AT = {}
@@ -28,24 +28,25 @@ def _take(ar, name, n):
     ARENA[ar] += (n + al - 1) // al * al
 
 
-for _n, _k in [("m", 448), ("r0", 64), ("nv0", 64), ("cum0", 72), ("id", 64), ("vr0", 456), ("vr1", 1032), ("vr2", 520), ("vr3", 456),
-               ("s", 384), ("ms", 384), ("tb", 392), ("pc", 16), ("j16", 128), ("j8", 64), ("j4", 112), ("m16", 128), ("lift", 384),
-               ("m4", 112), ("sel", 64), ("down", 64), ("up", 64), ("kp", 112), ("k3", 72), ("i16", 72), ("cj", 72), ("c513", 48),
-               ("k2", 136), ("junk", 640), ("mq", 64), ("y", 64), ("yv", 64), ("sg4", 8), ("ys", 64), ("wu", 64), ("nq", 64),
-               ("rest", 256), ("oz", 64), ("mark", 64), ("ed0", 64), ("nv", 192), ("g", 128), ("born", 192), ("np", 200),
-               ("rlo", 128), ("rhi", 128), ("nc", 192), ("d", 192), ("ed", 192), ("p", 384), ("fa", 128), ("fx", 384),
-               ("pay", 192), ("v2", 192), ("rv", 128), ("vb8", 64), ("tp", 64), ("pd", 64), ("p0", 112), ("pr", 112), ("sr", 112),
-               ("sd", 112), ("lh", 112), ("pk", 112), ("pkr", 384), ("pkd", 384), ("t3o", 72), ("hold", 384), ("dg", 1152),
-               ("t3", 216), ("b1", 72), ("gs", 72), ("xl", 24)]:
+for _n, _k in [("k2", 120), ("none", 16), ("r0", 64), ("nv0", 64), ("cum0", 72), ("id", 64), ("cum", 128), ("n1", 64), ("m", 512),
+               ("vr0", 456), ("vr1", 520), ("vr2", 520), ("vr3", 456), ("s", 384), ("ms", 384), ("tb", 392), ("pc", 16),
+               ("j16", 128), ("j8", 64), ("j4", 112), ("m16", 128), ("lift", 384), ("m4", 112), ("sel", 64), ("down", 64),
+               ("up", 64), ("kp", 112), ("k4", 96), ("cj", 72), ("junk", 640), ("mq", 64), ("y", 64), ("yv", 64), ("sg4", 8),
+               ("ys", 64), ("wu", 64), ("nq", 128), ("rest", 256), ("oz", 64), ("ed0", 64), ("nv", 192), ("g", 128),
+               ("born", 192), ("r1", 192), ("d", 192), ("ed", 192), ("p", 384), ("fa", 64), ("fx", 384), ("pay", 192), ("v2", 192),
+               ("rv", 128), ("vb8", 64), ("tp", 64), ("pd", 64), ("p0", 112), ("pr", 112), ("sr", 112), ("sd", 112), ("lh", 112),
+               ("pk", 112), ("pkr", 384), ("pkd", 384), ("t4o", 96), ("hold", 384), ("dg", 1152), ("t4", 288), ("b1", 144),
+               ("gs", 72), ("xl", 24)]:
     _take("f", _n, _k)
 for _t in range(R):
-    _take("w", "en%d" % _t, 8)
+    _take("w", "en%d" % _t, 12)
     _take("w", "el%d" % _t, 96)
-for _n, _k in [("eq", 384), ("pos", 448), ("qr", 384), ("sg", 392), ("cc", 392), ("rs", 392), ("lc", 392), ("li", 392), ("kr", 392)]:
+for _n, _k in [("eq", 384), ("pos", 512), ("qr", 384), ("sg", 392), ("cc", 392), ("rs", 392), ("lc", 392), ("li", 392), ("kr", 392),
+               ("step", 384)]:
     _take("h", _n, _k)
-for _n, _k in [("pi", 8), ("pj", 8), ("ui", 8), ("xi", 72), ("xk", 72), ("xb", 72), ("ki2", 24), ("hi", 24)]:
+for _n, _k in [("pi", 8), ("pj", 8), ("ui", 8), ("xi", 24), ("xk", 24), ("xb", 24), ("ki2", 48)]:
     _take("i", _n, _k)
-for _n, _k in [("zu", 4), ("uo", 8), ("es", 12), ("pu", 8), ("ru", 8), ("rk", 4), ("kl", 72)]:
+for _n, _k in [("zu", 4), ("uo", 8), ("pu", 8), ("ru", 8), ("rk", 4), ("kl", 72)]:
     _take("w", _n, _k)
 
 X4, U8, BF, F32 = "float8_e4m3fn_x4", "uint8", "bfloat16", "float32"
@@ -105,7 +106,7 @@ def collect(g, T, topo, core, rank):
         if d[0] == "@":
             return ap(d[1]).indirect(ap(d[2]))
         if d[3] < 0:
-            return T[d[0]][:, d[2] - 1:d[1] - 1:-1] if d[1] else T[d[0]][:, d[2] - 1::-1]
+            return T[d[0]][:, d[2] - 1:d[1] - 1:d[3]] if d[1] else T[d[0]][:, d[2] - 1::d[3]]
         return T[d[0]][:, d[1]:d[2]:d[3]] if d[3] > 1 else T[d[0]][:, d[1]:d[2]]
 
     def add(ways, rd, wr, late=0.0, **k):
@@ -142,8 +143,11 @@ def collect(g, T, topo, core, rank):
         else:
             add([vcp(out, a)], [a], [out])
 
+    def vscan(out, d0, d1, init, op0, op1):
+        return ("v", cyc(out, [d0, d1]), lambda: g.vector.tensor_tensor_scan(ap(out), ap(d0), ap(d1), ap(init), op0, op1))
+
     def scan(out, d0, d1, init, op0, op1):
-        add([("v", cyc(out, [d0, d1]), lambda: g.vector.tensor_tensor_scan(ap(out), ap(d0), ap(d1), ap(init), op0, op1))], [d0, d1, init], [out])
+        add([vscan(out, d0, d1, init, op0, op1)], [d0, d1, init], [out])
 
     def sact(out, a, fn, scale=None, bias=None, acc=None):
         k = {}
@@ -188,8 +192,12 @@ def collect(g, T, topo, core, rank):
     def iota(out, pat, base, cm=0):
         add([giota(out, pat, base, cm)], [], [out])
 
+    def vset(out, c):
+        return ("v", cyc(out, []), lambda: g.vector.memset(ap(out), float(c)))
+
     def fill(out, c):
-        add([("v", cyc(out, []), lambda: g.vector.memset(ap(out), float(c))), giota(out, [[0, size(out)]], int(c))], [], [out])
+        src = v("half", 0, size(out))
+        add([vset(out, c), giota(out, [[0, size(out)]], int(c)), sact(out, src, F.Identity, 0.0, float(c))], [src], [out])
 
     def quant(name, c0, c1, src):
         q, s = v("q" + name, c0, c1), v("s" + name, c0, c1)
@@ -205,8 +213,9 @@ def collect(g, T, topo, core, rank):
         e = g.sync if q == "y" else g.scalar
         add([(q, 60, lambda: e.dma_start(out(), src()))], rd, wr, late=LOAD + nbytes / 200.0, dma=True, last=last)
 
-    def zero(out, src):
-        dma("y", lambda: ap(out), lambda: ap(src), [src], [out], 128 * 4 * size(out))
+    def again(out, src):
+        pick = lambda: g.affine_select(ap(out), ap(src), [[0, size(out)]], A.is_gt, 0.0, 1, 0)
+        add([sact(out, src, F.Identity), vcp(out, src), ("g", 170 + 2 * CYC * size(out), pick)], [src], [out])
 
     def byt(d):
         return ap(d).bitcast(dt.uint8)
@@ -216,14 +225,13 @@ def collect(g, T, topo, core, rank):
     dma("y", lambda: T.zi[:, 0:3], lambda: T.z[:, :], [], [v("zi", 0, 3)], 2e3)
     dma("s", lambda: T.ub[:, :], lambda: T.u[:, :], [], [v("ub")], 131e3)
     for k, (c0, c1) in enumerate(CH[0]):
-        dma("ys"[k % 2], lambda c0=c0, c1=c1: T.pool0[:, XO + 4 * c0:XO + 4 * c1], lambda c0=c0, c1=c1: T.x[:, 4 * c0:4 * c1], [],
+        dma("y", lambda c0=c0, c1=c1: T.pool0[:, XO + 4 * c0:XO + 4 * c1], lambda c0=c0, c1=c1: T.x[:, 4 * c0:4 * c1], [],
             [v("pool0", XO + 4 * c0, XO + 4 * c1)], 131e3 + 1024 * (C - c0))
-    dma("y", lambda: byt(v("qw")), lambda: T.wc[:, :], [v("pool0", XO, XO + 4 * C)], [v("qw")], 262e3)
-    dma("y", lambda: T.sw[:, :], lambda: T.ws[:, :], [v("pool0", XO, XO + 4 * C)], [v("sw")], 330e3)
-    dma("y", lambda: T.vb[:, :], lambda: T.v[:, :], [v("pool0", XO, XO + 4 * C)], [v("vb")], 460e3)
 
+    add([vset(v("half"), 0.5)], [], [v("half")])
     iota(v("pi", 0, 1), [[0, 1]], 0, 1)
-    iota(v("tb", 1, 386), [[1, 385]], 0)
+    tb, hf = v("tb", 1, 386), v("half", 0, 385)
+    add([giota(tb, [[1, 385]], 0), vscan(tb, hf, hf, -1.0, A.add, A.add)], [hf], [tb])
     fill(v("tb", 0, 1), C)
     iota(v("j16", 0, 128), [[0, 8], [1, 16]], 0)
     iota(v("j8", 0, 64), [[0, 8], [1, 8]], 0)
@@ -238,27 +246,25 @@ def collect(g, T, topo, core, rank):
     ts(C4, TMP, 2.0, A.mult, T4, A.add)
     lin(C4, C4, None, 18 * B1K)
     lin(CE, Q16, 2 * B1K, 32 * B1K)
-    add([("v", cyc(v("half"), []), lambda: g.vector.memset(T.half[:, :], 0.5))], [], [v("half")])
+    fill(("f", AT["none"][1], AT["m"][1], 1), 0)
     fill(("f", AT["m"][1] + C, AT["vr0"][1] + 400, 1), 0)
     for t in (1, 2, 3):
-        zero(v("vr%d" % t, 8, 400), v("vr0", 8, 400))
-    zero(v("fx", 0, 384), v("vr0", 8, 392))
+        fill(v("vr%d" % t, 8, 400), 0)
+    fill(v("fx", 0, 384, 2), 0)
+    fill(v("t4", 2, 288, 4), 0)
     fill(v("dh", 4 * C, 4 * C + 8), 0)
     for t in range(R):
         fill(v("pool%d" % t, XO + 4 * C, XO + 4 * C + 16), 0)
     fill(v("mt", 448, 512), 0)
-    fill(v("pos", C, 448), 0)
-    fill(v("k2", 0, 66), 1000)
+    fill(v("pos", C, 512), 0)
+    fill(v("k2", 0, 66), 513)
     fill(v("k2", 66 + P0, 67 + P0), 2 * (P0 + 2))
-    fill(v("k2", 66 + P0 + 6, 130), 0)
-    fill(v("c513", 0, 48), 513)
     fill(v("born", 128, 192), 1)
-    fill(v("np", 7, 8), 1)
-    fill(v("rlo", 0, 128), 1023)
-    fill(v("rlo", 0, 128, 64), -1)
-    lin(v("rhi", 0, 128), v("rlo", 0, 128), -8192.0, -8193.0)
+    fill(v("rest", 192, 193), 0)
     fill(v("pr", 2 * P0, 112 + 112), C)
-    lin(v("mark", 0, 64), v("born", 128, 192), U)
+    add([vset(v("step", 0, C), U), sact(v("step", 0, C), v("half", 0, C), F.Identity, 2 * U)], [v("half", 0, C)], [v("step", 0, C)])
+    iota(v("d", 0, 192), [[0, 3], [-2 ** 15, 64]], 1 - 2 ** 15)
+    iota(v("n1", P0 + 2, P0 + 6), [[-2, 2], [-H, 2]], 2 - G0[1])
     iota(v("id", P0, P0 + 6), [[512, 3], [H, 2]], NEW - 512 + G0[0] - 2)
     iota(v("id", P0 + 6, 64), [[1, 10]], 0)
     ts(v("sel", 0, 64), v("j8", 0, 64), QQ, A.not_equal, BIG * 2.0 ** 13, A.mult)
@@ -272,10 +278,7 @@ def collect(g, T, topo, core, rank):
     tt(v("lift", 0, 64), v("lift", 0, 64), v("lift", 64, 128), A.add)
     lin(v("lift", 15, 64, 16), v("lift", 15, 64, 16), 1.0 / (U * LIFT))
     for a, b in ((64, 128), (128, 256), (256, 384)):
-        lin(v("lift", a, b), v("lift", 0, b - a))
-    iota(v("i16", 0, 24), [[16, 24]], int(OFF))
-    iota(v("i16", 24, 72), [[0, 2], [16, 24]], 0)
-    lin(v("cj", 0, 72), v("i16", 0, 72), None, Q16)
+        again(v("lift", a, b), v("lift", 0, b - a))
     lin(v("qr", 0, C), v("tb", 1, C + 1), -1.0 / 512, 0.375)
     add([("g", 170 + 2 * CYC * 516, lambda: g.affine_select(T.eye[:, 0:516], T.half[:, 0:516], [[1, 516]], A.is_equal, 0.0, -3, -4))],
         [v("half", 0, 516)], [v("eye", 0, 516)])
@@ -284,7 +287,7 @@ def collect(g, T, topo, core, rank):
     fill(v("kr", 0, 392, H), 0)
     iota(v("j4", 0, 112), [[0, 28], [2048, 4]], 0)
     iota(v("kp", 0, 112), [[0, H], [1024, 2]], 0)
-    iota(v("k3", 0, 72), [[0, 24], [1024, 3]], 0)
+    iota(v("k4", 0, 96), [[0, 24], [1024, 4]], 0)
     ts(v("lc", 0, 392), v("li", 0, 392), QQ, A.is_lt, 2.0 ** -120, A.mult)
     ts(v("m4", 0, 112), v("j4", 0, 112), TMP, A.subtract, B1K, A.min)
     lin(v("m4", 3, 112, 4), v("m4", 3, 112, 4), None, -8 * B1K)
@@ -297,15 +300,13 @@ def collect(g, T, topo, core, rank):
         [v("qu"), v("uo", 0, 8)], [v("qu2")])
     add([("s", 65 + 200 * CYC, lambda: g.scalar.activation(T.su2[:, 0:128], T.su[:, 0:128].indirect(ap(v("uo", 0, 8))), F.Copy))],
         [v("su"), v("uo", 0, 8)], [v("su2")])
-    quant("v", 0, 128, v("vb"))
-
-    PLAIN, OWN = [0, 128, 256], [64, 192, 320]
 
     def marks(t, e, nv):
-        act(v("p", PLAIN[t], PLAIN[t] + 64), nv, F.Relu, -BIG, THR)
+        a = 128 * t
+        act(v("p", a, a + 64), nv, F.Relu, -BIG, THR)
+        scan(v("p", a + 64, a + 128), v("p", a, a + 64), v("sel", 0, 64), BIG * 2.0 ** 13, A.min, A.max)
         act(v("fa", 0, 64), e, F.Relu, -2.0, 2.0 * C - 1)
-        lin(v("fx", 128 * t + 1, 128 * t + 128, 2), v("fa", 0, 64), -1.0, 2.0 * C)
-        tt(v("p", OWN[t], OWN[t] + 64), v("p", PLAIN[t], PLAIN[t] + 64), v("sel", 0, 64), A.max)
+        lin(v("fx", a + 1, a + 128, 2), v("fa", 0, 64), -1.0, 2.0 * C)
 
     cp(v("zu", 0, 3), v("zi", 0, 3))
     lin(v("r0", 0, P0), ind(v("tb", 0, 386), v("zu", 0, 3)))
@@ -315,16 +316,16 @@ def collect(g, T, topo, core, rank):
     for k in range(2):
         ts(v("en0", 4 * k, 4 * k + 4), v("ed0", 15, 64, 16), CE, A.add)
     marks(0, v("cum0", 0, 64), v("nv0", 0, 64))
-    cp(ind(v("vr0", 8, 456), v("en0", 0, 4)), v("mark", 0, 64))
+    cp(ind(v("vr0", 8, 456), v("en0", 0, 4)), v("step", 0, 64))
 
     k2 = lambda a, b: v("k2", 66 + a, 66 + b)
     lin(k2(0, P0), v("r0", 0, P0), 2.0, 2.0)
     act(v("junk", 0, 100), k2(-52, P0), F.Sign, None, -3.0, acc=k2(P0 + 1, P0 + 2))
     for k, (more, least) in enumerate([(58, 5.0), (58, 7.0), (66, 9.0), (66, 11.0)]):
         act(v("junk", 128 * k + 128, 128 * k + 178 + more), k2(-more, P0 + 2), F.Sign, None, -least, acc=k2(P0 + 2 + k, P0 + 3 + k))
-    scan(v("id", 1, P0), v("r0", 0, P0 - 1), v("c513", 0, P0 - 1), 0.0, A.add, A.add)
+    scan(v("id", 1, P0), v("r0", 0, P0 - 1), v("k2", 0, P0 - 1), 0.0, A.add, A.add)
     lin(v("mq", 0, 64), k2(0, 64), 2.0 ** 14, OFF)
-    tt(v("y", 0, 64), v("id", 0, 64), v("mq", 0, 64), A.subtract)
+    scan(v("y", 0, 64), v("id", 0, 64), v("mq", 0, 64), -1.0, A.max, A.subtract)
     scan(v("yv", 0, 64), v("y", 0, 64), v("lift", 0, 64), 0.0, A.min, A.mult)
     for k in range(4):
         act(v("junk", 128 * k + 128, 128 * k + 192), v("y", 0, 64), F.Sign, -1.0 / U, v("yv", 16 * k + 15, 16 * k + 16), acc=v("sg4", k, k + 1))
@@ -332,39 +333,49 @@ def collect(g, T, topo, core, rank):
     cp(ind(v("ys", 0, 64), v("rk", 0, 4)), v("y", 0, 64))
     lin(v("wu", 0, 64), v("ys", 0, 64), -2.0 ** -15, MAGIC)
     lin(v("nq", 0, 64), v("wu", 0, 64), 2.0 ** 15, -MAGIC * 2.0 ** 15)
-    tt(v("rest", 0, 64), v("nq", 0, 64), v("ys", 0, 64), A.add)
-    for t in (1, 2, 3):
-        lin(v("nv", 64 * t - 64, 64 * t), v("wu", 0, 64), None, -MAGIC - 2 * t)
-    for t in (1, 2):
-        relu(v("g", 64 * t - 64, 64 * t), v("rest", 0, 64), None, OFF - NEW - 512 * (t - 1) + G0[1] - G0[0])
+    scan(v("rest", 0, 64), v("ys", 0, 64), v("nq", 0, 64), 0.0, A.min, A.add)
+    lin(v("n1", 0, P0 + 2), k2(0, P0 + 2), 0.5, -2.0)
+    cp(ind(v("nv", 0, 64), v("rk", 0, 4)), v("n1", 0, 64))
+    relu(v("r1", 0, 64), v("nv", 0, 64), None, -1.0)
+    ts(v("born", 0, 64), v("nv", 0, 64), -100.0, A.is_gt)
+    lin(v("g", 0, 64), v("nv", 0, 64), -1.0)
+    scan(v("cum", 1, 64), v("r1", 0, 63), v("born", 0, 63), 0.0, A.add, A.add)
+    lin(v("nq", 64, 128), v("wu", 0, 64), None, -MAGIC - 4)
+    lin(v("nv", 128, 192), v("wu", 0, 64), None, -MAGIC - 6)
+    relu(v("g", 64, 128), v("rest", 0, 64), None, OFF - NEW - 512 + G0[1] - G0[0])
+    scan(v("nv", 64, 128, -1), v("nq", 64, 128, -1), v("g", 64, 128, -1), -1024.0, A.max, A.subtract)
+    relu(v("born", 64, 128), v("g", 64, 128), -1.0, 1.0)
+    relu(v("r1", 64, 192), v("nv", 64, 192), None, -1.0)
+    scan(v("cum", 65, 128), v("r1", 64, 127), v("born", 64, 127), 0.0, A.add, A.add)
+    scan(v("rest", 193, 256), v("r1", 128, 191), v("born", 128, 191), 0.0, A.add, A.add)
     for t, a, b in ((1, 0, 64), (2, 64, 192)):
-        n = b - a
-        tt(v("nv", a, a + 64), v("nv", a, a + 64), v("g", a, a + 64), A.subtract)
-        relu(v("born", a, a + 64), v("g", a, a + 64), -1.0, 1.0)
-        tt(v("np", 8 + a, 8 + b), v("nv", a, b), v("born", a, b), A.max)
-        scan(v("rest", 64 + a, 64 + b), v("rlo", 0, n), v("np", 7 + a, 7 + b), 0.0, A.min, A.add)
-        lin(v("nc", a, b), v("np", 7 + a, 7 + b), None, -2.0 ** 15)
-        scan(v("d", a, b), v("rhi", 0, n), v("nc", a, b), -2.0 ** 22, A.max, A.add)
-        tt(v("rest", 64 + a, 128 + a), v("rest", 64 + a, 128 + a), v("g", a, a + 64), A.max)
-        scan(v("ed", a, b), v("rest", 64 + a, 64 + b), v("m16", 0, n), -B1K, A.max, A.add)
-        ts(v("es", a // 16, b // 16), v("ed", a + 15, b, 16), CE, A.add)
-        for k in range(2):
-            ts(v("en%d" % t, 4 * k, 4 * k + 4), v("ed", a + 15, a + 64, 16), CE, A.add, 447.0, A.min)
+        scan(v("rest", 64 + a, 128 + a, -1), v("cum", a, a + 64, -1), v("g", a, a + 64, -1), 2048.0, A.min, A.max)
+        scan(v("ed", a, b), v("rest", 64 + a, 64 + b), v("m16", 0, b - a), -B1K, A.max, A.add)
+        ts(v("en%d" % t, 0, 4), v("ed", a + 15, a + 64, 16), CE, A.add)
+        ts(v("en%d" % t, 4, 4 + (b - a) // 16), v("ed", a + 15, b, 16), CE, A.add)
         marks(t, v("rest", 64 + a, 128 + a), v("nv", a, a + 64))
-        tt(v("pay", a, b), v("rest", a, b), v("d", a, b), A.subtract)
+        scan(v("pay", a, b), v("rest", a, b), v("d", a, b), 2.0 ** 20, A.min, A.subtract)
         lin(v("v2", a, b), v("pay", a, b), U)
-    for t in (1, 2, 3):
-        cp(ind(v("vr%d" % t, 8, (1032, 520, 456)[t - 1]), v("es", 4 * t - 4, 4 * t)), v("v2", 64 * t - 64, 64 * t))
-        scan(v("hold", 0, C), v("vr%d" % t, 8, 8 + C), v("vr%d" % t, 8, 8 + C), 0.0, A.min, A.min)
-        scan(v("dg", C * (t - 1), C * t), v("hold", 0, C), v("lift", 0, C), 0.0, A.min, A.mult)
-    for a, b, sh, msk, one in ((0, 24, 8, 511, 1.0), (24, 72, 14, 1023, -1.0)):
-        tt(v("xi", a, b), v("dg", 16 * a + 15, 16 * b, 16), v("cj", a, b), A.add)
-        ts(v("xk", a, b), v("xi", a, b), sh, A.logical_shift_right, 126, A.bitwise_and)
-        ts(v("kl", a, b), v("xk", a, b), one, A.add)
-        ts(v("xb", a, b), v("xi", a, b), msk, A.bitwise_and)
-        cp(v("t3", 3 * a, 3 * b, 3), v("xb", a, b))
-        lin(v("b1", a, b), v("t3", 3 * a, 3 * b, 3), B1K, B1K)
-        ts(v("gs", a, b), v("xb", a, b), float(C), A.is_ge, -float(G0[a // 24] + 2 * H), A.mult)
+    for t in range(R):
+        a, b, vr = 24 * t, 24 * t + 24, "vr%d" % (t + 1)
+        cp(ind(v(vr, 8, 520 if t < 2 else 456), v("en%d" % (t + 1), 0, 4) if t < 2 else v("en2", 8, 12)), v("v2", 64 * t, 64 * t + 64))
+        scan(v("hold", 0, C), v(vr, 8, 8 + C), v("step", 0, C), 0.0, A.min, A.add)
+        scan(v("dg", C * t, C * t + C), v("hold", 0, C), v("lift", 0, C), 0.0, A.min, A.mult)
+        got, base = v("dg", 16 * a + 15, 16 * b, 16), v("t4", 4 * a, 4 * b, 4)
+        if t:
+            ts(v("kl", a, b), got, 2.0 ** -14, A.mult, -1.0, A.add)
+            lin(v("cj", a, b), got, 2.0 ** -15, MAGIC)
+            lin(v("cj", a, b), v("cj", a, b), -2.0 ** 15, MAGIC * 2.0 ** 15)
+            tt(base, got, v("cj", a, b), A.add)
+        else:
+            ts(v("xi", a, b), got, OFF, A.add)
+            ts(v("xk", a, b), v("xi", a, b), 8, A.logical_shift_right, 126, A.bitwise_and)
+            ts(v("kl", a, b), v("xk", a, b), 1.0, A.add)
+            ts(v("xb", a, b), v("xi", a, b), 511, A.bitwise_and)
+            cp(base, v("xb", a, b))
+        lin(v("b1", 2 * a, 2 * b, 2), base, B1K, B1K - 1)
+        lin(v("b1", 2 * a + 1, 2 * b, 2), base, None, 1.0)
+        ts(v("gs", a, b), base, float(C), A.is_ge, -float(G0[t] + 2 * H), A.mult)
     relu(v("oz", 0, H), v("nv", 128, 128 + H), None, 0.0)
     dma("y", lambda: T.oz[:, :], lambda: T.f[0:128:16, AT["oz"][1]:AT["oz"][1] + H], [v("oz", 0, H)], [], 2e3, last=True)
 
@@ -378,7 +389,7 @@ def collect(g, T, topo, core, rank):
         sent[0] += k
         pick = byt if codes else ap
         return k, add([("g", c, lambda: g.remote_dma(pick(dst), pick(src), T.sem[sem], T.sem.sent, pid, rid, m))], [src], [],
-                      late=FLY + nbytes / RATE)
+                      late=FLY + nbytes / RATE / (NEARBY if topo.chip(core) == topo.chip(peer) else 1.0))
 
     for t in range(R):
         pool, nxt, xq, lq = "pool%d" % t, "pool%d" % (t + 1), "x%d" % t, "l%d" % t
@@ -400,12 +411,19 @@ def collect(g, T, topo, core, rank):
             add([("x", 0, None)], [], [v("q" + lq, c0, c1), v("s" + lq, c0, c1)], after=[o1, o2], sem=sem, cnt=k1 + k3)
             for b in range(4):
                 lin(v("dh", 4 * c0 + b, 4 * c1, 4), mm(3 + b, "e", 128 * b, lq, c0, c1))
-        tt(v("rv", 0, 128), ind(v("m", 0, 448), w("en", 0, 8)), v("p", PLAIN[t], PLAIN[t] + 128), A.subtract)
+        if t == 0:
+            landed = [v("ql0", *SEND[0][0])]
+            dma("y", lambda: byt(v("qw")), lambda: T.wc[:, :], landed, [v("qw")], 262e3)
+            dma("y", lambda: T.sw[:, :], lambda: T.ws[:, :], landed, [v("sw")], 330e3)
+        if t == 1:
+            dma("y", lambda: T.vb[:, :], lambda: T.v[:, :], [v("ql1")], [v("vb")], 131e3)
+            quant("v", 0, 128, v("vb"))
+        tt(v("rv", 0, 128), ind(v("m", 0, 512), w("en", 0, 8)), v("p", 128 * t, 128 * t + 128), A.subtract)
         scan(v("vb8", 0, H), v("down", 0, H), v("rv", 64, 64 + H), 0.0, A.add, A.max)
         for k in range(ns):
             o, a, b = v("sg", H * k, H * k + H), v("rv", 0, H), v("vb8", 8 * k + 7, 8 * k + 8)
             add([sact(o, a, F.Sign, -1.0, b), vts(o, a, b, A.subtract, -1.0, A.mult)], [a, b], [o])
-        tt(v("tp", 0, 64), ind(v("pos", 0, 448), w("en", 0, 4)), v("p", OWN[t], OWN[t] + 64), A.add)
+        tt(v("tp", 0, 64), ind(v("pos", 0, 512), w("en", 0, 4)), v("p", 128 * t + 64, 128 * t + 128), A.add)
         scan(v("pd", 0, H), v("up", 0, H), v("tp", 0, H), 0.0, A.add, A.min)
         ts(v("pu", 0, ns), v("pd", 7, 8 * ns, 8), -512.0, A.mult, 193.0, A.add)
         lin(v("p0", 0, 16 * ns), ind(v("tb", 0, 386), v("pu", 0, ns)))
@@ -428,20 +446,18 @@ def collect(g, T, topo, core, rank):
             o = mm((7, 0, 1, 2)[b], "w", 128 * b, "m", 0, 128)
             relu(v("rl", b, 448, 4), (o[0], o[1], o[1] + 112, 1), 0.03125)
             tt(v(pool, b, XO, 4) if b < 2 else v(pool, XO + 4 * G0[t] + b, None, 4), v("rl", b, 448, 4), v("aa", b, 448, 4), A.add)
-        tt(v("lh", 0, 112, 2), v("pr", 0, 112, 2), v("pr", 1, 112, 2), A.min)
-        tt(v("lh", 1, 112, 2), v("pr", 0, 112, 2), v("pr", 1, 112, 2), A.max)
+        scan(v("lh", 0, 111, -2), v("pr", 0, 111, -2), v("pr", 1, 112, -2), 512.0, A.min, A.min)
+        scan(v("lh", 1, 112, -2), v("pr", 0, 111, -2), v("pr", 1, 112, -2), 512.0, A.min, A.max)
         scan(v("pk", 0, 112), v("kp", 0, 112), v("lh", 0, 112), 0.0, A.mult, A.add)
         lin(v("pkr", 0, C), ind(v("pk", 0, 112), v("kl", 24 * t, 24 * t + 24)), U)
         scan(v("pkd", 0, C), v("pkr", 0, C), v("lift", 0, C), 0.0, A.min, A.mult)
-        t3 = lambda k: v("t3", 72 * t + k, 72 * t + 72, 3)
-        ts(v("ki2", 0, 24), v("pkd", 15, C, 16), -1.0, A.add)
-        ts(v("hi", 0, 24), v("ki2", 0, 24), 1023, A.bitwise_and)
-        tt(t3(1), v("pkd", 15, C, 16), v("b1", 24 * t, 24 * t + 24), A.is_lt)
-        tt(t3(2), v("hi", 0, 24), t3(0), A.is_le)
-        scan(v("t3o", 0, 72), v("k3", 0, 72), v("t3", 72 * t, 72 * t + 72), 0.0, A.min, A.add)
-        tt(v("xl", 0, 24), v("t3o", 2, 72, 3), v("gs", 24 * t, 24 * t + 24), A.add)
+        ts(v("ki2", 0, 48, 2), v("pkd", 15, C, 16), -1.0, A.add)
+        ts(v("ki2", 1, 48, 2), v("ki2", 0, 48, 2), 1023, A.bitwise_and)
+        tt(v("t4", 96 * t + 1, 96 * t + 96, 2), v("ki2", 0, 48), v("b1", 48 * t, 48 * t + 48), A.is_lt)
+        scan(v("t4o", 0, 96), v("k4", 0, 96), v("t4", 96 * t, 96 * t + 96), 0.0, A.min, A.add)
+        tt(v("xl", 0, 24), v("t4o", 3, 96, 4), v("gs", 24 * t, 24 * t + 24), A.add)
         for b in range(4):
-            ts(w("el", 24 * b, 24 * b + 24), v("xl", 0, 24) if b < 2 else v("t3o", 2, 72, 3), 4.0, A.mult, float(b + (XO if b < 2 else 0)), A.add)
+            ts(w("el", 24 * b, 24 * b + 24), v("xl", 0, 24) if b < 2 else v("t4o", 3, 96, 4), 4.0, A.mult, float(b + (XO if b < 2 else 0)), A.add)
         for k, (c0, c1) in enumerate(CH[t + 1]):
             for b in range(4):
                 at, win = XO if t + 1 < R else 0, v(pool, 0, XO + 4 * C) if b < 2 else v(pool, XO)
@@ -451,8 +467,8 @@ def collect(g, T, topo, core, rank):
         quant("x3", c0, c1, v("pool3", 4 * c0, 4 * c1))
         o = mm(k, "v", 0, "x3", c0, c1)
         lin(v("yb", c0, c1), o)
-        dma("y", lambda c0=c0, c1=c1: T.oc[:, 4 * c0:4 * c1], lambda c0=c0, c1=c1: byt(v("qx3", c0, c1)), [v("qx3", c0, c1)], [], 98e3, last=True)
-        dma("sy"[k % 2], lambda c0=c0, c1=c1: T.y[:, c0:c1], lambda c0=c0, c1=c1: T.yb[:, c0:c1], [v("yb", c0, c1)], [], 98e3, last=True)
+        dma("y", lambda c0=c0, c1=c1: T.oc[:, 4 * c0:4 * c1], lambda c0=c0, c1=c1: byt(v("qx3", c0, c1)), [v("qx3", c0, c1)], [], 512 * (c1 - c0), last=True)
+        dma("sy"[k % 2], lambda c0=c0, c1=c1: T.y[:, c0:c1], lambda c0=c0, c1=c1: T.yb[:, c0:c1], [v("yb", c0, c1)], [], 512 * (c1 - c0), last=True)
     for k in range(4):
         dma("ys"[k % 2], lambda k=k: T.osc[4 * k:4 * k + 4, :], lambda k=k: T.sx3[32 * k:32 * k + 4, :], [v("sx3")], [], 2e3, last=True)
     return ops, sent[0]
@@ -485,34 +501,7 @@ def order(ops):
     for j in range(n):
         for i in deps[j]:
             kids[i].append(j)
-    tail = [0.0] * n
-    for j in range(n - 1, -1, -1):
-        tail[j] = ops[j]["ways"][0][1] + ops[j]["late"] + max([WAKE + tail[k] for k in kids[j]] + [0.0])
-    return (deps,) + mend(ops, [sorted(d) for d in deps], kids, lay(ops, deps, kids, tail))
-
-
-def lay(ops, deps, kids, tail):
-    n = len(ops)
-    can, seq = [0.0] * n, []
-    left = [len(d) for d in deps]
-    ready, free = {k: [] for k in "vstygx"}, {k: 0.0 for k in "vstygx"}
-    for j in range(n):
-        if not left[j]:
-            ready[ops[j]["ways"][0][0]].append(j)
-    for _ in range(n):
-        at, k = min((max(free[k], min(can[j] for j in r)), k) for k, r in ready.items() if r)
-        c = max((j for j in ready[k] if can[j] <= at), key=lambda j: tail[j])
-        ready[k].remove(c)
-        seq.append(c)
-        cost = ops[c]["ways"][0][1]
-        if k != "x":
-            free[k] = at + cost
-        for j in kids[c]:
-            left[j] -= 1
-            can[j] = max(can[j], at + cost + ops[c]["late"] + WAKE)
-            if not left[j]:
-                ready[ops[j]["ways"][0][0]].append(j)
-    return seq
+    return (deps,) + mend(ops, [sorted(d) for d in deps], kids)
 
 
 def times(seq, p, was, deps, q, cost, late):
@@ -535,7 +524,31 @@ def times(seq, p, was, deps, q, cost, late):
     return start, done, why
 
 
-def mend(ops, deps, kids, seq):
+def pack(seq, before, q, cost, lead, trail):
+    done, start, busy = {}, {}, [[] for _ in range(6)]
+    for j in seq:
+        at = max([done[i] for i in before[j]] + [0.0]) + lead[j]
+        line, k = busy[q[j]], 0
+        if q[j] < 5:
+            for a, b in line:
+                if a >= at + cost[j]:
+                    break
+                if b > at:
+                    at = b
+                k += 1
+            line.insert(k, (at, at + cost[j]))
+        start[j], done[j] = at, at + cost[j] + trail[j]
+    return start, done
+
+
+def shake(seq, deps, kids, q, cost, late):
+    none = [0.0] * len(seq)
+    back = pack(seq[::-1], kids, q, cost, late, none)[1]
+    start = pack(sorted(seq, key=lambda i: -back[i]), deps, q, cost, none, late)[0]
+    return sorted(seq, key=lambda i: start[i])
+
+
+def mend(ops, deps, kids):
     n = len(ops)
     rng = np.random.default_rng(SEED)
     ways = [[("vstygx".index(w[0]), w[1]) for w in o["ways"]] for o in ops]
@@ -543,24 +556,37 @@ def mend(ops, deps, kids, seq):
     way = [0] * n
     q, cost = [w[0][0] for w in ways], [w[0][1] for w in ways]
     best = now = None
-    was = ([0.0] * n, [0.0] * n, [-1] * n)
+    seq, was = list(range(n)), ([0.0] * n, [0.0] * n, [-1] * n)
     for turn, (a, b, c, d, e) in enumerate(rng.random((TURNS, 5)).tolist()):
-        new, j, old, p = seq, 0, way[0], 0
-        if turn:
+        new, p, moved = seq, 0, []
+        if turn % SHAKE == 0:
+            new = shake(sorted(seq, key=lambda i: was[1][i]) if turn else seq, deps, kids, q, cost, late)
+        else:
             j = chain[int(a * len(chain))] if b < 0.7 else int(a * n)
-            old, p = way[j], at[j]
+            p = to = at[j]
             if len(ways[j]) > 1 and c < 0.3:
-                way[j] = 1 - old
-                q[j], cost[j] = ways[j][way[j]]
-            if way[j] == old or c < 0.15:
-                lo = max([at[i] + 1 for i in deps[j]] + [0])
-                hi = min([at[i] - 1 for i in kids[j]] + [n - 1])
-                to = min(max(p + int((d - 0.5) * (40 if c < 0.8 else 300)), lo), hi)
-                if to == p and way[j] == old:
+                moved = [(j, way[j], (way[j] + 1 + int(d * (len(ways[j]) - 1))) % len(ways[j]))]
+                if c > 0.2 and len(ways[j]) == 2:
+                    twin = [i for i in seq[max(p - 25, 0):p + 25] if q[i] == ways[j][moved[0][2]][0] and len(ways[i]) == 2]
+                    if twin:
+                        i = twin[int(e * 997) % len(twin)]
+                        moved.append((i, way[i], 1 - way[i]))
+            if not moved or c < 0.1:
+                to = min(max(p + int((d - 0.5) * (FAR[0] if c < 0.8 else FAR[1])), 0), n - 1)
+                if to == p and not moved:
                     continue
-                new = seq[:p] + seq[p + 1:]
-                new.insert(to, j)
-                p = min(p, to)
+                near = deps if to < p else kids
+                tied, go, stay = set(near[j]), [j], []
+                for i in (seq[to:p][::-1] if to < p else seq[p + 1:to + 1]):
+                    if i in tied:
+                        go.append(i)
+                        tied.update(near[i])
+                    else:
+                        stay.append(i)
+                new = seq[:to] + go[::-1] + stay[::-1] + seq[p + 1:] if to < p else seq[:p] + stay + go + seq[to + 1:]
+            p = min([p, to] + [at[i] for i, _o, _w in moved])
+        for i, _o, w in moved:
+            way[i], (q[i], cost[i]) = w, ways[i][w]
         got = times(new, p, was, deps, q, cost, late)
         worth = max(got[1]) + SOON * sum(got[1]) / n
         if now is None or worth <= now + SLACK * (1 - turn / TURNS) * e:
@@ -575,9 +601,9 @@ def mend(ops, deps, kids, seq):
                 chain.append(was[2][chain[-1]])
             if best is None or max(was[1]) < best[1]:
                 best = ([(i, was[0][i]) for i in seq], max(was[1]), list(way))
-        elif way[j] != old:
-            way[j] = old
-            q[j], cost[j] = ways[j][old]
+        else:
+            for i, o, _w in moved:
+                way[i], (q[i], cost[i]) = o, ways[i][o]
     return best
 
 
@@ -590,7 +616,8 @@ def rank_program(g, core, T, topo):
         KEPT["order"] = order(ops)
     deps, seq, _, way = KEPT["order"]
     q = [o["ways"][y][0] for o, y in zip(ops, way)]
-    seq = [j for j, _t in seq if q[j] != "x"]
+    first = [j for j, o in enumerate(ops) if o.get("dma") and not deps[j]]
+    seq = first + [j for j, _t in seq if q[j] != "x" and j not in first]
     at = {j: k for k, j in enumerate(seq)}
     known, before, waits, need = {}, {}, {}, set()
     for j in seq:

@@ -3,19 +3,27 @@ from concourse.mybir import dt, AluOpType as A, ActivationFunctionType as F
 
 C, H, R, P0 = 384, 56, 3, 48
 STEP = [1, 2, 1]
-XO = 8 * H
+WID = [96, 100, 104]
 G0 = [388, 452, 452]
-CH = [[(192, 384), (0, 192)]] * 3 + [[(128, 384), (0, 128)]]
+THIRDS = [(256, 384), (128, 256), (0, 128)]
+CH = [[(192, 384), (0, 192)], THIRDS, THIRDS, THIRDS]
+CUT = 128
 SEND = [[(192, 384), (0, 192)]] * 3
+ALL, OWN = [0, 192, 256], [64, 128, 320]
 BIG = 2.0 ** 80
+TINY = 2.0 ** -10
 U = -2.0 ** 75
 B1K, LIFT = 1024.0, 2.0 ** 24
 MAGIC = 1.5 * 2.0 ** 23
 OFF = 13112.0
 NEW = 50 * 512
-CYC, VFIX, SFIX, WAKE = 1.03, 10.0, 76.0, 185.0
-FLY, RATE, NEARBY, CALL, FIRST, LOAD = 1500.0, 80.0, 1.5, 250.0, 1000.0, 1300.0
-TURNS, SLACK, SOON, SHAKE, FAR, SEED = 280000, 200.0, 0.08, 200, (30, 200), 1
+CASES = [(0.93, 8, 50, 95, 1300, 900, 135, 0.68, 78, 1.25, 1.48, 14), (1.11, 23, 100, 188, 1200, 1300, 125, 0.25, 62, 0.92, 1.75, 30)]
+CYC, VFIX, SFIX, WAKE, FLY, LOAD, RATE, WEIGHT, SAME, PE, GAT, SMIN = np.array(CASES).T
+NEARBY, CALL, FIRST, LRATE = 1.5, 270.0, 1200.0, 310.0
+SPAN, STRIDE, MOVES, SWEEPS, HEAT, REACH, SEED = 64, 24, 500, 85, 110.0, 30, 2
+SORT, AIM, AHEAD = 5, 0.5, 700.0
+PART, AGAIN, TURNS, WARM = 200, 0, 12, 40.0
+SOON, NEAR, BAND, GROW = 0.1, 4.0, 2000.0, 1.12
 
 ARENA = {"f": 0, "h": 0, "i": 0, "w": 0}
 AT = {}
@@ -28,21 +36,21 @@ def _take(ar, name, n):
     ARENA[ar] += (n + al - 1) // al * al
 
 
-for _n, _k in [("k2", 120), ("none", 16), ("r0", 64), ("nv0", 64), ("cum0", 72), ("id", 64), ("cum", 128), ("n1", 64), ("m", 512),
-               ("vr0", 456), ("vr1", 520), ("vr2", 520), ("vr3", 456), ("s", 384), ("ms", 384), ("tb", 392), ("pc", 16),
-               ("j16", 128), ("j8", 64), ("j4", 112), ("m16", 128), ("lift", 384), ("m4", 112), ("sel", 64), ("down", 64),
-               ("up", 64), ("kp", 112), ("k4", 96), ("cj", 72), ("junk", 640), ("mq", 64), ("y", 64), ("yv", 64), ("sg4", 8),
+for _n, _k in [("k2", 120), ("none", 16), ("r0", 64), ("nv0", 64), ("id", 64), ("n1", 64), ("m", 512), ("cum0", 64), ("cum", 128),
+               ("vr1", 520), ("vr2", 520), ("vr3", 456), ("s", 384), ("ms", 384), ("pc", 16),
+               ("j16", 64), ("j8", 64), ("j4", 112), ("lift", 384), ("m4", 112), ("sel", 64), ("down", 64),
+               ("kp", 112), ("k4", 144), ("cj", 72), ("junk", 640), ("mq", 64), ("y", 64), ("yv", 64), ("sg4", 8),
                ("ys", 64), ("wu", 64), ("nq", 128), ("rest", 256), ("oz", 64), ("ed0", 64), ("nv", 192), ("g", 128),
-               ("born", 192), ("r1", 192), ("d", 192), ("ed", 192), ("p", 384), ("fa", 64), ("fx", 384), ("pay", 192), ("v2", 192),
+               ("born", 192), ("r1", 192), ("d", 192), ("ed", 192), ("p", 384), ("fa", 128), ("fx", 384), ("pay", 192), ("v2", 192),
                ("rv", 128), ("vb8", 64), ("tp", 64), ("pd", 64), ("p0", 112), ("pr", 112), ("sr", 112), ("sd", 112), ("lh", 112),
-               ("pk", 112), ("pkr", 384), ("pkd", 384), ("t4o", 96), ("hold", 384), ("dg", 1152), ("t4", 288), ("b1", 144),
-               ("gs", 72), ("xl", 24)]:
+               ("pk", 112), ("pkr", 384), ("pkd", 384), ("t4o", 144), ("hold0", 384), ("hold1", 384),
+               ("hold2", 384), ("dg", 1152), ("t4", 432), ("b1", 144)]:
     _take("f", _n, _k)
 for _t in range(R):
     _take("w", "en%d" % _t, 12)
     _take("w", "el%d" % _t, 96)
-for _n, _k in [("eq", 384), ("pos", 512), ("qr", 384), ("sg", 392), ("cc", 392), ("rs", 392), ("lc", 392), ("li", 392), ("kr", 392),
-               ("step", 384)]:
+for _n, _k in [("eq", 384), ("pos", 512), ("tb", 400), ("vr0", 464), ("sg", 392), ("cc", 392), ("rs", 392), ("lc", 392), ("li", 392),
+               ("kr", 392), ("step", 384)]:
     _take("h", _n, _k)
 for _n, _k in [("pi", 8), ("pj", 8), ("ui", 8), ("xi", 24), ("xk", 24), ("xb", 24), ("ki2", 48)]:
     _take("i", _n, _k)
@@ -54,7 +62,7 @@ SCRATCH = {"f": ("sbuf", [128, ARENA["f"]], F32), "h": ("sbuf", [128, ARENA["h"]
            "i": ("sbuf", [128, ARENA["i"]], "int32"), "w": ("sbuf", [128, ARENA["w"]], "uint16"),
            "zi": ("sbuf", [128, 4], "int32"), "ps": ("psum", [128, 4096], F32),
            "pool3": ("sbuf", [128, 4 * C], BF), "ub": ("sbuf", [128, 512], BF), "vb": ("sbuf", [128, 512], BF),
-           "half": ("sbuf", [128, 528], BF), "eye": ("sbuf", [128, 528], BF), "mt": ("sbuf", [128, 512], BF),
+           "tiny": ("sbuf", [128, 528], BF), "eye": ("sbuf", [128, 528], BF), "mt": ("sbuf", [128, 512], BF),
            "ah": ("sbuf", [128, 448], BF), "aa": ("sbuf", [128, 448], BF), "rl": ("sbuf", [128, 448], F32),
            "dh": ("sbuf", [128, 4 * C + 8], F32), "yb": ("sbuf", [128, C], F32)}
 for _n, _k in [("u", 128), ("u2", 128), ("v", 128), ("w", 512), ("e", 512), ("m", 128), ("x0", C), ("x1", C), ("x2", C), ("x3", C),
@@ -62,9 +70,9 @@ for _n, _k in [("u", 128), ("u2", 128), ("v", 128), ("w", 512), ("e", 512), ("m"
     SCRATCH["q" + _n] = ("sbuf", [128, _k], X4)
     SCRATCH["s" + _n] = ("sbuf", [128, _k], U8)
 for _t in range(R):
-    SCRATCH["pool%d" % _t] = ("sbuf", [128, XO + 4 * (G0[_t] + 2 * H)], BF)
-    SCRATCH["out%d" % _t] = ("sbuf", [128, 28], "uint16")
-    SCRATCH["lin%d" % _t] = ("sbuf", [128, 28], "uint16")
+    SCRATCH["pool%d" % _t] = ("sbuf", [128, 4 * (G0[_t] + 6 * H)], BF)
+    SCRATCH["out%d" % _t] = ("sbuf", [128, WID[_t] // 4], "uint16")
+    SCRATCH["lin%d" % _t] = ("sbuf", [128, WID[_t] // 4], "uint16")
 NSEM, NDMA = 110, 28
 SEMAPHORES = (["c%d" % k for k in range(NSEM)] + ["d%d" % k for k in range(NDMA)] + ["sent"]
               + [n + str(t) for n in ("qa", "qb", "la") for t in range(R)])
@@ -117,9 +125,9 @@ def collect(g, T, topo, core, rank):
         if out[0] == "@":
             return 50 + CYC * 3.8 * size(out)
         if ins and ins[0][0] == "@":
-            return 50 + CYC * 1.56 * size(out)
+            return 50 + CYC * GAT * size(out)
         if all(two(d) for d in [out] + ins):
-            k *= 0.5
+            k *= 0.75 if k == 2 else 0.5
         return VFIX + CYC * max(64.0, size(out) * k)
 
     def tt(out, a, b, op):
@@ -143,11 +151,9 @@ def collect(g, T, topo, core, rank):
         else:
             add([vcp(out, a)], [a], [out])
 
-    def vscan(out, d0, d1, init, op0, op1):
-        return ("v", cyc(out, [d0, d1]), lambda: g.vector.tensor_tensor_scan(ap(out), ap(d0), ap(d1), ap(init), op0, op1))
-
     def scan(out, d0, d1, init, op0, op1):
-        add([vscan(out, d0, d1, init, op0, op1)], [d0, d1, init], [out])
+        add([("v", cyc(out, [d0, d1]), lambda: g.vector.tensor_tensor_scan(ap(out), ap(d0), ap(d1), ap(init), op0, op1))],
+            [d0, d1, init], [out])
 
     def sact(out, a, fn, scale=None, bias=None, acc=None):
         k = {}
@@ -157,7 +163,7 @@ def collect(g, T, topo, core, rank):
             k["bias"] = bias
         if acc is not None:
             k["accum_out"] = acc
-        c = 15 + cyc(out, [a]) if a[0] == "@" else SFIX + CYC * max(64.0, size(out)) + (20 if acc else 0)
+        c = 15 + cyc(out, [a]) if a[0] == "@" else SFIX + CYC * np.maximum(SMIN, size(out)) + (20 if acc else 0)
         return ("s", c, lambda: g.scalar.activation(ap(out), ap(a), fn, **{x: ap(y) for x, y in k.items()}))
 
     def act(out, a, fn, scale=None, bias=None, acc=None):
@@ -196,7 +202,7 @@ def collect(g, T, topo, core, rank):
         return ("v", cyc(out, []), lambda: g.vector.memset(ap(out), float(c)))
 
     def fill(out, c):
-        src = v("half", 0, size(out))
+        src = v("tiny", 0, size(out))
         add([vset(out, c), giota(out, [[0, size(out)]], int(c)), sact(out, src, F.Identity, 0.0, float(c))], [src], [out])
 
     def quant(name, c0, c1, src):
@@ -206,12 +212,12 @@ def collect(g, T, topo, core, rank):
     def mm(bank, st, s0, mv, c0, c1):
         out = v("ps", 512 * bank, 512 * bank + c1 - c0)
         a, b, c, d = v("q" + st, s0, s0 + 128), v("s" + st, s0, s0 + 128), v("q" + mv, c0, c1), v("s" + mv, c0, c1)
-        add([("t", 1.0 * (c1 - c0 + 16), lambda: g.tensor.matmul_mx(ap(out), ap(a), ap(b), ap(c), ap(d), True, True))], [a, b, c, d], [out])
+        add([("t", PE * (c1 - c0 + 16), lambda: g.tensor.matmul_mx(ap(out), ap(a), ap(b), ap(c), ap(d), True, True))], [a, b, c, d], [out])
         return out
 
     def dma(q, out, src, rd, wr, nbytes, last=False):
         e = g.sync if q == "y" else g.scalar
-        add([(q, 60, lambda: e.dma_start(out(), src()))], rd, wr, late=LOAD + nbytes / 200.0, dma=True, last=last)
+        add([(q, 60, lambda: e.dma_start(out(), src()))], rd, wr, late=LOAD + nbytes / LRATE, dma=True, last=last)
 
     def again(out, src):
         pick = lambda: g.affine_select(ap(out), ap(src), [[0, size(out)]], A.is_gt, 0.0, 1, 0)
@@ -220,74 +226,65 @@ def collect(g, T, topo, core, rank):
     def byt(d):
         return ap(d).bitcast(dt.uint8)
 
-    Q16, HH, QQ, T4, S4, SGN, H56, THR, C4, TMP, CE = [v("pc", k, k + 1) for k in range(11)]
+    Q16, HH, QQ, T4, S4, SGN, THR, C4, TMP = [v("pc", k, k + 1) for k in range(9)]
 
     dma("y", lambda: T.zi[:, 0:3], lambda: T.z[:, :], [], [v("zi", 0, 3)], 2e3)
     dma("s", lambda: T.ub[:, :], lambda: T.u[:, :], [], [v("ub")], 131e3)
     for k, (c0, c1) in enumerate(CH[0]):
-        dma("y", lambda c0=c0, c1=c1: T.pool0[:, XO + 4 * c0:XO + 4 * c1], lambda c0=c0, c1=c1: T.x[:, 4 * c0:4 * c1], [],
-            [v("pool0", XO + 4 * c0, XO + 4 * c1)], 131e3 + 1024 * (C - c0))
+        dma("y", lambda c0=c0, c1=c1: T.pool0[:, 4 * c0:4 * c1], lambda c0=c0, c1=c1: T.x[:, 4 * c0:4 * c1], [],
+            [v("pool0", 4 * c0, 4 * c1)], 131e3 + 1024 * (C - c0))
 
-    add([vset(v("half"), 0.5)], [], [v("half")])
+    add([vset(v("tiny"), TINY)], [], [v("tiny")])
     iota(v("pi", 0, 1), [[0, 1]], 0, 1)
-    tb, hf = v("tb", 1, 386), v("half", 0, 385)
-    add([giota(tb, [[1, 385]], 0), vscan(tb, hf, hf, -1.0, A.add, A.add)], [hf], [tb])
-    fill(v("tb", 0, 1), C)
-    iota(v("j16", 0, 128), [[0, 8], [1, 16]], 0)
+    scan(v("tb", 0, C + 1), v("tiny", 0, C + 1), v("tiny", 0, C + 1), -193.0 / 512, A.add, A.add)
+    iota(v("j16", 0, 64), [[0, 4], [1, 16]], 0)
     iota(v("j8", 0, 64), [[0, 8], [1, 8]], 0)
     iota(v("ui", 0, 8), [[16, 8]], 0)
     for k, (sh, msk) in enumerate([(0, 15), (0, 1), (1, 7), (0, 3), (2, 3)]):
         ts(v("pj", k, k + 1), v("pi", 0, 1), sh, A.logical_shift_right, msk, A.bitwise_and)
     cp(v("pc", 0, 5), v("pj", 0, 5))
     lin(SGN, HH, -2.0, 1.0)
-    lin(H56, HH, float(H))
     lin(THR, HH, BIG, BIG / 2)
-    lin(TMP, S4, 2 * B1K, -B1K)
+    lin(TMP, S4, 2 * B1K, 8 * B1K)
     ts(C4, TMP, 2.0, A.mult, T4, A.add)
-    lin(C4, C4, None, 18 * B1K)
-    lin(CE, Q16, 2 * B1K, 32 * B1K)
     fill(("f", AT["none"][1], AT["m"][1], 1), 0)
-    fill(("f", AT["m"][1] + C, AT["vr0"][1] + 400, 1), 0)
+    fill(v("m", C, 512), 0)
+    fill(v("vr0", 16, 416), 0)
+    fill(v("cum", 0, 128, 64), 1)
     for t in (1, 2, 3):
         fill(v("vr%d" % t, 8, 400), 0)
     fill(v("fx", 0, 384, 2), 0)
-    fill(v("t4", 2, 288, 4), 0)
+    fill(v("t4", 2, 432, 6), 0)
     fill(v("dh", 4 * C, 4 * C + 8), 0)
     for t in range(R):
-        fill(v("pool%d" % t, XO + 4 * C, XO + 4 * C + 16), 0)
-    fill(v("mt", 448, 512), 0)
+        fill(v("pool%d" % t, 4 * C, 4 * C + 16), 0)
+    fill(v("mt", 4 * WID[0], 512), 0)
     fill(v("pos", C, 512), 0)
     fill(v("k2", 0, 66), 513)
     fill(v("k2", 66 + P0, 67 + P0), 2 * (P0 + 2))
     fill(v("born", 128, 192), 1)
-    fill(v("rest", 192, 193), 0)
-    fill(v("pr", 2 * P0, 112 + 112), C)
-    add([vset(v("step", 0, C), U), sact(v("step", 0, C), v("half", 0, C), F.Identity, 2 * U)], [v("half", 0, C)], [v("step", 0, C)])
-    iota(v("d", 0, 192), [[0, 3], [-2 ** 15, 64]], 1 - 2 ** 15)
+    fill(v("rest", 192, 193), 1)
+    fill(v("pr", 2 * P0, 112), C)
+    add([vset(v("step", 0, CUT), U), sact(v("step", 0, CUT), v("tiny", 0, CUT), F.Identity, U / TINY)], [v("tiny", 0, CUT)], [v("step", 0, CUT)])
+    iota(v("d", 0, 192), [[0, 3], [-2 ** 15, 64]], 2 - 2 ** 15)
     iota(v("n1", P0 + 2, P0 + 6), [[-2, 2], [-H, 2]], 2 - G0[1])
     iota(v("id", P0, P0 + 6), [[512, 3], [H, 2]], NEW - 512 + G0[0] - 2)
     iota(v("id", P0 + 6, 64), [[1, 10]], 0)
     ts(v("sel", 0, 64), v("j8", 0, 64), QQ, A.not_equal, BIG * 2.0 ** 13, A.mult)
     ts(v("down", 0, 64), v("j8", 0, 64), 0.0, A.is_equal, -BIG * 2.0 ** 15, A.mult)
-    lin(v("up", 0, 64), v("down", 0, 64), -1.0)
-    ts(v("m16", 0, 128), v("j16", 0, 128), Q16, A.subtract, 4 * B1K, A.mult)
-    ts(v("m16", 0, 128), v("m16", 0, 128), 2 * B1K, A.add, 2 * B1K, A.min)
-    lin(v("m16", 15, 128, 16), v("m16", 15, 128, 16), None, -64 * B1K)
     ts(v("lift", 0, 64), v("j16", 0, 64), Q16, A.is_equal, LIFT, A.mult)
     ts(v("lift", 64, 128), v("j16", 0, 64), Q16, A.is_gt)
     tt(v("lift", 0, 64), v("lift", 0, 64), v("lift", 64, 128), A.add)
     lin(v("lift", 15, 64, 16), v("lift", 15, 64, 16), 1.0 / (U * LIFT))
-    for a, b in ((64, 128), (128, 256), (256, 384)):
-        again(v("lift", a, b), v("lift", 0, b - a))
-    lin(v("qr", 0, C), v("tb", 1, C + 1), -1.0 / 512, 0.375)
-    add([("g", 170 + 2 * CYC * 516, lambda: g.affine_select(T.eye[:, 0:516], T.half[:, 0:516], [[1, 516]], A.is_equal, 0.0, -3, -4))],
-        [v("half", 0, 516)], [v("eye", 0, 516)])
+    again(v("lift", 64, 128), v("lift", 0, 64))
+    add([("g", 170 + 2 * CYC * 516, lambda: g.affine_select(T.eye[:, 0:516], T.tiny[:, 0:516], [[1, 516]], A.is_equal, 0.0, -3, -4))],
+        [v("tiny", 0, 516)], [v("eye", 0, 516)])
     iota(v("li", 0, 392), [[-8, 7], [1, H]], 0)
     fill(v("kr", 0, 392), 64)
     fill(v("kr", 0, 392, H), 0)
-    iota(v("j4", 0, 112), [[0, 28], [2048, 4]], 0)
+    iota(v("j4", 0, 112), [[0, 28], [2048, 4]], 9 * 1024)
     iota(v("kp", 0, 112), [[0, H], [1024, 2]], 0)
-    iota(v("k4", 0, 96), [[0, 24], [1024, 4]], 0)
+    iota(v("k4", 0, 144), [[0, 24], [1024, 6]], 0)
     ts(v("lc", 0, 392), v("li", 0, 392), QQ, A.is_lt, 2.0 ** -120, A.mult)
     ts(v("m4", 0, 112), v("j4", 0, 112), TMP, A.subtract, B1K, A.min)
     lin(v("m4", 3, 112, 4), v("m4", 3, 112, 4), None, -8 * B1K)
@@ -301,22 +298,20 @@ def collect(g, T, topo, core, rank):
     add([("s", 65 + 200 * CYC, lambda: g.scalar.activation(T.su2[:, 0:128], T.su[:, 0:128].indirect(ap(v("uo", 0, 8))), F.Copy))],
         [v("su"), v("uo", 0, 8)], [v("su2")])
 
-    def marks(t, e, nv):
-        a = 128 * t
-        act(v("p", a, a + 64), nv, F.Relu, -BIG, THR)
-        scan(v("p", a + 64, a + 128), v("p", a, a + 64), v("sel", 0, 64), BIG * 2.0 ** 13, A.min, A.max)
-        act(v("fa", 0, 64), e, F.Relu, -2.0, 2.0 * C - 1)
-        lin(v("fx", a + 1, a + 128, 2), v("fa", 0, 64), -1.0, 2.0 * C)
+    def marks(t):
+        scan(v("p", OWN[t], OWN[t] + 64), v("p", ALL[t], ALL[t] + 64), v("sel", 0, 64), BIG * 2.0 ** 13, A.min, A.max)
 
     cp(v("zu", 0, 3), v("zi", 0, 3))
-    lin(v("r0", 0, P0), ind(v("tb", 0, 386), v("zu", 0, 3)))
+    lin(v("r0", 0, P0), ind(v("tb", 0, C + 1), v("zu", 0, 3)), 512.0, 191.0)
     lin(v("nv0", 0, P0), v("r0", 0, P0), None, 1.0)
-    scan(v("cum0", 1, 65), v("r0", 0, 64), v("born", 128, 192), 0.0, A.add, A.add)
-    scan(v("ed0", 0, 64), v("cum0", 0, 64), v("m16", 0, 64), -B1K, A.max, A.add)
+    scan(v("cum0", 0, 64), v("r0", -1, 63), v("born", 128, 192), 0.0, A.add, A.add)
+    scan(v("ed0", 0, 64), v("cum0", 0, 64), v("lift", 0, 64), 0.0, A.max, A.mult)
     for k in range(2):
-        ts(v("en0", 4 * k, 4 * k + 4), v("ed0", 15, 64, 16), CE, A.add)
-    marks(0, v("cum0", 0, 64), v("nv0", 0, 64))
-    cp(ind(v("vr0", 8, 456), v("en0", 0, 4)), v("step", 0, 64))
+        ts(v("en0", 4 * k, 4 * k + 4), v("ed0", 15, 64, 16), U, A.mult, -1.0, A.add)
+    act(v("p", 0, 64), v("nv0", 0, 64), F.Relu, -BIG, THR)
+    marks(0)
+    lin(v("fx", 1, 128, 2), v("cum0", 0, 64), 2.0, -1.0)
+    cp(ind(v("vr0", 16, 464), v("en0", 0, 3)), v("step", 0, P0))
 
     k2 = lambda a, b: v("k2", 66 + a, 66 + b)
     lin(k2(0, P0), v("r0", 0, P0), 2.0, 2.0)
@@ -324,7 +319,7 @@ def collect(g, T, topo, core, rank):
     for k, (more, least) in enumerate([(58, 5.0), (58, 7.0), (66, 9.0), (66, 11.0)]):
         act(v("junk", 128 * k + 128, 128 * k + 178 + more), k2(-more, P0 + 2), F.Sign, None, -least, acc=k2(P0 + 2 + k, P0 + 3 + k))
     scan(v("id", 1, P0), v("r0", 0, P0 - 1), v("k2", 0, P0 - 1), 0.0, A.add, A.add)
-    lin(v("mq", 0, 64), k2(0, 64), 2.0 ** 14, OFF)
+    lin(v("mq", 0, 64), k2(0, 64), 2.0 ** 14, OFF - 1)
     scan(v("y", 0, 64), v("id", 0, 64), v("mq", 0, 64), -1.0, A.max, A.subtract)
     scan(v("yv", 0, 64), v("y", 0, 64), v("lift", 0, 64), 0.0, A.min, A.mult)
     for k in range(4):
@@ -338,30 +333,35 @@ def collect(g, T, topo, core, rank):
     cp(ind(v("nv", 0, 64), v("rk", 0, 4)), v("n1", 0, 64))
     relu(v("r1", 0, 64), v("nv", 0, 64), None, -1.0)
     ts(v("born", 0, 64), v("nv", 0, 64), -100.0, A.is_gt)
-    lin(v("g", 0, 64), v("nv", 0, 64), -1.0)
-    scan(v("cum", 1, 64), v("r1", 0, 63), v("born", 0, 63), 0.0, A.add, A.add)
+    lin(v("g", 0, 64), v("nv", 0, 64), -1.0, 1.0)
+    scan(v("cum", 1, 64), v("r1", 0, 63), v("born", 0, 63), 1.0, A.add, A.add)
     lin(v("nq", 64, 128), v("wu", 0, 64), None, -MAGIC - 4)
     lin(v("nv", 128, 192), v("wu", 0, 64), None, -MAGIC - 6)
     relu(v("g", 64, 128), v("rest", 0, 64), None, OFF - NEW - 512 + G0[1] - G0[0])
     scan(v("nv", 64, 128, -1), v("nq", 64, 128, -1), v("g", 64, 128, -1), -1024.0, A.max, A.subtract)
     relu(v("born", 64, 128), v("g", 64, 128), -1.0, 1.0)
     relu(v("r1", 64, 192), v("nv", 64, 192), None, -1.0)
-    scan(v("cum", 65, 128), v("r1", 64, 127), v("born", 64, 127), 0.0, A.add, A.add)
-    scan(v("rest", 193, 256), v("r1", 128, 191), v("born", 128, 191), 0.0, A.add, A.add)
+    scan(v("cum", 65, 128), v("r1", 64, 127), v("born", 64, 127), 1.0, A.add, A.add)
+    scan(v("rest", 193, 256), v("r1", 128, 191), v("born", 128, 191), 1.0, A.add, A.add)
     for t, a, b in ((1, 0, 64), (2, 64, 192)):
         scan(v("rest", 64 + a, 128 + a, -1), v("cum", a, a + 64, -1), v("g", a, a + 64, -1), 2048.0, A.min, A.max)
-        scan(v("ed", a, b), v("rest", 64 + a, 64 + b), v("m16", 0, b - a), -B1K, A.max, A.add)
-        ts(v("en%d" % t, 0, 4), v("ed", a + 15, a + 64, 16), CE, A.add)
-        ts(v("en%d" % t, 4, 4 + (b - a) // 16), v("ed", a + 15, b, 16), CE, A.add)
-        marks(t, v("rest", 64 + a, 128 + a), v("nv", a, a + 64))
+        scan(v("ed", a, b), v("rest", 64 + a, 64 + b), v("lift", 0, b - a), 0.0, A.max, A.mult)
+        ts(v("en%d" % t, 0, 4), v("ed", a + 15, a + 64, 16), U, A.mult, -1.0, A.add)
+        ts(v("en%d" % t, 4, 4 + (b - a) // 16), v("ed", a + 15, b, 16), U, A.mult, -1.0, A.add)
         scan(v("pay", a, b), v("rest", a, b), v("d", a, b), 2.0 ** 20, A.min, A.subtract)
         lin(v("v2", a, b), v("pay", a, b), U)
+    act(v("p", ALL[1], ALL[1] + 128), v("nv", 0, 128), F.Relu, -BIG, THR)
+    marks(1)
+    marks(2)
+    act(v("fa", 0, 128), v("rest", 64, 192), F.Relu, -2.0, 2.0 * C + 1)
+    lin(v("fx", 129, 384, 2), v("fa", 0, 128), -1.0, 2.0 * C)
     for t in range(R):
-        a, b, vr = 24 * t, 24 * t + 24, "vr%d" % (t + 1)
+        a, b, vr, hold = 24 * t, 24 * t + 24, "vr%d" % (t + 1), "hold%d" % t
         cp(ind(v(vr, 8, 520 if t < 2 else 456), v("en%d" % (t + 1), 0, 4) if t < 2 else v("en2", 8, 12)), v("v2", 64 * t, 64 * t + 64))
-        scan(v("hold", 0, C), v(vr, 8, 8 + C), v("step", 0, C), 0.0, A.min, A.add)
-        scan(v("dg", C * t, C * t + C), v("hold", 0, C), v("lift", 0, C), 0.0, A.min, A.mult)
-        got, base = v("dg", 16 * a + 15, 16 * b, 16), v("t4", 4 * a, 4 * b, 4)
+        for c in range(0, C, CUT):
+            scan(v(hold, c, c + CUT), v(vr, 8 + c, 8 + c + CUT), v("step", 0, CUT), v(hold, c - 1, c) if c else 0.0, A.min, A.add)
+            scan(v("dg", C * t + c, C * t + c + CUT), v(hold, c, c + CUT), v("lift", 0, CUT), 0.0, A.min, A.mult)
+        got, base = v("dg", 16 * a + 15, 16 * b, 16), v("t4", 6 * a + 1, 6 * b, 6)
         if t:
             ts(v("kl", a, b), got, 2.0 ** -14, A.mult, -1.0, A.add)
             lin(v("cj", a, b), got, 2.0 ** -15, MAGIC)
@@ -375,7 +375,8 @@ def collect(g, T, topo, core, rank):
             cp(base, v("xb", a, b))
         lin(v("b1", 2 * a, 2 * b, 2), base, B1K, B1K - 1)
         lin(v("b1", 2 * a + 1, 2 * b, 2), base, None, 1.0)
-        ts(v("gs", a, b), base, float(C), A.is_ge, -float(G0[t] + 2 * H), A.mult)
+        ts(v("t4", 6 * a + 4, 6 * b, 6), base, float(C), A.is_ge, 2.0 * H, A.mult)
+        again(v("t4", 6 * a + 5, 6 * b, 6), v("t4", 6 * a + 4, 6 * b, 6))
     relu(v("oz", 0, H), v("nv", 128, 128 + H), None, 0.0)
     dma("y", lambda: T.oz[:, :], lambda: T.f[0:128:16, AT["oz"][1]:AT["oz"][1] + H], [v("oz", 0, H)], [], 2e3, last=True)
 
@@ -394,23 +395,23 @@ def collect(g, T, topo, core, rank):
     for t in range(R):
         pool, nxt, xq, lq = "pool%d" % t, "pool%d" % (t + 1), "x%d" % t, "l%d" % t
         w = lambda name, a=0, b=64, s=1: v(name + str(t), a, b, s)
-        ns = 7 if t else 6
+        ns, n, at = 7 if t else 6, WID[t], 9 if t else 17
         peer = T.cores[rank ^ STEP[t]]
         for k, (c0, c1) in enumerate(CH[t]):
-            quant(xq, c0, c1, v(pool, XO + 4 * c0, XO + 4 * c1))
+            quant(xq, c0, c1, v(pool, 4 * c0, 4 * c1))
             o = mm(k, "u2", 0, xq, c0, c1)
             lin(v("s", c0, c1), o, SGN)
-            scan(v("m", c0, c1, -1), w("vr", 9 + c0, 9 + c1, -1), v("s", c0, c1, -1), v("m", c1, c1 + 1) if k else -BIG, A.add, A.max)
+            scan(v("m", c0, c1, -1), w("vr", at + c0, at + c1, -1), v("s", c0, c1, -1), v("m", c1, c1 + 1) if k else -BIG, A.add, A.max)
             lin(v("ms", c0, c1), v("m", c0, c1), SGN)
             tt(v("eq", c0, c1), o, v("ms", c0, c1), A.is_equal)
-            scan(v("pos", c0, c1, -1), v("eq", c0, c1, -1), v("qr", c0, c1, -1), v("pos", c1, c1 + 1), A.add, A.min)
+            scan(v("pos", c0, c1, -1), v("eq", c0, c1, -1), v("tb", C + 1 - c1, C + 1 - c0), v("pos", c1, c1 + 1), A.add, A.min)
         for k, (c0, c1) in enumerate(SEND[t]):
             sem, far = "q%s%d" % ("ab"[k], t), 640 * (C - c0) - 300 * k * (C - c1)
             k1, o1 = send(v("q" + xq, c0, c1), v("q" + lq, c0, c1), sem, peer, True, far)
             k3, o2 = send(v("s" + xq, c0, c1), v("s" + lq, c0, c1), sem, peer, False, far)
             add([("x", 0, None)], [], [v("q" + lq, c0, c1), v("s" + lq, c0, c1)], after=[o1, o2], sem=sem, cnt=k1 + k3)
             for b in range(4):
-                lin(v("dh", 4 * c0 + b, 4 * c1, 4), mm(3 + b, "e", 128 * b, lq, c0, c1))
+                lin(v("dh", 4 * c0 + b, 4 * c1, 4), mm(3 + b, "e", 128 * b, lq, c0, c1), 0.5 / TINY)
         if t == 0:
             landed = [v("ql0", *SEND[0][0])]
             dma("y", lambda: byt(v("qw")), lambda: T.wc[:, :], landed, [v("qw")], 262e3)
@@ -418,50 +419,55 @@ def collect(g, T, topo, core, rank):
         if t == 1:
             dma("y", lambda: T.vb[:, :], lambda: T.v[:, :], [v("ql1")], [v("vb")], 131e3)
             quant("v", 0, 128, v("vb"))
+        own, row = OWN[t] - 128 * t, ALL[t] - 128 * t
         tt(v("rv", 0, 128), ind(v("m", 0, 512), w("en", 0, 8)), v("p", 128 * t, 128 * t + 128), A.subtract)
-        scan(v("vb8", 0, H), v("down", 0, H), v("rv", 64, 64 + H), 0.0, A.add, A.max)
+        scan(v("vb8", 0, H), v("down", 0, H), v("rv", own, own + H), 0.0, A.add, A.max)
         for k in range(ns):
-            o, a, b = v("sg", H * k, H * k + H), v("rv", 0, H), v("vb8", 8 * k + 7, 8 * k + 8)
+            o, a, b = v("sg", H * k, H * k + H), v("rv", row, row + H), v("vb8", 8 * k + 7, 8 * k + 8)
             add([sact(o, a, F.Sign, -1.0, b), vts(o, a, b, A.subtract, -1.0, A.mult)], [a, b], [o])
-        tt(v("tp", 0, 64), ind(v("pos", 0, 512), w("en", 0, 4)), v("p", 128 * t + 64, 128 * t + 128), A.add)
-        scan(v("pd", 0, H), v("up", 0, H), v("tp", 0, H), 0.0, A.add, A.min)
-        ts(v("pu", 0, ns), v("pd", 7, 8 * ns, 8), -512.0, A.mult, 193.0, A.add)
-        lin(v("p0", 0, 16 * ns), ind(v("tb", 0, 386), v("pu", 0, ns)))
+        tt(v("tp", 0, 64), ind(v("pos", 0, 512), w("en", 0, 4)), v("p", OWN[t], OWN[t] + 64), A.subtract)
+        scan(v("pd", 0, H), v("down", 0, H), v("tp", 0, H), 0.0, A.add, A.max)
+        ts(v("pu", 0, ns), v("pd", 7, 8 * ns, 8), 512.0, A.mult, 192.0, A.add)
+        lin(v("p0", 0, 16 * ns), ind(v("tb", 0, C + 1), v("pu", 0, ns)), -512.0, 192.0)
         scan(v("pr", 0, 16 * ns), v("fx", 128 * t, 128 * t + 16 * ns), v("p0", 0, 16 * ns), 0.0, A.subtract, A.max)
-        tt(v("cc", 0, H * ns), v("sg", 0, H * ns), v("lc", 0, H * ns), A.is_lt)
-        scan(v("rs", 0, H * ns), v("kr", 0, H * ns), v("cc", 0, H * ns), 0.0, A.min, A.add)
-        ts(v("ru", 0, ns), v("rs", H - 1, H * ns, H), H56, A.add)
+        for a, b in ((0, 2 * H), (2 * H, 4 * H), (4 * H, H * ns)):
+            tt(v("cc", a, b), v("sg", a, b), v("lc", a, b), A.is_lt)
+            scan(v("rs", a, b), v("kr", a, b), v("cc", a, b), 0.0, A.min, A.add)
+        ts(v("ru", 0, ns), v("rs", H - 1, H * ns, H), 2.0, A.mult, HH, A.add)
         cp(ind(v("sr", 0, 112), v("ru", 0, ns)), v("pr", 0, 16 * ns))
-        scan(v("sd", 0, 112), v("sr", 0, 112), v("m4", 0, 112), -B1K, A.max, A.add)
+        scan(v("sd", 0, n), v("sr", 0, n), v("m4", 0, n), -B1K, A.max, A.add)
         lst, lin_ = v("out%d" % t), v("lin%d" % t)
-        ts(lst, v("sd", 3, 112, 4), 4.0, A.mult, C4, A.add)
-        k1, o1 = send(lst, lin_, "la%d" % t, peer, False, 7168)
+        ts(lst, v("sd", 3, n, 4), 4.0, A.mult, C4, A.add)
+        k1, o1 = send(lst, lin_, "la%d" % t, peer, False, 64 * n)
         add([("x", 0, None)], [], [lin_], after=[o1], sem="la%d" % t, cnt=k1)
-        for k in range(2):
-            lin(v("aa", 224 * k, 224 * k + 224), ind(v(pool, XO, XO + 4 * C + 8), v(lst[0], 14 * k, 14 * k + 14)))
-        lin(v("ah"), v("aa"), 0.5)
-        tt(v("mt", 0, 448), ind(v("dh"), lin_), v("ah"), A.add)
+        for a, b in ((0, 12), (12, n // 4)):
+            lin(v("aa", 16 * a, 16 * b), ind(v(pool, 0, 4 * C + 8), v(lst[0], a, b)))
+        lin(v("ah", 0, 4 * n), v("aa", 0, 4 * n), 0.5)
+        tt(v("mt", 0, 4 * n), ind(v("dh"), lin_), v("ah", 0, 4 * n), A.add)
         quant("m", 0, 128, v("mt"))
         for b in range(4):
             o = mm((7, 0, 1, 2)[b], "w", 128 * b, "m", 0, 128)
-            relu(v("rl", b, 448, 4), (o[0], o[1], o[1] + 112, 1), 0.03125)
-            tt(v(pool, b, XO, 4) if b < 2 else v(pool, XO + 4 * G0[t] + b, None, 4), v("rl", b, 448, 4), v("aa", b, 448, 4), A.add)
+            relu(v("rl", b, 4 * n, 4), (o[0], o[1], o[1] + n, 1), 0.03125)
+            for h in range(2):
+                to = 4 * (G0[t] + 2 * H * min(b, 2) + H * h) + b
+                tt(v(pool, to, to + 2 * n, 4), v("rl", 4 * h + b, 4 * n, 8), v("aa", 4 * h + b, 4 * n, 8), A.add)
         scan(v("lh", 0, 111, -2), v("pr", 0, 111, -2), v("pr", 1, 112, -2), 512.0, A.min, A.min)
         scan(v("lh", 1, 112, -2), v("pr", 0, 111, -2), v("pr", 1, 112, -2), 512.0, A.min, A.max)
         scan(v("pk", 0, 112), v("kp", 0, 112), v("lh", 0, 112), 0.0, A.mult, A.add)
-        lin(v("pkr", 0, C), ind(v("pk", 0, 112), v("kl", 24 * t, 24 * t + 24)), U)
-        scan(v("pkd", 0, C), v("pkr", 0, C), v("lift", 0, C), 0.0, A.min, A.mult)
+        for c in range(0, C, CUT):
+            lin(v("pkr", c, c + CUT), ind(v("pk", 0, 112), v("kl", 24 * t + c // 16, 24 * t + (c + CUT) // 16)), U)
+            scan(v("pkd", c, c + CUT), v("pkr", c, c + CUT), v("lift", 0, CUT), 0.0, A.min, A.mult)
         ts(v("ki2", 0, 48, 2), v("pkd", 15, C, 16), -1.0, A.add)
         ts(v("ki2", 1, 48, 2), v("ki2", 0, 48, 2), 1023, A.bitwise_and)
-        tt(v("t4", 96 * t + 1, 96 * t + 96, 2), v("ki2", 0, 48), v("b1", 48 * t, 48 * t + 48), A.is_lt)
-        scan(v("t4o", 0, 96), v("k4", 0, 96), v("t4", 96 * t, 96 * t + 96), 0.0, A.min, A.add)
-        tt(v("xl", 0, 24), v("t4o", 3, 96, 4), v("gs", 24 * t, 24 * t + 24), A.add)
+        tt(v("t4", 144 * t, 144 * t + 144, 3), v("ki2", 0, 48), v("b1", 48 * t, 48 * t + 48), A.is_lt)
+        scan(v("t4o", 0, 144), v("k4", 0, 144), v("t4", 144 * t, 144 * t + 144), 0.0, A.min, A.add)
         for b in range(4):
-            ts(w("el", 24 * b, 24 * b + 24), v("xl", 0, 24) if b < 2 else v("t4o", 3, 96, 4), 4.0, A.mult, float(b + (XO if b < 2 else 0)), A.add)
+            ts(w("el", 24 * b, 24 * b + 24), v("t4o", 3 + min(b, 2), 144, 6), 4.0, A.mult, float(b), A.add)
+            ops[-1]["early"] = True
         for k, (c0, c1) in enumerate(CH[t + 1]):
             for b in range(4):
-                at, win = XO if t + 1 < R else 0, v(pool, 0, XO + 4 * C) if b < 2 else v(pool, XO)
-                lin(v(nxt, at + 4 * c0 + b, at + 4 * c1, 4), ind(win, w("el", 24 * b + c0 // 16, 24 * b + c1 // 16)))
+                win = v(pool, 0, 4 * (G0[t] + 2 * H * (min(b, 2) + 1)))
+                lin(v(nxt, 4 * c0 + b, 4 * c1, 4), ind(win, w("el", 24 * b + c0 // 16, 24 * b + c1 // 16)))
 
     for k, (c0, c1) in enumerate(CH[R]):
         quant("x3", c0, c1, v("pool3", 4 * c0, 4 * c1))
@@ -504,30 +510,10 @@ def order(ops):
     return (deps,) + mend(ops, [sorted(d) for d in deps], kids)
 
 
-def times(seq, p, was, deps, q, cost, late):
-    start, done, why = list(was[0]), list(was[1]), list(was[2])
-    free, last = [0.0] * 6, [-1] * 6
-    for j in seq[max(p - 60, 0):p]:
-        free[q[j]], last[q[j]] = start[j] + cost[j], j
-    free[5], last[5] = 0.0, -1
-    for j in seq[p:]:
-        k = q[j]
-        at, by = free[k], last[k]
-        for i in deps[j]:
-            if done[i] > at:
-                at, by = done[i], i
-        start[j], why[j] = at, by
-        at += cost[j]
-        done[j] = at + late[j]
-        if k < 5:
-            free[k], last[k] = at, j
-    return start, done, why
-
-
-def pack(seq, before, q, cost, lead, trail):
+def pack(seq, before, q, cost, lead, trail, same):
     done, start, busy = {}, {}, [[] for _ in range(6)]
     for j in seq:
-        at = max([done[i] for i in before[j]] + [0.0]) + lead[j]
+        at = max([done[i] + same * (q[i] == q[j] < 2) for i in before[j]] + [0.0]) + lead[j]
         line, k = busy[q[j]], 0
         if q[j] < 5:
             for a, b in line:
@@ -541,69 +527,233 @@ def pack(seq, before, q, cost, lead, trail):
     return start, done
 
 
-def shake(seq, deps, kids, q, cost, late):
+def shake(seq, deps, kids, q, cost, late, same):
     none = [0.0] * len(seq)
-    back = pack(seq[::-1], kids, q, cost, late, none)[1]
-    start = pack(sorted(seq, key=lambda i: -back[i]), deps, q, cost, none, late)[0]
+    back = pack(seq[::-1], kids, q, cost, late, none, same)[1]
+    start = pack(sorted(seq, key=lambda i: -back[i]), deps, q, cost, none, late, same)[0]
     return sorted(seq, key=lambda i: start[i])
 
 
+def heads(seq, deps, q, cost, late, same):
+    start, done, free = [0.0] * len(seq), [0.0] * len(seq), [0.0] * 6
+    for j in seq:
+        start[j] = max([free[q[j]]] + [done[i] + same * (q[i] == q[j] < 2) for i in deps[j]])
+        done[j] = start[j] + cost[j] + late[j]
+        if q[j] < 5:
+            free[q[j]] = start[j] + cost[j]
+    return start, done
+
+
+def tails(seq, kids, q, cost, late, same):
+    rest, nxt = [0.0] * len(seq), [0.0] * 6
+    for j in seq[::-1]:
+        rest[j] = cost[j] + max(late[j] + max([rest[i] + same * (q[i] == q[j] < 2) for i in kids[j]] + [0.0]), nxt[q[j]])
+        if q[j] < 5:
+            nxt[q[j]] = rest[j]
+    return rest
+
+
+def stretch(win, cases, pure, ways, way, deps, kids, rnd, heat):
+    m = len(win)
+    loc = {j: k for k, j in enumerate(win)}
+    dp = [[loc[i] for i in deps[j] if i in loc] for j in win]
+    kd = [[loc[i] for i in kids[j] if i in loc] for j in win]
+    wy = [ways[j] for j in win]
+    w = [way[j] for j in win]
+    q = [wy[k][w[k]] for k in range(m)]
+    cs = []
+    for wt, cost, late, free, done, rest, after, same in cases:
+        far = lambda t, near: [[max([t[i] + same * (ways[i][way[i]] == x < 2) for i in near[j] if i not in loc] + [0.0]) for x in ways[j]]
+                               for j in win]
+        each = [[cost[j] for j in win], far(done, deps), far(rest, kids)]
+        c, ready, out = [[e[k][w[k]] for k in range(m)] for e in each]
+        cs.append([wt, each, c, [late[j] for j in win], free, after, ready, out, [1e9] * m, same])
+
+    def put(i, y):
+        w[i], q[i] = y, wy[i][y]
+        for x in cs:
+            x[2][i], x[6][i], x[7][i] = x[1][0][i][y], x[1][1][i][y], x[1][2][i][y]
+
+    def run(seq, p, dns, sts):
+        got = 0.0
+        for (wt, _c, c, lt, _f, after, ready, out, due, same), dn, st in zip(cs, dns, sts):
+            free, top, tot = list(st[0]), st[1], st[2]
+            for k in seq[p:]:
+                x = q[k]
+                at = free[x]
+                if ready[k] > at:
+                    at = ready[k]
+                for i in dp[k]:
+                    t = dn[i] + same if q[i] == x < 2 else dn[i]
+                    if t > at:
+                        at = t
+                at += c[k]
+                if x < 5:
+                    free[x] = at
+                at += lt[k]
+                dn[k] = at
+                tot += at
+                if at > due[k]:
+                    tot += NEAR * (at - due[k])
+                at += out[k]
+                if at > top:
+                    top = at
+            for x in range(5):
+                if free[x] + after[x] > top:
+                    top = free[x] + after[x]
+            got += wt * (top + SOON * tot / m)
+        return got
+
+    def tight(seq, dn, x):
+        c, lt, after, out = x[2], x[3], x[5], x[7]
+        prev, last = {}, {}
+        for k in seq:
+            prev[k], last[q[k]] = last.get(q[k]), k
+        k = max(seq, key=lambda i: max(dn[i] + out[i], dn[i] - lt[i] + after[q[i]] if q[i] < 5 and last[q[i]] == i else 0.0))
+        got = []
+        while k is not None:
+            got.append(k)
+            s, i = dn[k] - lt[k] - c[k] - 1e-6, prev[k]
+            if q[k] < 5 and i is not None and dn[i] - lt[i] >= s:
+                got += [k, i]
+                k = i
+            else:
+                k = next((i for i in dp[k] if dn[i] + x[9] * (q[i] == q[k] < 2) >= s), None)
+        return got
+
+    def states(seq, dns, p, was):
+        rows = []
+        for (_w, _c, c, lt, _f, _a, _r, out, due, _s), dn, st in zip(cs, dns, was[p]):
+            sts, free, top, tot = [], list(st[0]), st[1], st[2]
+            for k in seq[p:]:
+                sts.append((tuple(free), top, tot))
+                if q[k] < 5:
+                    free[q[k]] = dn[k] - lt[k]
+                at = dn[k]
+                tot += at
+                if at > due[k]:
+                    tot += NEAR * (at - due[k])
+                if at + out[k] > top:
+                    top = at + out[k]
+            rows.append(sts)
+        return was[:p] + list(zip(*rows))
+
+    seq, dns, null = list(range(m)), [[0.0] * m for _ in cs], [(x[4], 0.0, 0.0) for x in cs]
+    run(seq, 0, dns, null)
+    for x, dn, pu in zip(cs, dns, pure):
+        bar = max(dn[k] + x[7][k] for k in seq) - BAND
+        x[8][:] = [bar - pu[j] for j in win]
+    now = run(seq, 0, dns, null)
+    c0, l0 = cs[0][2], cs[0][3]
+    seq.sort(key=lambda k: dns[0][k] - l0[k] - c0[k])
+    sts, taken, hot = states(seq, dns, 0, [null]), 0, tight(seq, dns[0], cs[0])
+    for a, b, d, e in rnd:
+        j = hot[int(a * len(hot))] if a * 53 % 1 < AIM else seq[int(a * m)]
+        p = to = seq.index(j)
+        moved, new = [], seq
+        if len(wy[j]) > 1 and b < 0.35:
+            moved = [(j, w[j], (w[j] + 1 + int(d * (len(wy[j]) - 1))) % len(wy[j]))]
+            if b > 0.22:
+                twin = [i for i in seq[max(p - 12, 0):p + 12] if q[i] == wy[j][moved[0][2]] and q[j] in wy[i]]
+                if twin:
+                    i = twin[int(e * 997) % len(twin)]
+                    moved.append((i, w[i], wy[i].index(q[j])))
+                    p = min(p, seq.index(i))
+        if not moved or b < 0.1:
+            s = to
+            to = min(max(s + int((d * 7 % 1 - 0.5) * (REACH if e * 31 % 1 < 0.8 else 2 * m)), 0), m - 1)
+            if to == s and not moved:
+                continue
+            near = dp if to < s else kd
+            tied, go, stay = set(near[j]), [j], []
+            for i in (seq[to:s][::-1] if to < s else seq[s + 1:to + 1]):
+                if i in tied:
+                    go.append(i)
+                    tied.update(near[i])
+                else:
+                    stay.append(i)
+            new = seq[:to] + go[::-1] + stay[::-1] + seq[s + 1:] if to < s else seq[:s] + stay + go + seq[to + 1:]
+            p = min(p, to)
+        for i, _o, y in moved:
+            put(i, y)
+        d2 = [dn[:] for dn in dns]
+        got = run(new, p, d2, sts[p])
+        if got <= now + heat * e:
+            now, dns, seq, taken = got, d2, new, taken + 1
+            if taken % SORT == 0:
+                seq, p, x = sorted(new, key=lambda k: d2[0][k] - l0[k] - c0[k]), 0, taken // SORT % len(cs)
+                hot = tight(seq, dns[x], cs[x])
+            sts = states(seq, dns, p, sts)
+        else:
+            for i, o, _y in moved:
+                put(i, o)
+    for k in range(m):
+        way[win[k]] = w[k]
+    return [win[k] for k in seq]
+
+
 def mend(ops, deps, kids):
-    n = len(ops)
+    n, cases = len(ops), range(len(WAKE))
     rng = np.random.default_rng(SEED)
-    ways = [[("vstygx".index(w[0]), w[1]) for w in o["ways"]] for o in ops]
-    late = [o["late"] + WAKE for o in ops]
+    ways = [["vstygx".index(w[0]) for w in o["ways"]] for o in ops]
+    costs = [[[float((w[1] + 0 * WAKE)[s]) for w in o["ways"]] for o in ops] for s in cases]
+    late = [[float((o["late"] + WAKE)[s]) for o in ops] for s in cases]
     way = [0] * n
-    q, cost = [w[0][0] for w in ways], [w[0][1] for w in ways]
-    best = now = None
-    seq, was = list(range(n)), ([0.0] * n, [0.0] * n, [-1] * n)
-    for turn, (a, b, c, d, e) in enumerate(rng.random((TURNS, 5)).tolist()):
-        new, p, moved = seq, 0, []
-        if turn % SHAKE == 0:
-            new = shake(sorted(seq, key=lambda i: was[1][i]) if turn else seq, deps, kids, q, cost, late)
-        else:
-            j = chain[int(a * len(chain))] if b < 0.7 else int(a * n)
-            p = to = at[j]
-            if len(ways[j]) > 1 and c < 0.3:
-                moved = [(j, way[j], (way[j] + 1 + int(d * (len(ways[j]) - 1))) % len(ways[j]))]
-                if c > 0.2 and len(ways[j]) == 2:
-                    twin = [i for i in seq[max(p - 25, 0):p + 25] if q[i] == ways[j][moved[0][2]][0] and len(ways[i]) == 2]
-                    if twin:
-                        i = twin[int(e * 997) % len(twin)]
-                        moved.append((i, way[i], 1 - way[i]))
-            if not moved or c < 0.1:
-                to = min(max(p + int((d - 0.5) * (FAR[0] if c < 0.8 else FAR[1])), 0), n - 1)
-                if to == p and not moved:
-                    continue
-                near = deps if to < p else kids
-                tied, go, stay = set(near[j]), [j], []
-                for i in (seq[to:p][::-1] if to < p else seq[p + 1:to + 1]):
-                    if i in tied:
-                        go.append(i)
-                        tied.update(near[i])
-                    else:
-                        stay.append(i)
-                new = seq[:to] + go[::-1] + stay[::-1] + seq[p + 1:] if to < p else seq[:p] + stay + go + seq[to + 1:]
-            p = min([p, to] + [at[i] for i, _o, _w in moved])
-        for i, _o, w in moved:
-            way[i], (q[i], cost[i]) = w, ways[i][w]
-        got = times(new, p, was, deps, q, cost, late)
-        worth = max(got[1]) + SOON * sum(got[1]) / n
-        if now is None or worth <= now + SLACK * (1 - turn / TURNS) * e:
-            now = worth
-            seq = sorted(new, key=lambda i: got[0][i])
-            was = times(seq, 0, got, deps, q, cost, late)
-            at = [0] * n
-            for p, i in enumerate(seq):
-                at[i] = p
-            chain = [was[1].index(max(was[1]))]
-            while was[2][chain[-1]] >= 0:
-                chain.append(was[2][chain[-1]])
-            if best is None or max(was[1]) < best[1]:
-                best = ([(i, was[0][i]) for i in seq], max(was[1]), list(way))
-        else:
-            for i, o, _w in moved:
-                way[i], (q[i], cost[i]) = o, ways[i][o]
+    chosen = lambda: ([ways[j][way[j]] for j in range(n)], [[costs[s][j][way[j]] for j in range(n)] for s in cases])
+    q, cost = chosen()
+    same = SAME.tolist()
+    seq = shake(list(range(n)), deps, kids, q, cost[0], late[0], same[0])
+    pure = [[0.0] * n for s in cases]
+    for s in cases:
+        for j in range(n - 1, -1, -1):
+            pure[s][j] = max([pure[s][i] + GROW * (late[s][i] + min(costs[s][i])) for i in kids[j]] + [0.0])
+    worth = lambda x: sum(WEIGHT[s] * max(heads(x, deps, q, cost[s], late[s], same[s])[1]) for s in cases)
+    early = [j for j, o in enumerate(ops) if o.get("early")]
+    best, plan = None, [(0, n, k / SWEEPS, HEAT) for k in range(SWEEPS)]
+    for a in range(AGAIN):
+        a = int(a * 0.618 % 1 * n) - PART // 2
+        plan += [(a, a + PART, k / TURNS, WARM) for k in range(TURNS)]
+    for sweep, (lo, hi, part, heat) in enumerate(plan):
+        heat *= (1 - part) ** 2
+        for s in cases:
+            for j in early:
+                late[s][j] = float(WAKE[s]) + (AHEAD * max(1 - 1.3 * part, 0.0) if hi - lo == n else 0.0)
+        if part == 0 and best:
+            seq, way[:] = [i for i, _t in best[0]], best[2]
+            q, cost = chosen()
+        if sweep % 3 == 1 and hi - lo == n:
+            s = sweep // 3 % len(cases)
+            done = heads(seq, deps, q, cost[s], late[s], same[s])[1]
+            new = shake(sorted(seq, key=lambda i: done[i]), deps, kids, q, cost[s], late[s], same[s])
+            if worth(new) <= worth(seq) + heat:
+                seq = new
+        rest = [tails(seq, kids, q, cost[s], late[s], same[s]) for s in cases]
+        done, free, p = [[0.0] * n for s in cases], [[0.0] * 6 for s in cases], 0
+        first = int(rng.integers(STRIDE // 2, STRIDE))
+        while p < n:
+            lead = {}
+            for j in seq[p + SPAN:][::-1]:
+                lead[q[j]] = j
+            now = [(float(WEIGHT[s]), costs[s], late[s], tuple(free[s]), done[s], rest[s],
+                    [rest[s][lead[x]] if x in lead else 0.0 for x in range(5)], same[s]) for s in cases]
+            if p >= lo - first:
+                seq[p:p + SPAN] = stretch(seq[p:p + SPAN], now, pure, ways, way, deps, kids, rng.random((MOVES, 4)).tolist(), heat)
+            if p + SPAN >= min(n, hi):
+                break
+            step = STRIDE if p else first
+            for j in seq[p:p + step]:
+                k = ways[j][way[j]]
+                for s in cases:
+                    at = max([free[s][k]] + [done[s][i] + same[s] * (ways[i][way[i]] == k < 2) for i in deps[j]]) + costs[s][j][way[j]]
+                    done[s][j] = at + late[s][j]
+                    if k < 5:
+                        free[s][k] = at
+            p += step
+        q, cost = chosen()
+        start = heads(seq, deps, q, cost[0], late[0], same[0])[0]
+        seq.sort(key=lambda i: start[i])
+        if best is None or worth(seq) < best[1]:
+            best = ([(i, start[i]) for i in seq], worth(seq), list(way))
     return best
 
 

import numpy as np
from concourse.mybir import dt, AluOpType as A, ActivationFunctionType as F

C, H, R, P0 = 384, 56, 3, 48
STEP = [1, 2, 1]
WID = [96, 100, 104]
G0 = [388, 452, 452]
THIRDS = [(256, 384), (128, 256), (0, 128)]
CH = [[(192, 384), (0, 192)], THIRDS, THIRDS, THIRDS]
CUT = 128
SEND = [[(192, 384), (0, 192)]] * 3
ALL, OWN = [0, 192, 256], [64, 128, 320]
BIG = 2.0 ** 80
TINY = 2.0 ** -10
U = -2.0 ** 75
B1K, LIFT = 1024.0, 2.0 ** 24
MAGIC = 1.5 * 2.0 ** 23
OFF = 13112.0
NEW = 50 * 512
CASES = [(0.93, 8, 50, 95, 1300, 900, 135, 0.68, 78, 1.25, 1.48, 14), (1.11, 23, 100, 188, 1200, 1300, 125, 0.25, 62, 0.92, 1.75, 30)]
CYC, VFIX, SFIX, WAKE, FLY, LOAD, RATE, WEIGHT, SAME, PE, GAT, SMIN = np.array(CASES).T
NEARBY, CALL, FIRST, LRATE = 1.5, 270.0, 1200.0, 310.0
SPAN, STRIDE, MOVES, SWEEPS, HEAT, REACH, SEED = 64, 24, 500, 85, 110.0, 30, 2
SORT, AIM, AHEAD = 5, 0.5, 700.0
PART, AGAIN, TURNS, WARM = 200, 0, 12, 40.0
SOON, NEAR, BAND, GROW = 0.1, 4.0, 2000.0, 1.12

ARENA = {"f": 0, "h": 0, "i": 0, "w": 0}
AT = {}
KEPT = {}


def _take(ar, name, n):
    al = 8 if ar in "fi" else 16
    AT[name] = (ar, ARENA[ar])
    ARENA[ar] += (n + al - 1) // al * al


for _n, _k in [("k2", 120), ("none", 16), ("r0", 64), ("nv0", 64), ("id", 64), ("n1", 64), ("m", 512), ("cum0", 64), ("cum", 128),
               ("vr1", 520), ("vr2", 520), ("vr3", 456), ("s", 384), ("ms", 384), ("pc", 16),
               ("j16", 64), ("j8", 64), ("j4", 112), ("lift", 384), ("m4", 112), ("sel", 64), ("down", 64),
               ("kp", 112), ("k4", 144), ("cj", 72), ("junk", 640), ("mq", 64), ("y", 64), ("yv", 64), ("sg4", 8),
               ("ys", 64), ("wu", 64), ("nq", 128), ("rest", 256), ("oz", 64), ("ed0", 64), ("nv", 192), ("g", 128),
               ("born", 192), ("r1", 192), ("d", 192), ("ed", 192), ("p", 384), ("fa", 128), ("fx", 384), ("pay", 192), ("v2", 192),
               ("rv", 128), ("vb8", 64), ("tp", 64), ("pd", 64), ("p0", 112), ("pr", 112), ("sr", 112), ("sd", 112), ("lh", 112),
               ("pk", 112), ("pkr", 384), ("pkd", 384), ("t4o", 144), ("hold0", 384), ("hold1", 384),
               ("hold2", 384), ("dg", 1152), ("t4", 432), ("b1", 144)]:
    _take("f", _n, _k)
for _t in range(R):
    _take("w", "en%d" % _t, 12)
    _take("w", "el%d" % _t, 96)
for _n, _k in [("eq", 384), ("pos", 512), ("tb", 400), ("vr0", 464), ("sg", 392), ("cc", 392), ("rs", 392), ("lc", 392), ("li", 392),
               ("kr", 392), ("step", 384)]:
    _take("h", _n, _k)
for _n, _k in [("pi", 8), ("pj", 8), ("ui", 8), ("xi", 24), ("xk", 24), ("xb", 24), ("ki2", 48)]:
    _take("i", _n, _k)
for _n, _k in [("zu", 4), ("uo", 8), ("pu", 8), ("ru", 8), ("rk", 4), ("kl", 72)]:
    _take("w", _n, _k)

X4, U8, BF, F32 = "float8_e4m3fn_x4", "uint8", "bfloat16", "float32"
SCRATCH = {"f": ("sbuf", [128, ARENA["f"]], F32), "h": ("sbuf", [128, ARENA["h"]], BF),
           "i": ("sbuf", [128, ARENA["i"]], "int32"), "w": ("sbuf", [128, ARENA["w"]], "uint16"),
           "zi": ("sbuf", [128, 4], "int32"), "ps": ("psum", [128, 4096], F32),
           "pool3": ("sbuf", [128, 4 * C], BF), "ub": ("sbuf", [128, 512], BF), "vb": ("sbuf", [128, 512], BF),
           "tiny": ("sbuf", [128, 528], BF), "eye": ("sbuf", [128, 528], BF), "mt": ("sbuf", [128, 512], BF),
           "ah": ("sbuf", [128, 448], BF), "aa": ("sbuf", [128, 448], BF), "rl": ("sbuf", [128, 448], F32),
           "dh": ("sbuf", [128, 4 * C + 8], F32), "yb": ("sbuf", [128, C], F32)}
for _n, _k in [("u", 128), ("u2", 128), ("v", 128), ("w", 512), ("e", 512), ("m", 128), ("x0", C), ("x1", C), ("x2", C), ("x3", C),
               ("l0", C), ("l1", C), ("l2", C)]:
    SCRATCH["q" + _n] = ("sbuf", [128, _k], X4)
    SCRATCH["s" + _n] = ("sbuf", [128, _k], U8)
for _t in range(R):
    SCRATCH["pool%d" % _t] = ("sbuf", [128, 4 * (G0[_t] + 6 * H)], BF)
    SCRATCH["out%d" % _t] = ("sbuf", [128, WID[_t] // 4], "uint16")
    SCRATCH["lin%d" % _t] = ("sbuf", [128, WID[_t] // 4], "uint16")
NSEM, NDMA = 110, 28
SEMAPHORES = (["c%d" % k for k in range(NSEM)] + ["d%d" % k for k in range(NDMA)] + ["sent"]
              + [n + str(t) for n in ("qa", "qb", "la") for t in range(R)])


def v(name, a=0, b=None, s=1):
    if name in AT:
        ar, o = AT[name]
        return (ar, o + a, o + b, s)
    return (name, a, SCRATCH[name][1][1] if b is None else b, s)


def ind(win, off):
    return ("@", win, off)


def size(d):
    return 16 * size(d[2]) if d[0] == "@" else len(range(d[1], d[2], abs(d[3])))


def two(d):
    return d[0] != "@" and SCRATCH[d[0]][2] in (BF, "uint16")


def places(ds):
    o = []
    for d in ds:
        if isinstance(d, tuple):
            o += [d[1], d[2]] if d[0] == "@" else [d]
    return o


def collect(g, T, topo, core, rank):
    ops = []

    def ap(d):
        if not isinstance(d, tuple):
            return d
        if d[0] == "@":
            return ap(d[1]).indirect(ap(d[2]))
        if d[3] < 0:
            return T[d[0]][:, d[2] - 1:d[1] - 1:d[3]] if d[1] else T[d[0]][:, d[2] - 1::d[3]]
        return T[d[0]][:, d[1]:d[2]:d[3]] if d[3] > 1 else T[d[0]][:, d[1]:d[2]]

    def add(ways, rd, wr, late=0.0, **k):
        ops.append(dict(ways=ways, rd=places(rd), wr=places(wr), late=late, **k))
        return len(ops) - 1

    def cyc(out, ins, k=1.0):
        if out[0] == "@":
            return 50 + CYC * 3.8 * size(out)
        if ins and ins[0][0] == "@":
            return 50 + CYC * GAT * size(out)
        if all(two(d) for d in [out] + ins):
            k *= 0.75 if k == 2 else 0.5
        return VFIX + CYC * max(64.0, size(out) * k)

    def tt(out, a, b, op):
        c = cyc(out, [a, b], 1 if "ps" in (a[0], b[0]) else 2)
        add([("v", c, lambda: g.vector.tensor_tensor(ap(out), ap(a), ap(b), op))], [a, b], [out])

    def vts(out, a, s1, op0, s2=None, op1=None):
        if op1 is None:
            return ("v", cyc(out, [a]), lambda: g.vector.tensor_scalar(ap(out), ap(a), ap(s1), None, op0))
        return ("v", cyc(out, [a]), lambda: g.vector.tensor_scalar(ap(out), ap(a), ap(s1), ap(s2), op0, op1))

    def ts(out, a, s1, op0, s2=None, op1=None):
        add([vts(out, a, s1, op0, s2, op1)], [a, s1, s2], [out])

    def vcp(out, a):
        return ("v", cyc(out, [a]), lambda: g.vector.tensor_copy(ap(out), ap(a)))

    def cp(out, a):
        if out[0] == "@":
            add([vcp(out, a)], [a, out[2]], [out[1]])
        else:
            add([vcp(out, a)], [a], [out])

    def scan(out, d0, d1, init, op0, op1):
        add([("v", cyc(out, [d0, d1]), lambda: g.vector.tensor_tensor_scan(ap(out), ap(d0), ap(d1), ap(init), op0, op1))],
            [d0, d1, init], [out])

    def sact(out, a, fn, scale=None, bias=None, acc=None):
        k = {}
        if scale is not None:
            k["scale"] = scale
        if bias is not None:
            k["bias"] = bias
        if acc is not None:
            k["accum_out"] = acc
        c = 15 + cyc(out, [a]) if a[0] == "@" else SFIX + CYC * np.maximum(SMIN, size(out)) + (20 if acc else 0)
        return ("s", c, lambda: g.scalar.activation(ap(out), ap(a), fn, **{x: ap(y) for x, y in k.items()}))

    def act(out, a, fn, scale=None, bias=None, acc=None):
        add([sact(out, a, fn, scale, bias, acc)], [a, scale, bias], [out, acc])

    def lin(out, a, scale=None, bias=None):
        if scale is None and bias is None:
            w = vcp(out, a)
        elif bias is None:
            w = vts(out, a, scale, A.mult)
        elif scale is None:
            w = vts(out, a, bias, A.add)
        else:
            w = vts(out, a, scale, A.mult, bias, A.add)
        add([sact(out, a, F.Identity, scale, bias), w], [a, scale, bias], [out])

    def relu(out, a, scale=None, bias=None):
        ways = [sact(out, a, F.Relu, scale, bias)]
        if bias is None:
            ways.append(vts(out, a, scale, A.mult, 0.0, A.max))
        elif scale is None:
            ways.append(vts(out, a, bias, A.add, 0.0, A.max))
        add(ways, [a, scale, bias], [out])

    def giota(out, pat, base, cm=0):
        if SCRATCH[out[0]][2] == "int32":
            fn = lambda: g.iota(ap(out), pat, base, cm)
        else:
            fn = lambda: g.iota(ap(out), pat, base, cm, allow_small_or_imprecise_dtypes=True)
        return ("g", 130 + 2 * CYC * size(out), fn)

    def iota(out, pat, base, cm=0):
        add([giota(out, pat, base, cm)], [], [out])

    def vset(out, c):
        return ("v", cyc(out, []), lambda: g.vector.memset(ap(out), float(c)))

    def fill(out, c):
        src = v("tiny", 0, size(out))
        add([vset(out, c), giota(out, [[0, size(out)]], int(c)), sact(out, src, F.Identity, 0.0, float(c))], [src], [out])

    def quant(name, c0, c1, src):
        q, s = v("q" + name, c0, c1), v("s" + name, c0, c1)
        add([("v", (12 + 0.22 * size(src)) * CYC / 0.83, lambda: g.vector.quantize_mx(ap(q), ap(s), ap(src)))], [src], [q, s])

    def mm(bank, st, s0, mv, c0, c1):
        out = v("ps", 512 * bank, 512 * bank + c1 - c0)
        a, b, c, d = v("q" + st, s0, s0 + 128), v("s" + st, s0, s0 + 128), v("q" + mv, c0, c1), v("s" + mv, c0, c1)
        add([("t", PE * (c1 - c0 + 16), lambda: g.tensor.matmul_mx(ap(out), ap(a), ap(b), ap(c), ap(d), True, True))], [a, b, c, d], [out])
        return out

    def dma(q, out, src, rd, wr, nbytes, last=False):
        e = g.sync if q == "y" else g.scalar
        add([(q, 60, lambda: e.dma_start(out(), src()))], rd, wr, late=LOAD + nbytes / LRATE, dma=True, last=last)

    def again(out, src):
        pick = lambda: g.affine_select(ap(out), ap(src), [[0, size(out)]], A.is_gt, 0.0, 1, 0)
        add([sact(out, src, F.Identity), vcp(out, src), ("g", 170 + 2 * CYC * size(out), pick)], [src], [out])

    def byt(d):
        return ap(d).bitcast(dt.uint8)

    Q16, HH, QQ, T4, S4, SGN, THR, C4, TMP = [v("pc", k, k + 1) for k in range(9)]

    dma("y", lambda: T.zi[:, 0:3], lambda: T.z[:, :], [], [v("zi", 0, 3)], 2e3)
    dma("s", lambda: T.ub[:, :], lambda: T.u[:, :], [], [v("ub")], 131e3)
    for k, (c0, c1) in enumerate(CH[0]):
        dma("y", lambda c0=c0, c1=c1: T.pool0[:, 4 * c0:4 * c1], lambda c0=c0, c1=c1: T.x[:, 4 * c0:4 * c1], [],
            [v("pool0", 4 * c0, 4 * c1)], 131e3 + 1024 * (C - c0))

    add([vset(v("tiny"), TINY)], [], [v("tiny")])
    iota(v("pi", 0, 1), [[0, 1]], 0, 1)
    scan(v("tb", 0, C + 1), v("tiny", 0, C + 1), v("tiny", 0, C + 1), -193.0 / 512, A.add, A.add)
    iota(v("j16", 0, 64), [[0, 4], [1, 16]], 0)
    iota(v("j8", 0, 64), [[0, 8], [1, 8]], 0)
    iota(v("ui", 0, 8), [[16, 8]], 0)
    for k, (sh, msk) in enumerate([(0, 15), (0, 1), (1, 7), (0, 3), (2, 3)]):
        ts(v("pj", k, k + 1), v("pi", 0, 1), sh, A.logical_shift_right, msk, A.bitwise_and)
    cp(v("pc", 0, 5), v("pj", 0, 5))
    lin(SGN, HH, -2.0, 1.0)
    lin(THR, HH, BIG, BIG / 2)
    lin(TMP, S4, 2 * B1K, 8 * B1K)
    ts(C4, TMP, 2.0, A.mult, T4, A.add)
    fill(("f", AT["none"][1], AT["m"][1], 1), 0)
    fill(v("m", C, 512), 0)
    fill(v("vr0", 16, 416), 0)
    fill(v("cum", 0, 128, 64), 1)
    for t in (1, 2, 3):
        fill(v("vr%d" % t, 8, 400), 0)
    fill(v("fx", 0, 384, 2), 0)
    fill(v("t4", 2, 432, 6), 0)
    fill(v("dh", 4 * C, 4 * C + 8), 0)
    for t in range(R):
        fill(v("pool%d" % t, 4 * C, 4 * C + 16), 0)
    fill(v("mt", 4 * WID[0], 512), 0)
    fill(v("pos", C, 512), 0)
    fill(v("k2", 0, 66), 513)
    fill(v("k2", 66 + P0, 67 + P0), 2 * (P0 + 2))
    fill(v("born", 128, 192), 1)
    fill(v("rest", 192, 193), 1)
    fill(v("pr", 2 * P0, 112), C)
    add([vset(v("step", 0, CUT), U), sact(v("step", 0, CUT), v("tiny", 0, CUT), F.Identity, U / TINY)], [v("tiny", 0, CUT)], [v("step", 0, CUT)])
    iota(v("d", 0, 192), [[0, 3], [-2 ** 15, 64]], 2 - 2 ** 15)
    iota(v("n1", P0 + 2, P0 + 6), [[-2, 2], [-H, 2]], 2 - G0[1])
    iota(v("id", P0, P0 + 6), [[512, 3], [H, 2]], NEW - 512 + G0[0] - 2)
    iota(v("id", P0 + 6, 64), [[1, 10]], 0)
    ts(v("sel", 0, 64), v("j8", 0, 64), QQ, A.not_equal, BIG * 2.0 ** 13, A.mult)
    ts(v("down", 0, 64), v("j8", 0, 64), 0.0, A.is_equal, -BIG * 2.0 ** 15, A.mult)
    ts(v("lift", 0, 64), v("j16", 0, 64), Q16, A.is_equal, LIFT, A.mult)
    ts(v("lift", 64, 128), v("j16", 0, 64), Q16, A.is_gt)
    tt(v("lift", 0, 64), v("lift", 0, 64), v("lift", 64, 128), A.add)
    lin(v("lift", 15, 64, 16), v("lift", 15, 64, 16), 1.0 / (U * LIFT))
    again(v("lift", 64, 128), v("lift", 0, 64))
    add([("g", 170 + 2 * CYC * 516, lambda: g.affine_select(T.eye[:, 0:516], T.tiny[:, 0:516], [[1, 516]], A.is_equal, 0.0, -3, -4))],
        [v("tiny", 0, 516)], [v("eye", 0, 516)])
    iota(v("li", 0, 392), [[-8, 7], [1, H]], 0)
    fill(v("kr", 0, 392), 64)
    fill(v("kr", 0, 392, H), 0)
    iota(v("j4", 0, 112), [[0, 28], [2048, 4]], 9 * 1024)
    iota(v("kp", 0, 112), [[0, H], [1024, 2]], 0)
    iota(v("k4", 0, 144), [[0, 24], [1024, 6]], 0)
    ts(v("lc", 0, 392), v("li", 0, 392), QQ, A.is_lt, 2.0 ** -120, A.mult)
    ts(v("m4", 0, 112), v("j4", 0, 112), TMP, A.subtract, B1K, A.min)
    lin(v("m4", 3, 112, 4), v("m4", 3, 112, 4), None, -8 * B1K)
    for b in range(4):
        quant("e", 128 * b, 128 * b + 128, v("eye", 3 - b, 515 - b))

    quant("u", 0, 128, v("ub"))
    cp(v("uo", 0, 8), v("ui", 0, 8))
    add([("v", 50 + 200 * CYC, lambda: g.vector.tensor_copy(T.qu2[:, 0:128].bitcast(dt.uint32), T.qu[:, 0:128].bitcast(dt.uint32).indirect(ap(v("uo", 0, 8)))))],
        [v("qu"), v("uo", 0, 8)], [v("qu2")])
    add([("s", 65 + 200 * CYC, lambda: g.scalar.activation(T.su2[:, 0:128], T.su[:, 0:128].indirect(ap(v("uo", 0, 8))), F.Copy))],
        [v("su"), v("uo", 0, 8)], [v("su2")])

    def marks(t):
        scan(v("p", OWN[t], OWN[t] + 64), v("p", ALL[t], ALL[t] + 64), v("sel", 0, 64), BIG * 2.0 ** 13, A.min, A.max)

    cp(v("zu", 0, 3), v("zi", 0, 3))
    lin(v("r0", 0, P0), ind(v("tb", 0, C + 1), v("zu", 0, 3)), 512.0, 191.0)
    lin(v("nv0", 0, P0), v("r0", 0, P0), None, 1.0)
    scan(v("cum0", 0, 64), v("r0", -1, 63), v("born", 128, 192), 0.0, A.add, A.add)
    scan(v("ed0", 0, 64), v("cum0", 0, 64), v("lift", 0, 64), 0.0, A.max, A.mult)
    for k in range(2):
        ts(v("en0", 4 * k, 4 * k + 4), v("ed0", 15, 64, 16), U, A.mult, -1.0, A.add)
    act(v("p", 0, 64), v("nv0", 0, 64), F.Relu, -BIG, THR)
    marks(0)
    lin(v("fx", 1, 128, 2), v("cum0", 0, 64), 2.0, -1.0)
    cp(ind(v("vr0", 16, 464), v("en0", 0, 3)), v("step", 0, P0))

    k2 = lambda a, b: v("k2", 66 + a, 66 + b)
    lin(k2(0, P0), v("r0", 0, P0), 2.0, 2.0)
    act(v("junk", 0, 100), k2(-52, P0), F.Sign, None, -3.0, acc=k2(P0 + 1, P0 + 2))
    for k, (more, least) in enumerate([(58, 5.0), (58, 7.0), (66, 9.0), (66, 11.0)]):
        act(v("junk", 128 * k + 128, 128 * k + 178 + more), k2(-more, P0 + 2), F.Sign, None, -least, acc=k2(P0 + 2 + k, P0 + 3 + k))
    scan(v("id", 1, P0), v("r0", 0, P0 - 1), v("k2", 0, P0 - 1), 0.0, A.add, A.add)
    lin(v("mq", 0, 64), k2(0, 64), 2.0 ** 14, OFF - 1)
    scan(v("y", 0, 64), v("id", 0, 64), v("mq", 0, 64), -1.0, A.max, A.subtract)
    scan(v("yv", 0, 64), v("y", 0, 64), v("lift", 0, 64), 0.0, A.min, A.mult)
    for k in range(4):
        act(v("junk", 128 * k + 128, 128 * k + 192), v("y", 0, 64), F.Sign, -1.0 / U, v("yv", 16 * k + 15, 16 * k + 16), acc=v("sg4", k, k + 1))
    ts(v("rk", 0, 4), v("sg4", 0, 4), -0.5, A.mult, 31.5, A.add)
    cp(ind(v("ys", 0, 64), v("rk", 0, 4)), v("y", 0, 64))
    lin(v("wu", 0, 64), v("ys", 0, 64), -2.0 ** -15, MAGIC)
    lin(v("nq", 0, 64), v("wu", 0, 64), 2.0 ** 15, -MAGIC * 2.0 ** 15)
    scan(v("rest", 0, 64), v("ys", 0, 64), v("nq", 0, 64), 0.0, A.min, A.add)
    lin(v("n1", 0, P0 + 2), k2(0, P0 + 2), 0.5, -2.0)
    cp(ind(v("nv", 0, 64), v("rk", 0, 4)), v("n1", 0, 64))
    relu(v("r1", 0, 64), v("nv", 0, 64), None, -1.0)
    ts(v("born", 0, 64), v("nv", 0, 64), -100.0, A.is_gt)
    lin(v("g", 0, 64), v("nv", 0, 64), -1.0, 1.0)
    scan(v("cum", 1, 64), v("r1", 0, 63), v("born", 0, 63), 1.0, A.add, A.add)
    lin(v("nq", 64, 128), v("wu", 0, 64), None, -MAGIC - 4)
    lin(v("nv", 128, 192), v("wu", 0, 64), None, -MAGIC - 6)
    relu(v("g", 64, 128), v("rest", 0, 64), None, OFF - NEW - 512 + G0[1] - G0[0])
    scan(v("nv", 64, 128, -1), v("nq", 64, 128, -1), v("g", 64, 128, -1), -1024.0, A.max, A.subtract)
    relu(v("born", 64, 128), v("g", 64, 128), -1.0, 1.0)
    relu(v("r1", 64, 192), v("nv", 64, 192), None, -1.0)
    scan(v("cum", 65, 128), v("r1", 64, 127), v("born", 64, 127), 1.0, A.add, A.add)
    scan(v("rest", 193, 256), v("r1", 128, 191), v("born", 128, 191), 1.0, A.add, A.add)
    for t, a, b in ((1, 0, 64), (2, 64, 192)):
        scan(v("rest", 64 + a, 128 + a, -1), v("cum", a, a + 64, -1), v("g", a, a + 64, -1), 2048.0, A.min, A.max)
        scan(v("ed", a, b), v("rest", 64 + a, 64 + b), v("lift", 0, b - a), 0.0, A.max, A.mult)
        ts(v("en%d" % t, 0, 4), v("ed", a + 15, a + 64, 16), U, A.mult, -1.0, A.add)
        ts(v("en%d" % t, 4, 4 + (b - a) // 16), v("ed", a + 15, b, 16), U, A.mult, -1.0, A.add)
        scan(v("pay", a, b), v("rest", a, b), v("d", a, b), 2.0 ** 20, A.min, A.subtract)
        lin(v("v2", a, b), v("pay", a, b), U)
    act(v("p", ALL[1], ALL[1] + 128), v("nv", 0, 128), F.Relu, -BIG, THR)
    marks(1)
    marks(2)
    act(v("fa", 0, 128), v("rest", 64, 192), F.Relu, -2.0, 2.0 * C + 1)
    lin(v("fx", 129, 384, 2), v("fa", 0, 128), -1.0, 2.0 * C)
    for t in range(R):
        a, b, vr, hold = 24 * t, 24 * t + 24, "vr%d" % (t + 1), "hold%d" % t
        cp(ind(v(vr, 8, 520 if t < 2 else 456), v("en%d" % (t + 1), 0, 4) if t < 2 else v("en2", 8, 12)), v("v2", 64 * t, 64 * t + 64))
        for c in range(0, C, CUT):
            scan(v(hold, c, c + CUT), v(vr, 8 + c, 8 + c + CUT), v("step", 0, CUT), v(hold, c - 1, c) if c else 0.0, A.min, A.add)
            scan(v("dg", C * t + c, C * t + c + CUT), v(hold, c, c + CUT), v("lift", 0, CUT), 0.0, A.min, A.mult)
        got, base = v("dg", 16 * a + 15, 16 * b, 16), v("t4", 6 * a + 1, 6 * b, 6)
        if t:
            ts(v("kl", a, b), got, 2.0 ** -14, A.mult, -1.0, A.add)
            lin(v("cj", a, b), got, 2.0 ** -15, MAGIC)
            lin(v("cj", a, b), v("cj", a, b), -2.0 ** 15, MAGIC * 2.0 ** 15)
            tt(base, got, v("cj", a, b), A.add)
        else:
            ts(v("xi", a, b), got, OFF, A.add)
            ts(v("xk", a, b), v("xi", a, b), 8, A.logical_shift_right, 126, A.bitwise_and)
            ts(v("kl", a, b), v("xk", a, b), 1.0, A.add)
            ts(v("xb", a, b), v("xi", a, b), 511, A.bitwise_and)
            cp(base, v("xb", a, b))
        lin(v("b1", 2 * a, 2 * b, 2), base, B1K, B1K - 1)
        lin(v("b1", 2 * a + 1, 2 * b, 2), base, None, 1.0)
        ts(v("t4", 6 * a + 4, 6 * b, 6), base, float(C), A.is_ge, 2.0 * H, A.mult)
        again(v("t4", 6 * a + 5, 6 * b, 6), v("t4", 6 * a + 4, 6 * b, 6))
    relu(v("oz", 0, H), v("nv", 128, 128 + H), None, 0.0)
    dma("y", lambda: T.oz[:, :], lambda: T.f[0:128:16, AT["oz"][1]:AT["oz"][1] + H], [v("oz", 0, H)], [], 2e3, last=True)

    sent = [0]

    def send(src, dst, sem, peer, codes, nbytes):
        rid, pid = topo.addr(peer)[:2]
        m = topo.mask(core, peer)
        k = len(topo.engines(core, peer))
        c = CALL + (0.0 if sent[0] else FIRST)
        sent[0] += k
        pick = byt if codes else ap
        return k, add([("g", c, lambda: g.remote_dma(pick(dst), pick(src), T.sem[sem], T.sem.sent, pid, rid, m))], [src], [],
                      late=FLY + nbytes / RATE / (NEARBY if topo.chip(core) == topo.chip(peer) else 1.0))

    for t in range(R):
        pool, nxt, xq, lq = "pool%d" % t, "pool%d" % (t + 1), "x%d" % t, "l%d" % t
        w = lambda name, a=0, b=64, s=1: v(name + str(t), a, b, s)
        ns, n, at = 7 if t else 6, WID[t], 9 if t else 17
        peer = T.cores[rank ^ STEP[t]]
        for k, (c0, c1) in enumerate(CH[t]):
            quant(xq, c0, c1, v(pool, 4 * c0, 4 * c1))
            o = mm(k, "u2", 0, xq, c0, c1)
            lin(v("s", c0, c1), o, SGN)
            scan(v("m", c0, c1, -1), w("vr", at + c0, at + c1, -1), v("s", c0, c1, -1), v("m", c1, c1 + 1) if k else -BIG, A.add, A.max)
            lin(v("ms", c0, c1), v("m", c0, c1), SGN)
            tt(v("eq", c0, c1), o, v("ms", c0, c1), A.is_equal)
            scan(v("pos", c0, c1, -1), v("eq", c0, c1, -1), v("tb", C + 1 - c1, C + 1 - c0), v("pos", c1, c1 + 1), A.add, A.min)
        for k, (c0, c1) in enumerate(SEND[t]):
            sem, far = "q%s%d" % ("ab"[k], t), 640 * (C - c0) - 300 * k * (C - c1)
            k1, o1 = send(v("q" + xq, c0, c1), v("q" + lq, c0, c1), sem, peer, True, far)
            k3, o2 = send(v("s" + xq, c0, c1), v("s" + lq, c0, c1), sem, peer, False, far)
            add([("x", 0, None)], [], [v("q" + lq, c0, c1), v("s" + lq, c0, c1)], after=[o1, o2], sem=sem, cnt=k1 + k3)
            for b in range(4):
                lin(v("dh", 4 * c0 + b, 4 * c1, 4), mm(3 + b, "e", 128 * b, lq, c0, c1), 0.5 / TINY)
        if t == 0:
            landed = [v("ql0", *SEND[0][0])]
            dma("y", lambda: byt(v("qw")), lambda: T.wc[:, :], landed, [v("qw")], 262e3)
            dma("y", lambda: T.sw[:, :], lambda: T.ws[:, :], landed, [v("sw")], 330e3)
        if t == 1:
            dma("y", lambda: T.vb[:, :], lambda: T.v[:, :], [v("ql1")], [v("vb")], 131e3)
            quant("v", 0, 128, v("vb"))
        own, row = OWN[t] - 128 * t, ALL[t] - 128 * t
        tt(v("rv", 0, 128), ind(v("m", 0, 512), w("en", 0, 8)), v("p", 128 * t, 128 * t + 128), A.subtract)
        scan(v("vb8", 0, H), v("down", 0, H), v("rv", own, own + H), 0.0, A.add, A.max)
        for k in range(ns):
            o, a, b = v("sg", H * k, H * k + H), v("rv", row, row + H), v("vb8", 8 * k + 7, 8 * k + 8)
            add([sact(o, a, F.Sign, -1.0, b), vts(o, a, b, A.subtract, -1.0, A.mult)], [a, b], [o])
        tt(v("tp", 0, 64), ind(v("pos", 0, 512), w("en", 0, 4)), v("p", OWN[t], OWN[t] + 64), A.subtract)
        scan(v("pd", 0, H), v("down", 0, H), v("tp", 0, H), 0.0, A.add, A.max)
        ts(v("pu", 0, ns), v("pd", 7, 8 * ns, 8), 512.0, A.mult, 192.0, A.add)
        lin(v("p0", 0, 16 * ns), ind(v("tb", 0, C + 1), v("pu", 0, ns)), -512.0, 192.0)
        scan(v("pr", 0, 16 * ns), v("fx", 128 * t, 128 * t + 16 * ns), v("p0", 0, 16 * ns), 0.0, A.subtract, A.max)
        for a, b in ((0, 2 * H), (2 * H, 4 * H), (4 * H, H * ns)):
            tt(v("cc", a, b), v("sg", a, b), v("lc", a, b), A.is_lt)
            scan(v("rs", a, b), v("kr", a, b), v("cc", a, b), 0.0, A.min, A.add)
        ts(v("ru", 0, ns), v("rs", H - 1, H * ns, H), 2.0, A.mult, HH, A.add)
        cp(ind(v("sr", 0, 112), v("ru", 0, ns)), v("pr", 0, 16 * ns))
        scan(v("sd", 0, n), v("sr", 0, n), v("m4", 0, n), -B1K, A.max, A.add)
        lst, lin_ = v("out%d" % t), v("lin%d" % t)
        ts(lst, v("sd", 3, n, 4), 4.0, A.mult, C4, A.add)
        k1, o1 = send(lst, lin_, "la%d" % t, peer, False, 64 * n)
        add([("x", 0, None)], [], [lin_], after=[o1], sem="la%d" % t, cnt=k1)
        for a, b in ((0, 12), (12, n // 4)):
            lin(v("aa", 16 * a, 16 * b), ind(v(pool, 0, 4 * C + 8), v(lst[0], a, b)))
        lin(v("ah", 0, 4 * n), v("aa", 0, 4 * n), 0.5)
        tt(v("mt", 0, 4 * n), ind(v("dh"), lin_), v("ah", 0, 4 * n), A.add)
        quant("m", 0, 128, v("mt"))
        for b in range(4):
            o = mm((7, 0, 1, 2)[b], "w", 128 * b, "m", 0, 128)
            relu(v("rl", b, 4 * n, 4), (o[0], o[1], o[1] + n, 1), 0.03125)
            for h in range(2):
                to = 4 * (G0[t] + 2 * H * min(b, 2) + H * h) + b
                tt(v(pool, to, to + 2 * n, 4), v("rl", 4 * h + b, 4 * n, 8), v("aa", 4 * h + b, 4 * n, 8), A.add)
        scan(v("lh", 0, 111, -2), v("pr", 0, 111, -2), v("pr", 1, 112, -2), 512.0, A.min, A.min)
        scan(v("lh", 1, 112, -2), v("pr", 0, 111, -2), v("pr", 1, 112, -2), 512.0, A.min, A.max)
        scan(v("pk", 0, 112), v("kp", 0, 112), v("lh", 0, 112), 0.0, A.mult, A.add)
        for c in range(0, C, CUT):
            lin(v("pkr", c, c + CUT), ind(v("pk", 0, 112), v("kl", 24 * t + c // 16, 24 * t + (c + CUT) // 16)), U)
            scan(v("pkd", c, c + CUT), v("pkr", c, c + CUT), v("lift", 0, CUT), 0.0, A.min, A.mult)
        ts(v("ki2", 0, 48, 2), v("pkd", 15, C, 16), -1.0, A.add)
        ts(v("ki2", 1, 48, 2), v("ki2", 0, 48, 2), 1023, A.bitwise_and)
        tt(v("t4", 144 * t, 144 * t + 144, 3), v("ki2", 0, 48), v("b1", 48 * t, 48 * t + 48), A.is_lt)
        scan(v("t4o", 0, 144), v("k4", 0, 144), v("t4", 144 * t, 144 * t + 144), 0.0, A.min, A.add)
        for b in range(4):
            ts(w("el", 24 * b, 24 * b + 24), v("t4o", 3 + min(b, 2), 144, 6), 4.0, A.mult, float(b), A.add)
            ops[-1]["early"] = True
        for k, (c0, c1) in enumerate(CH[t + 1]):
            for b in range(4):
                win = v(pool, 0, 4 * (G0[t] + 2 * H * (min(b, 2) + 1)))
                lin(v(nxt, 4 * c0 + b, 4 * c1, 4), ind(win, w("el", 24 * b + c0 // 16, 24 * b + c1 // 16)))

    for k, (c0, c1) in enumerate(CH[R]):
        quant("x3", c0, c1, v("pool3", 4 * c0, 4 * c1))
        o = mm(k, "v", 0, "x3", c0, c1)
        lin(v("yb", c0, c1), o)
        dma("y", lambda c0=c0, c1=c1: T.oc[:, 4 * c0:4 * c1], lambda c0=c0, c1=c1: byt(v("qx3", c0, c1)), [v("qx3", c0, c1)], [], 512 * (c1 - c0), last=True)
        dma("sy"[k % 2], lambda c0=c0, c1=c1: T.y[:, c0:c1], lambda c0=c0, c1=c1: T.yb[:, c0:c1], [v("yb", c0, c1)], [], 512 * (c1 - c0), last=True)
    for k in range(4):
        dma("ys"[k % 2], lambda k=k: T.osc[4 * k:4 * k + 4, :], lambda k=k: T.sx3[32 * k:32 * k + 4, :], [v("sx3")], [], 2e3, last=True)
    return ops, sent[0]


def cells(d):
    if d[0] == "ps":
        return d[0], {d[1] // 512}
    return d[0], set(range(d[1], d[2], abs(d[3])))


def order(ops):
    n = len(ops)
    deps = [set(o.get("after", [])) for o in ops]
    seen = {}
    for j, o in enumerate(ops):
        for wr, ds in ((False, o["rd"]), (True, o["wr"])):
            for d in ds:
                name, c = cells(d)
                for i, wi, ci in seen.get(name, []):
                    if i != j and (wr or wi or name == "ps") and not c.isdisjoint(ci):
                        deps[j].add(i)
        for wr, ds in ((False, o["rd"]), (True, o["wr"])):
            for d in ds:
                name, c = cells(d)
                if wr:
                    seen[name] = [e for e in seen.get(name, []) if not e[2] <= c]
                seen.setdefault(name, []).append((j, wr, c))
    kids = [[] for _ in ops]
    for j in range(n):
        for i in deps[j]:
            kids[i].append(j)
    return (deps,) + mend(ops, [sorted(d) for d in deps], kids)


def pack(seq, before, q, cost, lead, trail, same):
    done, start, busy = {}, {}, [[] for _ in range(6)]
    for j in seq:
        at = max([done[i] + same * (q[i] == q[j] < 2) for i in before[j]] + [0.0]) + lead[j]
        line, k = busy[q[j]], 0
        if q[j] < 5:
            for a, b in line:
                if a >= at + cost[j]:
                    break
                if b > at:
                    at = b
                k += 1
            line.insert(k, (at, at + cost[j]))
        start[j], done[j] = at, at + cost[j] + trail[j]
    return start, done


def shake(seq, deps, kids, q, cost, late, same):
    none = [0.0] * len(seq)
    back = pack(seq[::-1], kids, q, cost, late, none, same)[1]
    start = pack(sorted(seq, key=lambda i: -back[i]), deps, q, cost, none, late, same)[0]
    return sorted(seq, key=lambda i: start[i])


def heads(seq, deps, q, cost, late, same):
    start, done, free = [0.0] * len(seq), [0.0] * len(seq), [0.0] * 6
    for j in seq:
        start[j] = max([free[q[j]]] + [done[i] + same * (q[i] == q[j] < 2) for i in deps[j]])
        done[j] = start[j] + cost[j] + late[j]
        if q[j] < 5:
            free[q[j]] = start[j] + cost[j]
    return start, done


def tails(seq, kids, q, cost, late, same):
    rest, nxt = [0.0] * len(seq), [0.0] * 6
    for j in seq[::-1]:
        rest[j] = cost[j] + max(late[j] + max([rest[i] + same * (q[i] == q[j] < 2) for i in kids[j]] + [0.0]), nxt[q[j]])
        if q[j] < 5:
            nxt[q[j]] = rest[j]
    return rest


def stretch(win, cases, pure, ways, way, deps, kids, rnd, heat):
    m = len(win)
    loc = {j: k for k, j in enumerate(win)}
    dp = [[loc[i] for i in deps[j] if i in loc] for j in win]
    kd = [[loc[i] for i in kids[j] if i in loc] for j in win]
    wy = [ways[j] for j in win]
    w = [way[j] for j in win]
    q = [wy[k][w[k]] for k in range(m)]
    cs = []
    for wt, cost, late, free, done, rest, after, same in cases:
        far = lambda t, near: [[max([t[i] + same * (ways[i][way[i]] == x < 2) for i in near[j] if i not in loc] + [0.0]) for x in ways[j]]
                               for j in win]
        each = [[cost[j] for j in win], far(done, deps), far(rest, kids)]
        c, ready, out = [[e[k][w[k]] for k in range(m)] for e in each]
        cs.append([wt, each, c, [late[j] for j in win], free, after, ready, out, [1e9] * m, same])

    def put(i, y):
        w[i], q[i] = y, wy[i][y]
        for x in cs:
            x[2][i], x[6][i], x[7][i] = x[1][0][i][y], x[1][1][i][y], x[1][2][i][y]

    def run(seq, p, dns, sts):
        got = 0.0
        for (wt, _c, c, lt, _f, after, ready, out, due, same), dn, st in zip(cs, dns, sts):
            free, top, tot = list(st[0]), st[1], st[2]
            for k in seq[p:]:
                x = q[k]
                at = free[x]
                if ready[k] > at:
                    at = ready[k]
                for i in dp[k]:
                    t = dn[i] + same if q[i] == x < 2 else dn[i]
                    if t > at:
                        at = t
                at += c[k]
                if x < 5:
                    free[x] = at
                at += lt[k]
                dn[k] = at
                tot += at
                if at > due[k]:
                    tot += NEAR * (at - due[k])
                at += out[k]
                if at > top:
                    top = at
            for x in range(5):
                if free[x] + after[x] > top:
                    top = free[x] + after[x]
            got += wt * (top + SOON * tot / m)
        return got

    def tight(seq, dn, x):
        c, lt, after, out = x[2], x[3], x[5], x[7]
        prev, last = {}, {}
        for k in seq:
            prev[k], last[q[k]] = last.get(q[k]), k
        k = max(seq, key=lambda i: max(dn[i] + out[i], dn[i] - lt[i] + after[q[i]] if q[i] < 5 and last[q[i]] == i else 0.0))
        got = []
        while k is not None:
            got.append(k)
            s, i = dn[k] - lt[k] - c[k] - 1e-6, prev[k]
            if q[k] < 5 and i is not None and dn[i] - lt[i] >= s:
                got += [k, i]
                k = i
            else:
                k = next((i for i in dp[k] if dn[i] + x[9] * (q[i] == q[k] < 2) >= s), None)
        return got

    def states(seq, dns, p, was):
        rows = []
        for (_w, _c, c, lt, _f, _a, _r, out, due, _s), dn, st in zip(cs, dns, was[p]):
            sts, free, top, tot = [], list(st[0]), st[1], st[2]
            for k in seq[p:]:
                sts.append((tuple(free), top, tot))
                if q[k] < 5:
                    free[q[k]] = dn[k] - lt[k]
                at = dn[k]
                tot += at
                if at > due[k]:
                    tot += NEAR * (at - due[k])
                if at + out[k] > top:
                    top = at + out[k]
            rows.append(sts)
        return was[:p] + list(zip(*rows))

    seq, dns, null = list(range(m)), [[0.0] * m for _ in cs], [(x[4], 0.0, 0.0) for x in cs]
    run(seq, 0, dns, null)
    for x, dn, pu in zip(cs, dns, pure):
        bar = max(dn[k] + x[7][k] for k in seq) - BAND
        x[8][:] = [bar - pu[j] for j in win]
    now = run(seq, 0, dns, null)
    c0, l0 = cs[0][2], cs[0][3]
    seq.sort(key=lambda k: dns[0][k] - l0[k] - c0[k])
    sts, taken, hot = states(seq, dns, 0, [null]), 0, tight(seq, dns[0], cs[0])
    for a, b, d, e in rnd:
        j = hot[int(a * len(hot))] if a * 53 % 1 < AIM else seq[int(a * m)]
        p = to = seq.index(j)
        moved, new = [], seq
        if len(wy[j]) > 1 and b < 0.35:
            moved = [(j, w[j], (w[j] + 1 + int(d * (len(wy[j]) - 1))) % len(wy[j]))]
            if b > 0.22:
                twin = [i for i in seq[max(p - 12, 0):p + 12] if q[i] == wy[j][moved[0][2]] and q[j] in wy[i]]
                if twin:
                    i = twin[int(e * 997) % len(twin)]
                    moved.append((i, w[i], wy[i].index(q[j])))
                    p = min(p, seq.index(i))
        if not moved or b < 0.1:
            s = to
            to = min(max(s + int((d * 7 % 1 - 0.5) * (REACH if e * 31 % 1 < 0.8 else 2 * m)), 0), m - 1)
            if to == s and not moved:
                continue
            near = dp if to < s else kd
            tied, go, stay = set(near[j]), [j], []
            for i in (seq[to:s][::-1] if to < s else seq[s + 1:to + 1]):
                if i in tied:
                    go.append(i)
                    tied.update(near[i])
                else:
                    stay.append(i)
            new = seq[:to] + go[::-1] + stay[::-1] + seq[s + 1:] if to < s else seq[:s] + stay + go + seq[to + 1:]
            p = min(p, to)
        for i, _o, y in moved:
            put(i, y)
        d2 = [dn[:] for dn in dns]
        got = run(new, p, d2, sts[p])
        if got <= now + heat * e:
            now, dns, seq, taken = got, d2, new, taken + 1
            if taken % SORT == 0:
                seq, p, x = sorted(new, key=lambda k: d2[0][k] - l0[k] - c0[k]), 0, taken // SORT % len(cs)
                hot = tight(seq, dns[x], cs[x])
            sts = states(seq, dns, p, sts)
        else:
            for i, o, _y in moved:
                put(i, o)
    for k in range(m):
        way[win[k]] = w[k]
    return [win[k] for k in seq]


def mend(ops, deps, kids):
    n, cases = len(ops), range(len(WAKE))
    rng = np.random.default_rng(SEED)
    ways = [["vstygx".index(w[0]) for w in o["ways"]] for o in ops]
    costs = [[[float((w[1] + 0 * WAKE)[s]) for w in o["ways"]] for o in ops] for s in cases]
    late = [[float((o["late"] + WAKE)[s]) for o in ops] for s in cases]
    way = [0] * n
    chosen = lambda: ([ways[j][way[j]] for j in range(n)], [[costs[s][j][way[j]] for j in range(n)] for s in cases])
    q, cost = chosen()
    same = SAME.tolist()
    seq = shake(list(range(n)), deps, kids, q, cost[0], late[0], same[0])
    pure = [[0.0] * n for s in cases]
    for s in cases:
        for j in range(n - 1, -1, -1):
            pure[s][j] = max([pure[s][i] + GROW * (late[s][i] + min(costs[s][i])) for i in kids[j]] + [0.0])
    worth = lambda x: sum(WEIGHT[s] * max(heads(x, deps, q, cost[s], late[s], same[s])[1]) for s in cases)
    early = [j for j, o in enumerate(ops) if o.get("early")]
    best, plan = None, [(0, n, k / SWEEPS, HEAT) for k in range(SWEEPS)]
    for a in range(AGAIN):
        a = int(a * 0.618 % 1 * n) - PART // 2
        plan += [(a, a + PART, k / TURNS, WARM) for k in range(TURNS)]
    for sweep, (lo, hi, part, heat) in enumerate(plan):
        heat *= (1 - part) ** 2
        for s in cases:
            for j in early:
                late[s][j] = float(WAKE[s]) + (AHEAD * max(1 - 1.3 * part, 0.0) if hi - lo == n else 0.0)
        if part == 0 and best:
            seq, way[:] = [i for i, _t in best[0]], best[2]
            q, cost = chosen()
        if sweep % 3 == 1 and hi - lo == n:
            s = sweep // 3 % len(cases)
            done = heads(seq, deps, q, cost[s], late[s], same[s])[1]
            new = shake(sorted(seq, key=lambda i: done[i]), deps, kids, q, cost[s], late[s], same[s])
            if worth(new) <= worth(seq) + heat:
                seq = new
        rest = [tails(seq, kids, q, cost[s], late[s], same[s]) for s in cases]
        done, free, p = [[0.0] * n for s in cases], [[0.0] * 6 for s in cases], 0
        first = int(rng.integers(STRIDE // 2, STRIDE))
        while p < n:
            lead = {}
            for j in seq[p + SPAN:][::-1]:
                lead[q[j]] = j
            now = [(float(WEIGHT[s]), costs[s], late[s], tuple(free[s]), done[s], rest[s],
                    [rest[s][lead[x]] if x in lead else 0.0 for x in range(5)], same[s]) for s in cases]
            if p >= lo - first:
                seq[p:p + SPAN] = stretch(seq[p:p + SPAN], now, pure, ways, way, deps, kids, rng.random((MOVES, 4)).tolist(), heat)
            if p + SPAN >= min(n, hi):
                break
            step = STRIDE if p else first
            for j in seq[p:p + step]:
                k = ways[j][way[j]]
                for s in cases:
                    at = max([free[s][k]] + [done[s][i] + same[s] * (ways[i][way[i]] == k < 2) for i in deps[j]]) + costs[s][j][way[j]]
                    done[s][j] = at + late[s][j]
                    if k < 5:
                        free[s][k] = at
            p += step
        q, cost = chosen()
        start = heads(seq, deps, q, cost[0], late[0], same[0])[0]
        seq.sort(key=lambda i: start[i])
        if best is None or worth(seq) < best[1]:
            best = ([(i, start[i]) for i in seq], worth(seq), list(way))
    return best


def rank_program(g, core, T, topo):
    rank = T.rank_of(core)
    if rank is None:
        return
    ops, sent = collect(g, T, topo, core, rank)
    if "order" not in KEPT:
        KEPT["order"] = order(ops)
    deps, seq, _, way = KEPT["order"]
    q = [o["ways"][y][0] for o, y in zip(ops, way)]
    first = [j for j, o in enumerate(ops) if o.get("dma") and not deps[j]]
    seq = first + [j for j, _t in seq if q[j] != "x" and j not in first]
    at = {j: k for k, j in enumerate(seq)}
    known, before, waits, need = {}, {}, {}, set()
    for j in seq:
        kn = known.setdefault(q[j], set())
        waits[j] = []
        for i in sorted(deps[j], key=lambda i: -at.get(i, 10 ** 6)):
            if i not in kn:
                waits[j].append(i)
                need.add(i)
                kn.add(i)
                kn |= before.get(i, set())
        before[j] = set(kn)
    last = [j for j in seq if ops[j].get("last")]
    need |= set(last)
    sig, user, count, nd = {}, [None] * NSEM, [0] * NSEM, 0
    for j, o in enumerate(ops):
        if q[j] == "x":
            sig[j] = (o["sem"], o["cnt"])
    for j in seq:
        if j not in need:
            continue
        if ops[j].get("dma"):
            sig[j] = ("d%d" % nd, 16)
            nd += 1
            continue
        k = [k for k in range(NSEM) if user[k] is None or user[k] in before[j]][0]
        user[k] = j
        count[k] += 1
        sig[j] = ("c%d" % k, count[k])
    eng = {"v": g.vector, "s": g.scalar, "t": g.tensor, "y": g.sync, "g": g}
    for j in seq:
        o = ops[j]
        for i in waits[j]:
            eng[q[j]].wait_ge(T.sem[sig[i][0]], sig[i][1])
        ins = o["ways"][way[j]][2]()
        if j in need:
            ins.then_inc(T.sem[sig[j][0]], 16 if o.get("dma") else 1)
    for j in last:
        g.sync.wait_ge(T.sem[sig[j][0]], 16)
    g.wait_ge(T.sem.sent, sent)
